import numpy as np, ml_dtypes
CORES = [1,5,17,21,33,37,49,53]
N = 8
BF = ml_dtypes.bfloat16
def gentries(a):
    return np.ascontiguousarray(a.reshape(8, 16, -1).transpose(0, 2, 1)).reshape(8, -1)
def gtable(e):
    e = np.asarray(e); return np.ascontiguousarray(e.reshape(8, -1, 16).transpose(0, 2, 1)).reshape(128, -1).astype(np.int32)
W, B, L, T, H, A = 4096, 12, 128, 3, 3, 768
def codes(rng, lo, hi):
    return np.floor(rng.random((N, 8, 16, W)) * (rng.integers(lo, hi + 1, (N, 8, 1, W)) + 1)).astype(np.int64)
def names(rng):
    hub = rng.integers(0, W, W // 16)
    def some(*shape):
        return np.where(rng.random(shape) < 0.5, hub[rng.integers(0, W // 16, shape)], rng.integers(0, W, shape))
    return some(N, 8, 16, W), some(N, 8, L)
def vals(rng, size):
    return np.clip(rng.standard_normal((N, 8, 16, W), dtype=np.float32) * np.exp2(size), -64, 64)
def plainvals(rng):
    return vals(rng, rng.integers(-2, 3, (N, 8, 16, 1)))
def pack(k, v, nm, s):
    two = nm[..., :W // 2] + W * nm[..., W // 2:]
    return {"kt": k.reshape(N, 128, W).astype(np.float32).astype(BF), "vt": v.reshape(N, 128, W).astype(np.float32).astype(BF),
            "bp": np.ascontiguousarray(two.reshape(N, 128, W // 2)).astype(np.int32), "st": np.stack([gtable(a) for a in s])}
def near():
    i, j = np.triu_indices(768); i = i + 256; j = j + 256; a = i * j
    where = np.full(2 ** 20 + 1, -1); where[a] = np.arange(len(a))
    b = (2 ** 36 + a // 2) // a; m = where[b]
    h = np.nonzero((m >= 0) & (np.abs(a * b - 2 ** 36) < 2 ** 13))[0]; m = m[h]
    z = np.concatenate([np.stack([i[h], j[h], i[m], j[m]], 1), np.stack([i[h], j[h], j[m], i[m]], 1)])
    y = z.astype(np.float32) * np.float32(2.0 ** -10); p = y[:, 0] * y[:, 1]; lim = np.float32(0.0625)
    return z[(((p * y[:, 2]) * y[:, 3]) < lim) != ((p * (y[:, 2] * y[:, 3])) < lim)]
def over(rng):
    i, j = np.triu_indices(768); i = i + 256; j = j + 256
    where = np.full(2 ** 20 + 1, -1); where[i * j] = np.arange(len(i))
    x = rng.integers(256, 1024, (3, 2 ** 19)); y = x.astype(np.float32) * np.float32(2.0 ** -10); R = (y[0] * y[1]) * y[2]
    h = np.nonzero((R > 0.07) & (R < 0.25))[0]; x = x[:, h]; R = R[h]
    c = (R.astype(np.float64) * 2.0 ** 27).astype(np.int64); m = where[(2 ** 43 + c // 2) // c]
    h = np.nonzero(m >= 0)[0]; m = m[h]; R = R[h]; z = np.stack([x[0, h], x[1, h], x[2, h], i[m], j[m]], 1)
    y = z.astype(np.float32) * np.float32(2.0 ** -10); u = y[:, 3]; v = y[:, 4]; lim = np.float32(0.0625); right = ((R * u) * v) < lim
    m24, m26 = [(((np.rint(R * np.float32(2.0 ** b)) * np.float32(2.0 ** -b)) * u) * v) < lim for b in (24, 26)]
    return z[((R * (u * v)) < lim) != right], z[(m24 != right) | (m26 != right)]
def setup_inputs(rng):
    nm, s = names(rng)
    return pack(codes(rng, 12, 15), plainvals(rng), nm, s)
def setup_inputs_spread(rng):
    nm, s = names(rng); weak = rng.random((N, 8, 1, W)) < 0.3
    k = np.where(weak, codes(rng, 4, 11), codes(rng, 14, 15)); s = np.where(rng.random(s.shape) < 0.5, s, (W * rng.random(s.shape) ** 4).astype(np.int64))
    return pack(k, vals(rng, rng.integers(-3, 4, (N, 8, 1, W))), nm, s)
def setup_inputs_ends(rng):
    k = 15 * (rng.random((N, 8, 16, W)) < rng.choice(np.array([0.0, 0.25, 0.25, 0.5, 1.0]), (N, 8, 1, W))).astype(np.int64)
    four = 15 * (rng.permutation(16) < 4).astype(np.int64); kind = np.argsort(rng.random((N, 8)), axis=1) % 3; kind[N - 1, 7] = 0
    k[..., 0] = np.where(kind[..., None] == 1, 15, four); k[..., W - 1] = np.where(kind[..., None] == 0, 15, four)
    e = (W - 1) * rng.integers(0, 2, (N, 8, 16, W // 2)); m = rng.random(e.shape) < 0.66
    nm = np.concatenate([np.where(m, e, rng.integers(0, W, e.shape)), np.where(m, e, rng.integers(0, W, e.shape))], axis=3)
    s = np.where(rng.random((N, 8, L)) < 0.72, (W - 1) * rng.integers(0, 2, (N, 8, L)), rng.integers(0, W, (N, 8, L))); s[..., L - 1] = W - 1
    v = plainvals(rng); v = np.where(rng.random(v.shape) < 0.3, np.where(rng.random(v.shape) < 0.5, 64.0, -64.0), v)
    return pack(k, v, nm, s)
def setup_inputs_crowd(rng):
    nm, s = names(rng); k = rng.integers(2, 7, (N, 8, 16, W)); k[1::2] = rng.integers(11, 16, (N // 2, 8, 16, W))
    o = rng.permutation(W); n = (H + 1) * L; ch = o[:H * L].reshape(H, L); u = o[H * L:n]; nul = o[n:n + 16]; big = o[n + 16:n + 80]; pk = o[n + 80:n + 80 + H]; top = o[n + 96:n + 112]
    def lead(r, g, keys, to):
        k[r, g][:, nul] = 0; nm[r, g][:, keys] = nul[rng.integers(0, 16, (16, len(keys)))]; nm[r, g, 15, keys] = to
    for r in range(0, N, 2):
        kind = rng.permutation(8); h5 = (int(np.nonzero(kind == 5)[0][0]) - 1) % 8
        nm[r, h5][rng.random((16, W)) < 0.25] = pk[0]
        for g in range(8):
            p = int(rng.choice(np.array([0, W - 1, rng.integers(0, W), rng.integers(0, W)])))
            if kind[g] in (0, 1, 7): nm[r, g, 15] = p
            if kind[g] == 2: nm[r, g, 15] = rng.choice(rng.integers(0, W, 3), W)
            if kind[g] == 1:
                x = (p + 1 + rng.permutation(W - 1)[:H + 1]) % W; nm[r, g, 15, x[:H]] = x[1:]
                a = s[r, g].copy(); a[np.isin(a, x)] = p; a[int(rng.choice(np.array([0, L - 1, rng.integers(0, L)])))] = x[0]; s[r, g] = a
            if kind[g] in (4, 6):
                x = k[r, g]; x[:, ch[0]] = rng.integers(12, 16, (16, L)); x[:, big] = rng.integers(11, 16, (16, 64))
                for h in range(1, H):
                    x[:, ch[h]] = 0; lead(r, g, ch[h - 1], ch[h])
                nm[r, g][:, ch[H - 1]] = big[rng.integers(0, 64, (16, L))]; a = rng.permutation(ch[0])
                if kind[g] == 6: a[int(rng.choice(np.array([0, L - 1, rng.integers(0, L)])))] = nul[0]
                s[r, g] = a; b, c = (r - 1) % N, (g - 1) % 8
                k[b, c][:, ch[0]] = 0; lead(b, c, u, rng.permutation(ch[0])); lead(b, c, ch[0], ch[0]); s[b, c] = rng.permutation(u)
            if kind[g] == 5:
                k[r, g][:, u] = rng.integers(4, 8, (16, L)); k[r, g][:, pk[0]] = 0
                lead(r, g, u, pk[0]); lead(r, g, pk[:1], pk[:1]); s[r, g] = rng.permutation(u); b, c = r + 1, (g + 1) % 8
                k[b, c][:, top] = 15
                for h in range(1, H):
                    k[b, c][:, pk[h]] = 0; lead(b, c, pk[h - 1:h], pk[h:h + 1])
                nm[b, c][:, pk[H - 1]] = rng.permutation(top); s[b, c] = np.where(s[b, c] == pk[0], top[0], s[b, c])
    return pack(k, plainvals(rng), nm, s)
def setup_inputs_corners(rng):
    nm, s = names(rng); k = codes(rng, 12, 15); own = np.arange(W)
    for r in range(N):
        kind = rng.permutation(8) % 4
        for g in range(8):
            if kind[g] == 0:
                nm[r, g, :15] = own; nm[r, g, 15] = np.where(rng.random(W) < 0.5, own, nm[r, g, 15])
            if kind[g] == 1:
                e = rng.integers(0, 3, (15, W)); nm[r, g, :15] = np.where(e == 0, 0, np.where(e == 1, W - 1, own)); nm[r, g, 15] = (own - 1) % W
            if kind[g] == 2:
                hot = rng.permutation(W) < W // 2; a = np.nonzero(hot)[0]; b = np.nonzero(~hot)[0]
                k[r, g] = np.where(hot, rng.integers(12, 16, (16, W)), 0); page = b[rng.integers(0, len(b), (16, W))]
                one = own[rng.random(W) < 0.7]; page[rng.integers(0, 16, len(one)), one] = a[rng.integers(0, len(a), len(one))]
                nm[r, g] = page; s[r, g] = a[rng.integers(0, len(a), L)]
            if kind[g] == 3:
                k[r, g] = rng.integers(0, 3, (16, W)); s[r, g, 0] = 0; s[r, g, L - 1] = W - 1
    return pack(k, plainvals(rng), nm, s)
def setup_inputs_order(rng):
    nm, s = names(rng); k = codes(rng, 12, 15); z = near(); zp, zm = over(rng); lane = np.arange(L); row = np.arange(16)[:, None]
    o = rng.permutation(W); a, b, d, nul, fac = o[:L], o[L:2 * L], o[2 * L:3 * L], o[3 * L:3 * L + 16], o[3 * L + 16:3 * L + 784]
    w = rng.permutation(16); e = w[:8, None]; sc = A + 1024 - np.arange(256, 1024)
    for r in range(N):
        kind = rng.permutation(8) % 2
        for g in range(8):
            x = k[r, g]; v = nm[r, g]
            x[w[:9, None], nul] = 0
            x[:, fac] = rng.integers(0, 16, (16, 768))
            x[e, fac] = (sc[None, :] + 15 * np.arange(8)[:, None]) // 15 // 8; x[w[8], fac] = sc % 15
            if kind[g]: continue
            x[:, a] = 0; x[e, a] = 15; x[w[8], a] = 1
            x[w[:9, None], o[L:3 * L]] = 0
            lay = rng.integers(0, 4 if r % 2 else 6, L); full = lane[lay < 3]; half = lane[lay == 3]; far = lane[lay > 3]
            y = fac[z[rng.integers(0, len(z), L)] - 256]
            y5 = fac[np.where((lay == 4)[:, None], zp[rng.integers(0, len(zp), L)], zm[rng.integers(0, len(zm), L)]) - 256]
            page = np.where((lay < 3) & (row >= 4 * lay + 4), v[:, a], nul[rng.integers(0, 16, (16, L))])
            for n in range(4): page[4 * lay[full] + n, full] = y[full, n]
            page[:2, half] = y[half, :2].T; page[15, half] = b[half]
            page[:3, far] = y5[far, :3].T; page[15, far] = d[far]
            v[:, a] = page; v[:2, b] = y[:, 2:].T; s[r, g] = a
            v[:, d[far]] = nul[rng.integers(0, 16, (16, len(far)))]; v[15, d[far]] = d[far]
            nm[(r + 1) % N, (g + 1) % 8][:2, d[far]] = y5[far, 3:].T
    return pack(k, plainvals(rng), nm, s)
def check_ranges(d):
    bad = []
    a = np.asarray(d["kt"]).astype(np.float64)
    if not np.all((a >= 0) & (a <= 15) & (a == np.floor(a))): bad.append("range of kt")
    a = np.asarray(d["vt"]).astype(np.float64)
    if not np.all((a >= -64) & (a <= 64)): bad.append("range of vt")
    for n, hi in (("bp", W * W - 1), ("st", W - 1)):
        if np.min(d[n]) < 0 or np.max(d[n]) > hi: bad.append("range of " + n)
    return bad
def take(tab, c):
    return np.take_along_axis(tab, c[:, :, None, :], 3)
def reference(kt, vt, bp, st):
    k = kt.astype(np.float32).astype(np.int64).reshape(N, 8, 16, W)
    sg = np.reciprocal(1.0 + np.exp(-vt.astype(np.float64))).reshape(N, 8, 16, W)
    u = bp.astype(np.int64).reshape(N, 8, 16, W // 2); pg = np.concatenate([u & (W - 1), u >> B], axis=3)
    c = np.stack([gentries(a) for a in st]).astype(np.int64)
    q = take(k, c); R = np.ones((N, 8, L), np.float32); acc = np.zeros((N, 8, 16, L)); one = np.float32(1); out = []
    for t in range(T):
        if t:
            c, q, R, acc = [np.roll(np.roll(a, 1, axis=0), t, axis=1) for a in (c, q, R, acc)]
        came = c; whole = np.ones((N, 8, L), bool)
        for h in range(H):
            nm = take(pg, c); flat = nm.reshape(N, 8, 16 * L)
            s = np.add.reduce(q[:, :, :, None, :] * take(k, flat).reshape(N, 8, 16, 16, L), axis=2)
            beta = np.minimum(np.maximum(s - A, 0), 960).astype(np.float32) * np.float32(2.0 ** -10)
            v = take(sg, flat).reshape(N, 8, 16, 16, L)
            broke = np.zeros((N, 8, L), bool); nxt = nm[:, :, 15]
            for i in range(16):
                on = ~broke; bi = beta[:, :, i]
                acc = acc + np.where(on, R.astype(np.float64) * bi.astype(np.float64), 0.0)[:, :, None, :] * v[:, :, :, i]
                R = np.where(on, R * (one - bi), R)
                hit = on & (R < np.float32(0.0625))
                nxt = np.where(hit, nm[:, :, i], nxt); broke = broke | hit
            c = nxt; q = np.where(broke[:, :, None, :], take(k, c), q); R = np.where(broke, one, R)
            cut = whole & broke; whole = whole & ~broke
        out.append((acc + R.astype(np.float64)[:, :, None, :] * take(sg, c)).reshape(N, 128, L))
        if t < T - 1:
            for j in range(L - 1, -1, -1):
                a, g = np.nonzero(cut[:, :, j])
                pg[a, g, 15, came[a, g, j]] = c[a, g, j]
    return {"ya": np.concatenate(out, axis=2).astype(np.float32)}

def check_inputs(d):
    bad = list(check_ranges(d))
    if not bad:
        for name, y in reference(**d).items():
            for q in range(N):
                v = np.abs(np.asarray(y[q], np.float64))
                if v.max() > 7 * np.sqrt(np.mean(v * v)): bad.append('%s of rank %d is uneven' % (name, q))
    return bad

@@ -1,0 +1,598 @@
+from concourse.mybir import AluOpType, AxisListType, ActivationFunctionType
+
+W = 4096
+F32, BF, I32, U16 = "float32", "bfloat16", "int32", "uint16"
+
+
+def _sb(shape, dtype):
+    return ("sbuf", shape, dtype)
+
+
+SCRATCH = {
+    "kx": _sb([128, W + 128], BF), "vv": _sb([128, W], BF), "bpi": _sb([128, W // 2], I32),
+    "pg": _sb([128, W + 128], I32), "sti": _sb([128, 8], I32),
+    "cl0": _sb([128, 16], U16), "cl1": _sb([128, 16], U16),
+    "nm0": _sb([128, 128], U16), "nm1": _sb([128, 128], U16),
+    "qs": _sb([128, 128], BF), "qd": _sb([128, 4096], BF), "nd": _sb([128, 1024], F32),
+    "kg": _sb([128, 2048], BF), "vg": _sb([128, 2048], BF), "nv": _sb([128, 128], U16),
+    "lv": _sb([128, 8], U16), "i3": _sb([128, 8], F32), "fd": _sb([128, 2], F32),
+    "vs0": _sb([128, 2048], F32), "vs1": _sb([128, 2048], F32),
+    "ff0": _sb([128, 137], F32), "ff1": _sb([128, 137], F32),
+    "ax0": _sb([128, 137], F32), "ax1": _sb([128, 137], F32), "tha": _sb([128, 136], F32),
+    "d1": _sb([128, 136], F32), "sc": _sb([128, 272], F32),
+    "dead": _sb([128, 8], F32), "rn": _sb([128, 8], F32),
+    "dd": _sb([128, 8, 17], F32), "be": _sb([128, 8, 17], F32), "rm": _sb([128, 8, 17], F32), "ww": _sb([128, 128], F32), "wt": _sb([128, 128], F32),
+    "wd0": _sb([128, 1024], F32), "wd1": _sb([128, 1024], F32),
+    "came": _sb([128, 8], F32), "xa": _sb([128, 128], F32), "xb": _sb([128, 128], F32), "crow": _sb([128, 128], F32),
+    "v0": _sb([128, 128], F32), "cd": _sb([128, 8], F32), "whole": _sb([128, 8], F32), "cut": _sb([128, 8], F32),
+    "cutw": _sb([128, 8], F32), "delta": _sb([128, 8], F32), "tt": _sb([128, 1024], BF),
+    "win": _sb([128, 128], F32), "wsum": _sb([128, 128], F32), "t1": _sb([128, 8], F32), "t2": _sb([128, 8], F32),
+    "offs": _sb([128, 8], U16), "vals": _sb([128, 128], F32),
+    "sg": _sb([128, 128], F32), "rep": _sb([128, 128], F32), "accs": _sb([128, 1024], F32),
+    "accr": _sb([128, 128], F32), "yo0": _sb([128, 128], F32), "yo1": _sb([128, 128], F32), "yo2": _sb([128, 128], F32),
+    "snd0": _sb([128, 144], F32), "snd1": _sb([128, 144], F32), "msg1": _sb([128, 144], F32), "msg2": _sb([128, 144], F32),
+    "acn0": _sb([128, 128], F32), "acn1": _sb([128, 128], F32), "ain1": _sb([128, 128], F32), "ain2": _sb([128, 128], F32),
+    "ip": _sb([128, 1], I32), "ib": _sb([128, 8], I32), "fb": _sb([128, 8], F32), "fc": _sb([128, 12], F32),
+    "ij": _sb([128, 8], F32), "i2": _sb([128, 8], F32), "ia": _sb([128, 128], I32), "ia2": _sb([128, 128], I32),
+    "ma": _sb([128, 128], F32), "em": _sb([128, 34], F32), "ig": _sb([128, 128], I32), "ig2": _sb([128, 128], I32),
+    "ones": _sb([128, 256], F32), "pm": _sb([128, 256], F32), "id2": _sb([128, 256], F32), "idb": _sb([128, 128], BF),
+    "jr": _sb([128, 16, 16], F32), "jr1": _sb([128, 128], F32), "jr2": _sb([128, 128], F32),
+    "bo0": _sb([128, 128], F32), "bof": _sb([128, 128], F32), "bob": _sb([128, 128], BF),
+    "ms0": _sb([128, 128], F32), "ms": _sb([128, 128], F32), "selg": _sb([128, 128], F32), "sel15": _sb([128, 128], F32),
+    "cb": _sb([128, 256], BF), "cc": _sb([128, 512], BF), "cs": _sb([128, 16, 17], BF),
+    "half": _sb([128, 128], F32), "pw": _sb([128, 128], F32), "pw2": _sb([128, 128], F32),
+    "thr": _sb([128, 128], F32), "segm": _sb([128, 128], F32), "pa": _sb([128, 16], F32), "colw": _sb([128, 8], F32),
+    "dum": _sb([128, 8], F32), "ds4": _sb([128, 8], F32),
+    "lq": _sb([128, 8], U16), "ln": _sb([128, 8], U16), "lx": _sb([128, 8], U16), "lw": _sb([128, 8], U16),
+    "lj": _sb([128, 8], U16), "lc": _sb([128, 8], U16),
+    "ps": ("psum", [128, 8, 4, 32], F32), "pz": ("psum", [128, 512], F32),
+    "pva": ("psum", [128, 1024], BF), "pvb": ("psum", [128, 1024], BF),
+    "paa": ("psum", [128, 512], F32), "pab": ("psum", [128, 512], F32), "px": ("psum", [128, 3, 170], F32),
+}
+BANKS = ("ps", "px", "pz", "pva", "pvb", "paa", "pab")
+SEMAPHORES = ["am1", "am2", "aa1", "aa2"] + ["sem%d" % k for k in range(140)]
+
+
+def rank_program(g, core, T, topo):
+    rank = T.rank_of(core)
+    if rank is None:
+        return
+    A = AluOpType
+    ACT = ActivationFunctionType
+    nxt = T.cores[(rank + 1) % len(T.cores)]
+    prv = T.cores[(rank - 1) % len(T.cores)]
+    rid, pid, _se = topo.addr(nxt)
+
+    def eight(src, dst):
+        eng = topo.engines(src, dst)[:8]
+        return sum(1 << e for e in eng), len(eng)
+    out_mask, out_n = eight(core, nxt)
+    in_n = eight(prv, core)[1]
+
+    V, S, P, Y, G = "v", "s", "p", "y", "g"
+    queue = {V: g.vector, S: g.scalar, P: g.tensor, Y: g.sync, G: g}
+    known = {q: set() for q in queue}
+    ops = []
+    lastw, readers, bank = {}, {}, {b: [] for b in BANKS}
+    semof, count, lastop, waited = {}, {}, {}, set()
+
+    def sem_of(name):
+        if name not in semof:
+            semof[name] = name if name in SEMAPHORES else "sem%d" % len([k for k in semof if k not in SEMAPHORES])
+            count[name] = 0
+        return T.sem[semof[name]]
+
+    def wait(q, d):
+        if d in known[q]:
+            return
+        name, n, before = ops[d]
+        queue[q].wait_ge(sem_of(name), n)
+        waited.add(d)
+        known[q] |= before
+        known[q].add(d)
+
+    def note(me, q, r, w):
+        for k in r:
+            if k in bank:
+                bank[k].append((q, me))
+            else:
+                readers.setdefault(k, []).append(me)
+        for k in w:
+            if k in bank:
+                bank[k].append((q, me))
+            else:
+                lastw[k] = me
+                readers[k] = []
+
+    def op(q, name, r, w, fn, step=1):
+        deps = set()
+        for k in list(r) + list(w):
+            if k in bank:
+                deps |= {d for (e, d) in bank[k] if e != q}
+                bank[k] = [(e, d) for (e, d) in bank[k] if e == q]
+            elif k in lastw:
+                deps.add(lastw[k])
+        for k in w:
+            deps |= set(readers.get(k, []))
+        if name in lastop:
+            deps.add(lastop[name])
+        for d in sorted(deps, reverse=True):
+            wait(q, d)
+        sem = sem_of(name)
+        ins = fn(queue[q], sem)
+        if ins is None:
+            count[name] += step
+        else:
+            for i in (ins if isinstance(ins, list) else [ins]):
+                i.then_inc(sem, step)
+                count[name] += step
+        me = len(ops)
+        ops.append((name, count[name], set(known[q])))
+        lastop[name] = me
+        note(me, q, r, w)
+        return me
+
+    def arrival(name, key):
+        sem_of(name)
+        count[name] += in_n
+        me = len(ops)
+        ops.append((name, count[name], set()))
+        lastop[name] = me
+        lastw[key] = me
+
+    nc = [0]
+
+    def const(q, r, w, fn):
+        nc[0] += 1
+        return op(q, "c%s%d" % (q, nc[0] % 8), r, w, fn)
+
+    def ts(out, in0, s1, s2, o0, o1=None):
+        if o1 is None:
+            return lambda e, s: e.tensor_scalar(out, in0, s1, None, o0)
+        return lambda e, s: e.tensor_scalar(out, in0, s1, s2, o0, o1)
+
+    def tt(out, a, b, o):
+        return lambda e, s: e.tensor_tensor(out, a, b, o)
+
+    def cp(out, a):
+        return lambda e, s: e.tensor_copy(out, a)
+
+    def act(out, a, f, **kw):
+        return lambda e, s: e.activation(out, a, f, **kw)
+
+    def mm(out, l, r):
+        return lambda e, s: e.matmul(out, l, r, True, True)
+
+    def iota(out, pat, base, cm, flt=False):
+        if flt:
+            return lambda e, s: e.iota(out, pat, base, cm, allow_small_or_imprecise_dtypes=True)
+        return lambda e, s: e.iota(out, pat, base, cm)
+
+    def sel(out, a, pat, o, base, cm):
+        return lambda e, s: e.affine_select(out, a, pat, o, 0.0, base, cm)
+
+    def dma(name, out, a, r, w, q=Y):
+        return op(q, name, r, w, lambda e, s: e.dma_start(out, a), 16)
+
+    def send(name, dst, src, rsem, key):
+        def fn(e, s):
+            e.remote_dma(dst, src, T.sem[rsem], s, pid, rid, out_mask)
+        return op(G, name, key, [], fn, out_n)
+
+    dma("ld_st", T.sti[:], T.st[:], [], ["sti"], S)
+    dma("ld_b0", T.bpi[:, 0:1024], T.bp[:, 0:1024], [], ["bpi0"])
+    dma("ld_b1", T.bpi[:, 1024:2048], T.bp[:, 1024:2048], [], ["bpi1"])
+    dma("ld_k", T.kx[:, 0:W], T.kt[:], [], ["kx"])
+    dma("ld_v", T.vv[:], T.vt[:], [], ["vv"])
+    for t in (1, 2):
+        arrival("am%d" % t, "msg%d" % t)
+        arrival("aa%d" % t, "ain%d" % t)
+
+    const(G, [], ["ip"], iota(T.ip[:], [[0, 1]], 0, 1))
+    const(G, [], ["ia"], iota(T.ia[:], [[0, 8], [-1, 16]], 16, 1))
+    const(G, [], ["ij"], iota(T.ij[:], [[1, 8]], 0, 0, True))
+    const(G, [], ["i2"], iota(T.i2[:], [[64, 4], [512, 2]], 0, 0, True))
+    const(G, [], ["i3"], iota(T.i3[:], [[8, 4], [64, 2]], 0, 0, True))
+    const(V, [], ["nd"], lambda e, s: e.memset(T.nd[:], 0.0))
+    const(V, [], ["ones", "cc"], lambda e, s: [e.memset(T.ones[:], 1.0), e.memset(T.cc[0:1, :], 0.0),
+                                               e.memset(T.cs[0:1, :, 1:17], 1.75), e.memset(T.cs[0:1, :, 0], 0.0)])
+    const(S, ["nd"], ["qd"], lambda e, s: [
+        e.activation(T.qd[:, 1024 * x:1024 * x + 1024], T.nd[:], ACT.Identity) for x in range(4)])
+    const(S, ["nd"], ["wd0", "wd1"], lambda e, s: [
+        e.activation(T.wd0[:], T.nd[:], ACT.Identity), e.activation(T.wd1[:], T.nd[:], ACT.Identity)])
+    fl = dict(allow_small_or_imprecise_dtypes=True)
+    const(G, [], ["cb", "ff0", "ff1", "ax0", "ax1", "d1", "pgx", "em0"], lambda e, s: [
+        e.iota(T.cb[0:1, :], [[-1, 2], [0, 128]], 1, 0, **fl),
+        e.iota(T.ff0[:, 136:137], [[0, 1]], 0, 0, **fl), e.iota(T.ff1[:, 136:137], [[0, 1]], 0, 0, **fl),
+        e.iota(T.ax0[:, 136:137], [[0, 1]], 0, 0, **fl), e.iota(T.ax1[:, 136:137], [[0, 1]], 0, 0, **fl),
+        e.iota(T.d1[:], [[0, 136]], 0, 0, **fl),
+        e.iota(T.em[:, 16:17], [[0, 1]], 0, 0, **fl), e.iota(T.pg[:, W:W + 128], [[0, 128]], 0, 0)])
+    const(G, [], ["d1"], iota(T.d1[:, 0::17], [[0, 8]], 1, 0, True))
+    pp = [[-1, 8], [-8, 4], [-32, 4]]
+    const(G, ["ones"], ["pm"], lambda e, s: [
+        e.affine_select(T.pm[:, 0:128], T.ones[:, 0:128], pp, A.is_equal, 0.0, 0, 1),
+        e.affine_select(T.pm[:, 128:256], T.ones[:, 0:128], pp, A.is_equal, 0.0, 0, 1)])
+    const(G, ["ones"], ["bo0"], sel(T.bo0[:], T.ones[:, 0:128], [[-16, 8], [0, 16]], A.is_ge, 0, 1))
+    const(G, [], ["ig"], iota(T.ig[:], [[-1, 8], [0, 16]], 8, 1))
+    const(G, ["ones"], ["id2"], sel(T.id2[:], T.ones[:], [[0, 2], [-1, 128]], A.is_equal, 0, 1))
+    const(G, ["bo0"], ["bof"], sel(T.bof[:], T.bo0[:], [[16, 8], [0, 16]], A.is_ge, 15, -1))
+    const(G, ["ones"], ["idb"], sel(T.idb[:], T.ones[:, 0:128], [[-1, 128]], A.is_equal, 0, 1))
+    const(G, ["ones"], ["ms0"], sel(T.ms0[:], T.ones[:, 0:128], [[0, 8], [-8, 4], [-32, 4]], A.is_ge, 0, 1))
+    const(G, ["bo0"], ["bob"], sel(T.bob[:], T.bo0[:], [[16, 8], [0, 16]], A.is_ge, 15, -1))
+    const(G, ["ms0"], ["ms"], sel(T.ms[:], T.ms0[:], [[0, 8], [8, 4], [32, 4]], A.is_ge, 7, -1))
+    const(G, ["ones"], ["jr0"], sel(T.jr[:], T.ones[:], [[-8, 16], [0, 2], [-1, 8]], A.is_equal, 0, 1))
+    const(G, ["jr0"], ["jr"], lambda e, s: [
+        e.affine_select(T["jr%d" % u][:], T.jr[:, :, 8 - u:16 - u], [[0, 128]], A.is_ge, 0.0, 0, 0) for u in (1, 2)])
+
+    sh, an = A.logical_shift_right, A.bitwise_and
+    const(V, ["ip"], ["ib"], lambda e, s: [
+        e.tensor_scalar(T.ib[:, 0:1], T.ip[:], 3, None, an),
+        e.tensor_scalar(T.ib[:, 1:2], T.ip[:], 12, None, an),
+        e.tensor_scalar(T.ib[:, 2:3], T.ip[:], 4, None, sh),
+        e.tensor_scalar(T.ib[:, 3:4], T.ip[:], 8, None, an),
+        e.tensor_scalar(T.ib[:, 4:5], T.ip[:], 7, None, an),
+        e.tensor_scalar(T.ib[:, 5:6], T.ip[:], 15, None, an),
+        e.tensor_scalar(T.ib[:, 6:7], T.ip[:], 3, 3, sh, an),
+        e.tensor_scalar(T.ib[:, 7:8], T.ip[:], 5, None, sh)])
+    const(V, ["ia"], ["ia2"], ts(T.ia2[:], T.ia[:], 15, None, an))
+    const(V, ["ib"], ["fb"], cp(T.fb[:], T.ib[:]))
+    const(V, ["ia2"], ["ma"], ts(T.ma[:], T.ia2[:], 0.0, None, A.is_equal))
+    fb = [T.fb[:, k:k + 1] for k in range(8)]
+    fc = [T.fc[:, k:k + 1] for k in range(12)]
+    const(V, ["fb"], ["fca"], lambda e, s: [
+        e.tensor_scalar(fc[0], fb[0], 32.0, fb[2], A.mult, A.add),
+        e.tensor_scalar(fc[1], fb[0], 64.0, fb[2], A.mult, A.add),
+        e.tensor_scalar(fc[2], fb[3], 32.0, fb[4], A.mult, A.add),
+        e.tensor_scalar(fc[3], fb[6], 4.0, fb[7], A.mult, A.add),
+        e.tensor_scalar(T.fd[:, 0:1], fb[3], 4.0, fb[2], A.mult, A.add)])
+    op(V, "cvc", ["sti"], ["cl0"], cp(T.cl0[:, 0:8], T.sti[:]))
+    const(V, ["fb", "fca"], ["fcb"], lambda e, s: [
+        e.tensor_scalar(fc[4], fb[1], 2.0, fc[0], A.mult, A.add),
+        e.tensor_scalar(fc[5], fb[1], 34.0, fc[0], A.mult, A.add),
+        e.tensor_scalar(fc[6], fb[1], 64.0, fc[1], A.mult, A.add),
+        e.tensor_scalar(fc[7], fb[2], 8.0, fc[2], A.mult, A.add),
+        e.tensor_scalar(fc[8], fb[5], float(W), None, A.add),
+        e.tensor_scalar(fc[9], fc[3], float(W), None, A.add),
+        e.tensor_scalar(T.fd[:, 1:2], fb[4], 128.0, T.fd[:, 0:1], A.mult, A.add)])
+    for k in (0, 1):
+        a, b = 1024 * k, 1024 * k + 1024
+        op(V, "unp%d" % k, ["bpi%d" % k], ["pg%d" % k], lambda e, s: [
+            e.tensor_scalar(T.pg[:, a:b], T.bpi[:, a:b], W - 1, None, an),
+            e.tensor_scalar(T.pg[:, 2048 + a:2048 + b], T.bpi[:, a:b], 12, None, sh)])
+    PG = ["pg0", "pg1", "pgx"]
+
+    def first_constants():
+        const(V, ["fcb", "ij", "i2", "i3"], ["lists"], lambda e, s: [
+            e.tensor_scalar(T.lv[:], T.i3[:], T.fd[:, 1:2], None, A.add),
+            e.tensor_scalar(T.ln[:], T.ij[:], 128.0, fc[4], A.mult, A.add),
+            e.tensor_scalar(T.lq[:], T.ij[:], 512.0, fc[5], A.mult, A.add),
+            e.tensor_scalar(T.lx[:], T.ij[:], 8.0, fc[6], A.mult, A.add),
+            e.tensor_scalar(T.lw[:], T.i2[:], fc[7], None, A.add),
+            e.tensor_scalar(T.dum[:], T.ij[:], 16.0, fc[8], A.mult, A.add),
+            e.tensor_scalar(T.ds4[:], T.ij[:], 16.0, fc[9], A.mult, A.add),
+            e.tensor_scalar(T.lc[:], T.ij[:], 17.0, None, A.mult),
+            e.tensor_copy(T.lj[:], T.ij[:])])
+        const(V, ["ma", "em0", "sti"], ["em", "came", "tha"], lambda e, s: [
+            e.tensor_tensor(T.em[:, 1:16], T.ma[:, 1:16], T.ma[:, 0:15], A.subtract),
+            e.tensor_tensor(T.em[:, 18:33], T.ma[:, 1:16], T.ma[:, 0:15], A.subtract),
+            e.tensor_copy(T.em[:, 0:1], T.ma[:, 0:1]), e.tensor_copy(T.em[:, 17:18], T.ma[:, 0:1]),
+            e.tensor_scalar(T.em[:, 33:34], T.ma[:, 15:16], -1.0, None, A.mult),
+            e.memset(T.tha[:], 0.0625),
+            e.tensor_scalar(fc[10], T.ma[:, 15:16], -1.0, 1.0, A.mult, A.add),
+            e.tensor_copy(T.came[:], T.sti[:])])
+        const(V, [], ["tha"], lambda e, s: e.memset(T.tha[:, 0::17], 2.0))
+
+    def late_constants_a():
+        const(V, ["ones"], ["half", "segm"], lambda e, s: [
+            e.tensor_scalar(T.half[:], T.ones[:, 0:128], 0.5, None, A.mult), e.memset(T.segm[:], 1.0)])
+        const(V, ["ig"], ["ig2"], ts(T.ig2[:], T.ig[:], 7, None, an))
+        const(V, ["half", "ones"], ["pw"], lambda e, s: e.tensor_tensor_scan(
+            T.pw[:], T.half[:], T.ones[:, 0:128], 2.0 ** 64, A.mult, A.mult))
+        const(V, ["ig2"], ["selg"], ts(T.selg[:], T.ig2[:], 0.0, None, A.is_equal))
+        const(G, ["selg"], ["sel15"], sel(T.sel15[:], T.selg[:], [[0, 8], [1, 16]], A.is_equal, -15, 0))
+
+    def late_constants_b():
+        const(V, [], ["segm"], lambda e, s: e.memset(T.segm[:, 0::16], 0.0))
+        const(V, ["pw", "ma"], ["pw2", "pa"], lambda e, s: [
+            e.tensor_tensor(T.pw2[:], T.pw[:], T.ma[:], A.mult),
+            e.tensor_tensor(T.pa[:], T.pw[:, 63:79], T.ma[:, 0:16], A.mult)])
+        const(V, ["pw2", "pa"], ["thr", "fc11"], lambda e, s: [
+            e.tensor_scalar(T.thr[:], T.pw2[:], 2.5, None, A.mult),
+            e.tensor_reduce(fc[11], T.pa[:], AxisListType.X, A.add)])
+        const(V, ["fc11", "pw"], ["colw"], ts(T.colw[:], T.pw[:, 0::16], fc[11], None, A.mult))
+
+    RX = T.px[:, 2, 0:128]
+
+    def weights(n, part=None):
+        f, r, a, r0 = "ff%d" % (n % 2), "rs%d" % (n % 2), "ax%d" % (n % 2), 128 + 136 * (n % 2)
+        if part == 0:
+            op(V, "be", [f], ["be"], ts(T.be[:], T[f][:, 1:137], -1.0, 1.0, A.mult, A.add))
+        if part == 3:
+            op(S, "bes", [f], ["be"], act(T.be[:], T[f][:, 1:137], ACT.Identity, bias=1.0, scale=-1.0))
+        if part in (None, 1):
+            op(V, "rm", [r, a, "pz"], ["rm"], tt(T.rm[:], T.pz[:, r0:r0 + 136], T[a][:, 0:136], A.mult))
+        if part in (None, 2):
+            op(V, "ww", ["be", "rm"], ["ww"], tt(T.ww[:], T.rm[:, :, 0:16], T.be[:, :, 0:16], A.mult))
+
+    def turn_w():
+        op(P, "wtp", ["ww", "id2"], ["pz"], mm(T.pz[:, 0:128], T.ww[:], T.id2[:, 0:128]))
+
+    def take_w():
+        op(V, "wtc", ["pz"], ["wt"], cp(T.wt[:], T.pz[:, 0:128]))
+
+    def spread_w(n, taken=False):
+        wd = "wd%d" % (n % 2)
+        if not taken:
+            take_w()
+        op(V, "wds", ["wt", "lists"], [wd], cp(T[wd][:, 0:1024].indirect(T.lw[:]), T.wt[:]))
+
+    def acc_in(t):
+        op(P, "arot", ["ain%d" % t, "id2"], ["px"], mm(RX, T.id2[:, 128 - 16 * t:256 - 16 * t], T["ain%d" % t][:]))
+        op(V, "accr", ["px"], ["accr"], cp(T.accr[:], RX))
+
+    def turn_v():
+        for half, b in enumerate(("pva", "pvb")):
+            op(P, "vt" + b, ["vg" + b, "idb"], [b], lambda e, s: [
+                e.transpose(T[b][:, 128 * x:128 * x + 128], T.vg[:, 1024 * half + 128 * x:1024 * half + 128 * x + 128], T.idb[:])
+                for x in range(8)])
+
+    def sigmoid(n):
+        vs = "vs%d" % (n % 2)
+        for half, b in enumerate(("pva", "pvb")):
+            op(S, "sg" + b, [b], [vs + b], act(T[vs][:, 1024 * half:1024 * half + 1024], T[b][:], ACT.Sigmoid))
+
+    def acc_open():
+        for b in ("paa", "pab"):
+            op(P, "ai" + b, ["cb", "cc"], [b], lambda e, s: e.matmul(T[b][:], T.cb[0:1, 128:256], T.cc[0:1, :], True, False))
+
+    def acc_add(n, half):
+        b, vs, wd = ("paa", "pab")[half], "vs%d" % (n % 2), "wd%d" % (n % 2)
+        op(P, "am" + b, [vs + ("pva", "pvb")[half], wd], [b], lambda e, s: [
+            e.matmul(T[b][:, 64 * x:64 * x + 64], T[vs][:, 1024 * half + 128 * x:1024 * half + 128 * x + 128],
+                     T[wd][:, 512 * half + 64 * x:512 * half + 64 * x + 64], False, n % 3 == 2 and x == 7) for x in range(8)])
+
+    def acc_out(q, half):
+        b, o = ("paa", "pab")[half], T.accs[:, 512 * half:512 * half + 512]
+        op(q, "ao" + q + b, [b], ["accs%d" % half], act(o, T[b][:], ACT.Identity) if q == S else cp(o, T[b][:]))
+    ACCS = ["accs0", "accs1", "lists"]
+
+    def picked():
+        return T.accs[:, 0:1024].indirect(T.lx[:])
+
+    def report(t):
+        acn, yo = "acn%d" % t, "yo%d" % t
+        if t == 0:
+            op(V, "acn", ACCS, [acn], cp(T[acn][:], picked()))
+        else:
+            op(V, "acn", ACCS + ["accr"], [acn], tt(T[acn][:], picked(), T.accr[:], A.add))
+        send("sa%d" % t, T["ain%d" % (t + 1)][:], T[acn][:], "aa%d" % (t + 1), [acn])
+        op(V, "yo", [acn, "rep"], [yo], tt(T[yo][:], T[acn][:], T.rep[:], A.add))
+        dma("st%d" % t, T.ya[:, 128 * t:128 * t + 128], T[yo][:], [yo], [])
+
+    def rest_value(cl):
+        op(S, "sgc", ["vv", cl], ["sg"], act(T.sg[:], T.vv[:, 0:W].indirect(T[cl][:, 0:8]), ACT.Sigmoid))
+
+    def rest_row():
+        op(V, "xb", ["rn", "ms", "lists"], ["xb"], tt(T.xb[:], T.rn[:, 0:8].indirect(T.lj[:]), T.ms[:], A.mult))
+        op(P, "rrow", ["xb", "selg"], ["px"], mm(RX, T.selg[:], T.xb[:]))
+
+    def rest_term():
+        op(V, "rep", ["sg", "px"], ["rep"], tt(T.rep[:], T.sg[:], RX, A.mult))
+
+    def kchunk(q, nm, a, b, name):
+        o, i = T.kg[:, 256 * a:256 * b], T.kx[:, 0:W].indirect(T[nm][:, 16 * a:16 * b])
+        op(q, name, ["kx", nm], ["kg%d" % x for x in range(a, b)], cp(o, i) if q == V else act(o, i, ACT.Identity))
+
+    def scores(a, b, name, stops):
+        op(P, name, ["qd"] + ["kg%d" % x for x in range(a, b)], ["ps"], lambda e, s: [
+            e.matmul(T.ps[:, m // 4, :, 1:17], T.qd[:, 128 * m:128 * m + 128], T.kg[:, 64 * m:64 * m + 64],
+                     False, m in stops) for m in range(4 * a, 4 * b)])
+
+    for n in range(9):
+        t, h = divmod(n, 3)
+        cl, cn, nm = "cl%d" % (n % 2), "cl%d" % ((n + 1) % 2), "nm%d" % (n % 2)
+        ff, rs, ax = "ff%d" % (n % 2), "rs%d" % (n % 2), "ax%d" % (n % 2)
+        msg = "msg%d" % t
+        came, camek = (T.came, "came") if t == 0 else (T[msg], msg)
+        qk, qkk = (T.ds4[:], "lists") if h == 0 else (T.sc[:, 136::17], "scq")
+        end = n == 8
+        split = 6 if end else (5 if h > 0 else 4)
+        mid = 4 if split == 6 else 3
+        stops = (15, 31 if (end or split == 4) else 4 * split - 1)
+
+        op(P, "si", ["cb", "cc"], ["ps"], lambda e, s: [
+            e.matmul(T.ps[:, 4 * x:4 * x + 4, :, 0:17], T.cb[0:1, 0:128], T.cs[0:1], True, False) for x in (0, 1)])
+        if h == 0 and t > 0:
+            op(V, "cvc", [msg], [cl], cp(T[cl][:, 0:8], T[msg][:, 0:8]))
+            op(P, "qrot", [msg, "id2"], ["px"], mm(RX, T.id2[:, 128 - 16 * t:256 - 16 * t], T[msg][:, 16:144]))
+        op(V, "nm", PG + [cl], [nm], cp(T[nm][:], T.pg[:, 0:W].indirect(T[cl][:, 0:8])))
+        if n == 0:
+            first_constants()
+        if h == 0 and t > 0:
+            spread_w(n - 1, True)
+        if h == 2 and t > 0:
+            report(t - 1)
+        if h == 2:
+            acc_add(n - 2, 0)
+        elif t > 0:
+            acc_add(n - 2, 1)
+        qscale = -1.0 / 1024
+        if h > 0:
+            op(S, "qs", ["kx", "kxx", cl], ["qs"],
+               act(T.qs[:], T.kx[:, 0:W + 128].indirect(T[cl][:, 8:16]), ACT.Identity, scale=qscale))
+            turn_v()
+        elif t == 0:
+            op(S, "qs", ["kx", cl], ["qs"], act(T.qs[:], T.kx[:, 0:W].indirect(T[cl][:, 0:8]), ACT.Identity, scale=qscale))
+        else:
+            op(S, "qs", ["px"], ["qs"], act(T.qs[:], RX, ACT.Identity, scale=qscale))
+        if end:
+            acc_add(n - 2, 1)
+            weights(n - 1, 3)
+            weights(n - 1, 1)
+        op(V, "nd", [nm, "lists"], ["nd"], cp(T.nd[:, 0:1024].indirect(T.ln[:]), T[nm][:]))
+        if end:
+            weights(n - 1, 2)
+            turn_w()
+        else:
+            op(P, "dn", ["nd", "em"], ["px"], lambda e, s: [
+                e.matmul(T.px[:, 0:2, 17 * x:17 * x + 17], T.nd[:, 128 * x:128 * x + 128], T.em[:], True, True)
+                for x in range(8)])
+        kchunk(V, nm, 0, 2, "k0")
+        if not end:
+            kchunk(S, nm, split, 8, "k3")
+        if h == 0:
+            op(S, "kxx", ["qs"], ["kxx"], act(T.kx[:, W:W + 128], T.qs[:], ACT.Identity, scale=-1024.0))
+        else:
+            if not end:
+                weights(n - 1, 3)
+            if h == 1 and t > 0:
+                acc_out(S, 1)
+            sigmoid(n - 1)
+        op(V, "qd", ["qs", "lists"], ["qd"], cp(T.qd[:, 0:4096].indirect(T.lq[:]), T.qs[:]))
+        scores(0, 2, "sco0", stops)
+        if h > 0 and not end:
+            scores(split, 8, "sco3", stops)
+        op(V, "nv", ["nd", "lists"], ["nv"], cp(T.nv[:], T.nd[:, 0:1024].indirect(T.lv[:])))
+        for x, b in enumerate(("pva", "pvb")):
+            op(S, "vg" + b, ["vv", "nv"], ["vg" + b], act(
+                T.vg[:, 1024 * x:1024 * x + 1024], T.vv[:, 0:W].indirect(T.nv[:, 64 * x:64 * x + 64]), ACT.Identity))
+        if h == 0:
+            scores(split, 8, "sco3", stops)
+        if end:
+            spread_w(n - 1)
+            acc_add(n - 1, 0)
+        kchunk(V, nm, 2, mid, "k1")
+        scores(2, mid, "sco1", stops)
+        kchunk(V, nm, mid, split, "k2")
+        scores(mid, split, "sco2", stops)
+        if end:
+            kchunk(V, nm, 6, 8, "k3v")
+            scores(6, 8, "sco3", stops)
+            turn_v()
+            acc_add(n - 1, 1)
+        elif h > 0:
+            weights(n - 1)
+            turn_w()
+        elif t == 0:
+            late_constants_a()
+        else:
+            op(V, "d1", [msg], ["d1"], cp(T.d1[:, 0::17], T[msg][:, 8:16]))
+            rest_row()
+        if h == 2 and not end:
+            acc_add(n - 2, 1)
+        if h == 0 and t > 0:
+            acc_add(n - 1, 0)
+            acc_out(S, 0)
+        if h == 1:
+            acc_open()
+        op(V, "clamp", ["ps"], [ff], lambda e, s: [
+            e.tensor_scalar(T[ff][32 * b:32 * b + 32, 0:136], T.ps[32 * b:32 * b + 32, :, b, 0:17], 0.0625, 1.0, A.max, A.min)
+            for b in range(4)])
+        if not end:
+            op(V, "g2", [qkk, "px"], ["px", "g2"], tt(T.px[:, 1, 16:136:17], qk, T.px[:, 1, 16:136:17], A.add))
+        r0 = 128 + 136 * (n % 2)
+        rall, r15 = T.pz[:, r0:r0 + 136], T.pz[:, r0 + 16:r0 + 136:17]
+        op(V, "rs", [ff, "d1"], [rs, "pz"], lambda e, s: e.tensor_tensor_scan(
+            rall, T[ff][:, 0:136], T.d1[:], 0.0, A.mult, A.max))
+        if h == 2 and t < 2:
+            op(V, "whole", ["ax0", "ax1"], ["whole"], tt(T.whole[:], T.ax0[:, 16:136:17], T.ax1[:, 16:136:17], A.mult))
+        if h == 0 and t > 0:
+            rest_term()
+        if end:
+            weights(n, 0)
+            op(V, "ax", [rs, "pz"], [ax], ts(T[ax][:, 0:136], rall, 0.0625, None, A.is_ge))
+            weights(n, 1)
+            op(V, "dd", [ax], ["dd"], tt(T.dd[:], T[ax][:, 0:136], T[ax][:, 1:137], A.subtract))
+            weights(n, 2)
+            op(V, "dd", ["dd", "rm"], ["dd"], tt(T.dd[:, :, 15], T.dd[:, :, 15], T.rm[:, :, 16], A.add))
+            op(V, "wwe", ["dd", "ww"], ["ww"], tt(T.ww[:], T.ww[:], T.dd[:, :, 0:16], A.add))
+            turn_w()
+            spread_w(n)
+            sigmoid(n)
+            acc_in(t)
+            acc_add(n, 0)
+            acc_add(n, 1)
+            acc_out(V, 0)
+            acc_out(V, 1)
+            op(V, "yo", ACCS + ["accr"], ["yo2"], tt(T.yo2[:], picked(), T.accr[:], A.add))
+            dma("st2", T.ya[:, 256:384], T.yo2[:], ["yo2"], [])
+            break
+        op(V, "ax", [rs, "pz", "tha"], [ax], tt(T[ax][:, 0:136], rall, T.tha[:], A.is_ge))
+        op(V, "dead", [rs, "pz"], ["dead"], ts(T.dead[:], r15, 0.0625, None, A.is_lt))
+
+        def first_on():
+            op(V, "on", [], [ax], lambda e, s: e.memset(T[ax][:, 0:136:17], 1.0))
+        op(V, "sc", [ax, "px"], ["sc"], lambda e, s: e.tensor_tensor_scan(
+            T.sc[:, 135::-1], T[ax][:, 136:0:-1], T.px[:, 0, 135::-1], 0.0, A.mult, A.add))
+        if not end:
+            op(V, "scq", [ax, "px", "g2"], ["scq"], lambda e, s: e.tensor_tensor_scan(
+                T.sc[:, 271:135:-1], T[ax][:, 136:0:-1], T.px[:, 1, 135::-1], 0.0, A.mult, A.add))
+            op(P, "pc", ["sc", "scq", "pm"], ["px"], mm(T.px[:, 0, 136:152], T.pm[:, 0:128], T.sc[:, 0::17]))
+            first_on()
+        cs = T.sc[:, 0:136:17]
+
+        def lists():
+            op(V, "cvc", ["px"], [cn], cp(T[cn][:], T.px[:, 0, 136:152]))
+        if h < 2:
+            op(V, "d1", ["dead", rs, "pz"], ["d1"], tt(T.d1[:, 0::17], T.dead[:], r15, A.max))
+            if h > 0:
+                spread_w(n - 1)
+                lists()
+            elif t < 2:
+                if t == 0:
+                    late_constants_b()
+                op(V, "xa", [camek, "ma", "lists"], ["xa"], tt(T.xa[:], came[:, 0:8].indirect(T.lj[:]), T.ma[:], A.mult))
+                op(V, "cd", [camek, "lists"], ["cd"], tt(T.cd[:], came[:, 0:8], T.dum[:], A.subtract))
+                op(P, "crp", ["xa", "bof"], ["pz"], mm(T.pz[:, 0:128], T.bof[:], T.xa[:]))
+                lists()
+                op(V, "v0", [nm, "em"], ["v0"], ts(T.v0[:], T[nm][:], fc[10], None, A.mult))
+                op(V, "crow", ["pz"], ["crow"], cp(T.crow[:], T.pz[:, 0:128]))
+            else:
+                lists()
+                acc_in(t - 1)
+        elif t < 2:
+            u, snd = t + 1, "snd%d" % t
+            op(V, "rn", ["dead", rs, "pz"], ["rn"], tt(T.rn[:], T.dead[:], r15, A.max))
+            op(V, "cut", ["whole", "dead"], ["cut"], tt(T.cut[:], T.whole[:], T.dead[:], A.mult))
+            take_w()
+            lists()
+            op(P, "pq", ["sc", "rn", "cut", "pm", "jr"], ["px"], lambda e, s: [
+                e.matmul(T.px[:, 1, 136:144], T.pm[:, 128 - 16 * u:256 - 16 * u], cs, True, True),
+                e.matmul(T.px[:, 1, 144:152], T["jr%d" % u][:], T.rn[:], True, True),
+                e.matmul(T.px[:, 1, 152:160], T.pm[:, 0:128], T.cut[:], True, True)])
+            op(V, "snb", ["kx", "kxx", cn], [snd + "b"], cp(T[snd][:, 16:144], T.kx[:, 0:W + 128].indirect(T[cn][:, 8:16])))
+            op(V, "xa", ["sc", "ms", "lists"], ["xa"], tt(T.xa[:], T.sc[:, 0:136].indirect(T.lc[:]), T.ms[:], A.mult))
+            op(V, "sna", ["px"], [snd + "a"], cp(T[snd][:, 0:16], T.px[:, 1, 136:152]))
+            send("sm%d" % t, T["msg%d" % u][:], T[snd][:], "am%d" % u, [snd + "a", snd + "b"])
+            op(V, "cutw", ["px", "colw", "cd"], ["cutw", "delta"], lambda e, s: [
+                e.tensor_tensor(T.cutw[:], T.px[:, 1, 152:160], T.colw[:], A.mult),
+                e.tensor_tensor(T.delta[:], T.px[:, 1, 152:160], T.cd[:], A.mult)])
+            op(P, "c15", ["xa", "sel15"], ["px"], mm(RX, T.sel15[:], T.xa[:]))
+            op(V, "tt", ["crow", camek, "cutw"], ["tt"], lambda e, s: [
+                e.tensor_scalar(T.tt[:, 144 * x:128 * x + 128], T.crow[:, 16 * x:128], came[:, x:x + 1], T.cutw[:, x:x + 1],
+                                A.is_equal, A.mult) for x in range(8)])
+            op(P, "ssum", ["tt", "bob"], ["pz"], lambda e, s: [
+                e.matmul(T.pz[:, 16 * x:128], T.bob[:], T.tt[:, 144 * x:128 * x + 128], x == 0, x == 7)
+                for x in range(8)])
+            turn_v()
+            spread_w(n - 1, True)
+            op(V, "win", ["pz", "thr"], ["win"], tt(T.win[:], T.pz[:, 0:128], T.thr[:], A.is_lt))
+            weights(n, 0)
+            op(V, "wsum", ["win", "segm"], ["wsum"], lambda e, s: e.tensor_tensor_scan(
+                T.wsum[:], T.segm[:], T.win[:], 0.0, A.mult, A.add))
+            weights(n, 1)
+            op(V, "t1", ["wsum", "delta"], ["t1"], tt(T.t1[:], T.wsum[:, 15::16], T.delta[:], A.mult))
+            weights(n, 2)
+            turn_w()
+            acc_add(n - 1, 0)
+            op(V, "t2", ["t1", "lists"], ["t2"], tt(T.t2[:], T.t1[:], T.dum[:], A.add))
+            op(V, "vals", ["v0", "px"], ["vals"], tt(T.vals[:], T.v0[:], RX, A.add))
+            op(V, "offs", ["t2"], ["offs"], cp(T.offs[:], T.t2[:]))
+            take_w()
+            op(V, "cutp", ["vals", "offs"], PG, cp(T.pg[:, 0:W + 128].indirect(T.offs[:]), T.vals[:]))
+            rest_value(cn)
+            sigmoid(n)
+
+    for name in list(lastop):
+        if lastop[name] not in waited:
+            wait(G, lastop[name])

@@ -1,6 +1,7 @@
 from concourse.mybir import AluOpType, AxisListType, ActivationFunctionType
 
 W = 4096
+SPLIT, MID = 10, 8
 F32, BF, I32, U16 = "float32", "bfloat16", "int32", "uint16"
 
 
@@ -16,13 +17,14 @@ SCRATCH = {
     "qs": _sb([128, 128], BF), "qd": _sb([128, 4096], BF), "nd": _sb([128, 1024], F32),
     "kg": _sb([128, 2048], BF), "vg": _sb([128, 2048], BF), "nv": _sb([128, 128], U16),
     "lv": _sb([128, 8], U16), "i3": _sb([128, 8], F32), "fd": _sb([128, 2], F32),
-    "vs0": _sb([128, 2048], F32), "vs1": _sb([128, 2048], F32),
+    "vs0": _sb([128, 2048], F32), "vs1": _sb([128, 2048], F32), "vs2": _sb([128, 2048], F32),
     "ff0": _sb([128, 137], F32), "ff1": _sb([128, 137], F32),
     "ax0": _sb([128, 137], F32), "ax1": _sb([128, 137], F32), "tha": _sb([128, 136], F32),
     "d1": _sb([128, 136], F32), "sc": _sb([128, 272], F32),
     "dead": _sb([128, 8], F32), "rn": _sb([128, 8], F32),
-    "dd": _sb([128, 8, 17], F32), "be": _sb([128, 8, 17], F32), "rm": _sb([128, 8, 17], F32), "ww": _sb([128, 128], F32), "wt": _sb([128, 128], F32),
-    "wd0": _sb([128, 1024], F32), "wd1": _sb([128, 1024], F32),
+    "dd": _sb([128, 8, 17], F32), "be": _sb([128, 8, 17], F32), "rm": _sb([128, 8, 17], F32),
+    "ww": _sb([128, 128], F32), "wt": _sb([128, 128], F32),
+    "wd0": _sb([128, 8, 128], F32), "wd1": _sb([128, 8, 128], F32), "wd2": _sb([128, 1024], F32),
     "came": _sb([128, 8], F32), "xa": _sb([128, 128], F32), "xb": _sb([128, 128], F32), "crow": _sb([128, 128], F32),
     "v0": _sb([128, 128], F32), "cd": _sb([128, 8], F32), "whole": _sb([128, 8], F32), "cut": _sb([128, 8], F32),
     "cutw": _sb([128, 8], F32), "delta": _sb([128, 8], F32), "tt": _sb([128, 1024], BF),
@@ -194,12 +196,12 @@ def rank_program(g, core, T, topo):
     const(G, [], ["i2"], iota(T.i2[:], [[64, 4], [512, 2]], 0, 0, True))
     const(G, [], ["i3"], iota(T.i3[:], [[8, 4], [64, 2]], 0, 0, True))
     const(V, [], ["nd"], lambda e, s: e.memset(T.nd[:], 0.0))
-    const(V, [], ["ones", "cc"], lambda e, s: [e.memset(T.ones[:], 1.0), e.memset(T.cc[0:1, :], 0.0),
-                                               e.memset(T.cs[0:1, :, 1:17], 1.75), e.memset(T.cs[0:1, :, 0], 0.0)])
+    const(V, [], ["ones", "cc", "half"], lambda e, s: [
+        e.memset(T.ones[:], 1.0), e.memset(T.cc[0:1, :], 0.0), e.memset(T.half[:], 0.5),
+        e.memset(T.cs[0:1, :, 1:17], 1.75), e.memset(T.cs[0:1, :, 0], 0.0)])
     const(S, ["nd"], ["qd"], lambda e, s: [
         e.activation(T.qd[:, 1024 * x:1024 * x + 1024], T.nd[:], ACT.Identity) for x in range(4)])
-    const(S, ["nd"], ["wd0", "wd1"], lambda e, s: [
-        e.activation(T.wd0[:], T.nd[:], ACT.Identity), e.activation(T.wd1[:], T.nd[:], ACT.Identity)])
+    const(S, ["nd"], ["wd0"], act(T.wd0[:], T.nd[:], ACT.Sigmoid, bias=-200.0))
     fl = dict(allow_small_or_imprecise_dtypes=True)
     const(G, [], ["cb", "ff0", "ff1", "ax0", "ax1", "d1", "pgx", "em0"], lambda e, s: [
         e.iota(T.cb[0:1, :], [[-1, 2], [0, 128]], 1, 0, **fl),
@@ -208,12 +210,12 @@ def rank_program(g, core, T, topo):
         e.iota(T.d1[:], [[0, 136]], 0, 0, **fl),
         e.iota(T.em[:, 16:17], [[0, 1]], 0, 0, **fl), e.iota(T.pg[:, W:W + 128], [[0, 128]], 0, 0)])
     const(G, [], ["d1"], iota(T.d1[:, 0::17], [[0, 8]], 1, 0, True))
+    const(G, [], ["ig"], iota(T.ig[:], [[-1, 8], [0, 16]], 8, 1))
     pp = [[-1, 8], [-8, 4], [-32, 4]]
     const(G, ["ones"], ["pm"], lambda e, s: [
         e.affine_select(T.pm[:, 0:128], T.ones[:, 0:128], pp, A.is_equal, 0.0, 0, 1),
         e.affine_select(T.pm[:, 128:256], T.ones[:, 0:128], pp, A.is_equal, 0.0, 0, 1)])
     const(G, ["ones"], ["bo0"], sel(T.bo0[:], T.ones[:, 0:128], [[-16, 8], [0, 16]], A.is_ge, 0, 1))
-    const(G, [], ["ig"], iota(T.ig[:], [[-1, 8], [0, 16]], 8, 1))
     const(G, ["ones"], ["id2"], sel(T.id2[:], T.ones[:], [[0, 2], [-1, 128]], A.is_equal, 0, 1))
     const(G, ["bo0"], ["bof"], sel(T.bof[:], T.bo0[:], [[16, 8], [0, 16]], A.is_ge, 15, -1))
     const(G, ["ones"], ["idb"], sel(T.idb[:], T.ones[:, 0:128], [[-1, 128]], A.is_equal, 0, 1))
@@ -223,6 +225,9 @@ def rank_program(g, core, T, topo):
     const(G, ["ones"], ["jr0"], sel(T.jr[:], T.ones[:], [[-8, 16], [0, 2], [-1, 8]], A.is_equal, 0, 1))
     const(G, ["jr0"], ["jr"], lambda e, s: [
         e.affine_select(T["jr%d" % u][:], T.jr[:, :, 8 - u:16 - u], [[0, 128]], A.is_ge, 0.0, 0, 0) for u in (1, 2)])
+    const(G, ["ones"], ["segm"], sel(T.segm[:], T.ones[:, 0:128], [[0, 8], [1, 16]], A.is_gt, 0, 0))
+    const(G, [], ["wd1"], iota(T.wd1[:], [[0, 1024]], 0, 0, True))
+    const(G, [], ["wd2"], iota(T.wd2[:], [[0, 1024]], 0, 0, True))
 
     sh, an = A.logical_shift_right, A.bitwise_and
     const(V, ["ip"], ["ib"], lambda e, s: [
@@ -280,26 +285,20 @@ def rank_program(g, core, T, topo):
             e.memset(T.tha[:], 0.0625),
             e.tensor_scalar(fc[10], T.ma[:, 15:16], -1.0, 1.0, A.mult, A.add),
             e.tensor_copy(T.came[:], T.sti[:])])
-        const(V, [], ["tha"], lambda e, s: e.memset(T.tha[:, 0::17], 2.0))
-
-    def late_constants_a():
-        const(V, ["ones"], ["half", "segm"], lambda e, s: [
-            e.tensor_scalar(T.half[:], T.ones[:, 0:128], 0.5, None, A.mult), e.memset(T.segm[:], 1.0)])
         const(V, ["ig"], ["ig2"], ts(T.ig2[:], T.ig[:], 7, None, an))
         const(V, ["half", "ones"], ["pw"], lambda e, s: e.tensor_tensor_scan(
             T.pw[:], T.half[:], T.ones[:, 0:128], 2.0 ** 64, A.mult, A.mult))
+        const(V, [], ["tha"], lambda e, s: e.memset(T.tha[:, 0::17], 2.0))
         const(V, ["ig2"], ["selg"], ts(T.selg[:], T.ig2[:], 0.0, None, A.is_equal))
         const(G, ["selg"], ["sel15"], sel(T.sel15[:], T.selg[:], [[0, 8], [1, 16]], A.is_equal, -15, 0))
-
-    def late_constants_b():
-        const(V, [], ["segm"], lambda e, s: e.memset(T.segm[:, 0::16], 0.0))
         const(V, ["pw", "ma"], ["pw2", "pa"], lambda e, s: [
             e.tensor_tensor(T.pw2[:], T.pw[:], T.ma[:], A.mult),
             e.tensor_tensor(T.pa[:], T.pw[:, 63:79], T.ma[:, 0:16], A.mult)])
-        const(V, ["pw2", "pa"], ["thr", "fc11"], lambda e, s: [
-            e.tensor_scalar(T.thr[:], T.pw2[:], 2.5, None, A.mult),
-            e.tensor_reduce(fc[11], T.pa[:], AxisListType.X, A.add)])
-        const(V, ["fc11", "pw"], ["colw"], ts(T.colw[:], T.pw[:, 0::16], fc[11], None, A.mult))
+        const(V, ["pa"], ["fc11"], lambda e, s: e.tensor_reduce(fc[11], T.pa[:], AxisListType.X, A.add))
+
+    def late_constants():
+        const(S, ["pw2"], ["thr"], act(T.thr[:], T.pw2[:], ACT.Identity, scale=2.5))
+        const(S, ["fc11", "pw"], ["colw"], act(T.colw[:], T.pw[:, 0::16], ACT.Identity, scale=fc[11]))
 
     RX = T.px[:, 2, 0:128]
 
@@ -317,17 +316,19 @@ def rank_program(g, core, T, topo):
     def turn_w():
         op(P, "wtp", ["ww", "id2"], ["pz"], mm(T.pz[:, 0:128], T.ww[:], T.id2[:, 0:128]))
 
-    def take_w():
-        op(V, "wtc", ["pz"], ["wt"], cp(T.wt[:], T.pz[:, 0:128]))
-
-    def spread_w(n, taken=False):
+    def spread_w(n):
         wd = "wd%d" % (n % 2)
-        if not taken:
-            take_w()
-        op(V, "wds", ["wt", "lists"], [wd], cp(T[wd][:, 0:1024].indirect(T.lw[:]), T.wt[:]))
+        op(V, "wtc", ["pz"], ["wt"], cp(T.wt[:], T.pz[:, 0:128]))
+        if n >= 7:
+            op(V, "wds", ["wt", "lists"], ["wd2"], cp(T.wd2[:, 0:1024].indirect(T.lw[:]), T.wt[:]))
+        else:
+            op(Y, "wdd", ["wt"], [wd], lambda e, s: [
+                e.dma_start(T[wd][16 * x:16 * x + 16, x, :], T.wt[16 * x:16 * x + 16, :]) for x in range(8)], 16)
 
     def acc_in(t):
         op(P, "arot", ["ain%d" % t, "id2"], ["px"], mm(RX, T.id2[:, 128 - 16 * t:256 - 16 * t], T["ain%d" % t][:]))
+
+    def acc_take():
         op(V, "accr", ["px"], ["accr"], cp(T.accr[:], RX))
 
     def turn_v():
@@ -337,19 +338,25 @@ def rank_program(g, core, T, topo):
                 for x in range(8)])
 
     def sigmoid(n):
-        vs = "vs%d" % (n % 2)
+        vs = "vs%d" % (n % 3)
         for half, b in enumerate(("pva", "pvb")):
             op(S, "sg" + b, [b], [vs + b], act(T[vs][:, 1024 * half:1024 * half + 1024], T[b][:], ACT.Sigmoid))
 
-    def acc_open():
-        for b in ("paa", "pab"):
-            op(P, "ai" + b, ["cb", "cc"], [b], lambda e, s: e.matmul(T[b][:], T.cb[0:1, 128:256], T.cc[0:1, :], True, False))
+    def acc_open(half):
+        b = ("paa", "pab")[half]
+        op(P, "ai" + b, ["cb", "cc"], [b], lambda e, s: e.matmul(T[b][:], T.cb[0:1, 128:256], T.cc[0:1, :], True, False))
 
     def acc_add(n, half):
-        b, vs, wd = ("paa", "pab")[half], "vs%d" % (n % 2), "wd%d" % (n % 2)
+        b, vs, wd = ("paa", "pab")[half], "vs%d" % (n % 3), "wd%d" % (2 if n >= 7 else n % 2)
+
+        def spread(jl):
+            if n >= 7:
+                return T.wd2[:, 64 * jl:64 * jl + 64]
+            p = 32 * (jl % 4) + 8 * (jl // 4)
+            return T[wd][:, :, p:p + 8]
         op(P, "am" + b, [vs + ("pva", "pvb")[half], wd], [b], lambda e, s: [
             e.matmul(T[b][:, 64 * x:64 * x + 64], T[vs][:, 1024 * half + 128 * x:1024 * half + 128 * x + 128],
-                     T[wd][:, 512 * half + 64 * x:512 * half + 64 * x + 64], False, n % 3 == 2 and x == 7) for x in range(8)])
+                     spread(8 * half + x), False, n % 3 == 2 and x == 7) for x in range(8)])
 
     def acc_out(q, half):
         b, o = ("paa", "pab")[half], T.accs[:, 512 * half:512 * half + 512]
@@ -360,12 +367,15 @@ def rank_program(g, core, T, topo):
         return T.accs[:, 0:1024].indirect(T.lx[:])
 
     def report(t):
-        acn, yo = "acn%d" % t, "yo%d" % t
+        acn = "acn%d" % t
         if t == 0:
             op(V, "acn", ACCS, [acn], cp(T[acn][:], picked()))
         else:
             op(V, "acn", ACCS + ["accr"], [acn], tt(T[acn][:], picked(), T.accr[:], A.add))
         send("sa%d" % t, T["ain%d" % (t + 1)][:], T[acn][:], "aa%d" % (t + 1), [acn])
+
+    def output(t):
+        acn, yo = "acn%d" % t, "yo%d" % t
         op(V, "yo", [acn, "rep"], [yo], tt(T[yo][:], T[acn][:], T.rep[:], A.add))
         dma("st%d" % t, T.ya[:, 128 * t:128 * t + 128], T[yo][:], [yo], [])
 
@@ -380,13 +390,13 @@ def rank_program(g, core, T, topo):
         op(V, "rep", ["sg", "px"], ["rep"], tt(T.rep[:], T.sg[:], RX, A.mult))
 
     def kchunk(q, nm, a, b, name):
-        o, i = T.kg[:, 256 * a:256 * b], T.kx[:, 0:W].indirect(T[nm][:, 16 * a:16 * b])
+        o, i = T.kg[:, 128 * a:128 * b], T.kx[:, 0:W].indirect(T[nm][:, 8 * a:8 * b])
         op(q, name, ["kx", nm], ["kg%d" % x for x in range(a, b)], cp(o, i) if q == V else act(o, i, ACT.Identity))
 
     def scores(a, b, name, stops):
         op(P, name, ["qd"] + ["kg%d" % x for x in range(a, b)], ["ps"], lambda e, s: [
             e.matmul(T.ps[:, m // 4, :, 1:17], T.qd[:, 128 * m:128 * m + 128], T.kg[:, 64 * m:64 * m + 64],
-                     False, m in stops) for m in range(4 * a, 4 * b)])
+                     False, m in stops) for m in range(2 * a, 2 * b)])
 
     for n in range(9):
         t, h = divmod(n, 3)
@@ -396,9 +406,9 @@ def rank_program(g, core, T, topo):
         came, camek = (T.came, "came") if t == 0 else (T[msg], msg)
         qk, qkk = (T.ds4[:], "lists") if h == 0 else (T.sc[:, 136::17], "scq")
         end = n == 8
-        split = 6 if end else (5 if h > 0 else 4)
-        mid = 4 if split == 6 else 3
-        stops = (15, 31 if (end or split == 4) else 4 * split - 1)
+        split = 12 if end else (SPLIT if h > 0 else 8)
+        mid = 8 if end else (MID if h > 0 else 6)
+        stops = (15, 31 if (end or split == 8) else 2 * split - 1)
 
         op(P, "si", ["cb", "cc"], ["ps"], lambda e, s: [
             e.matmul(T.ps[:, 4 * x:4 * x + 4, :, 0:17], T.cb[0:1, 0:128], T.cs[0:1], True, False) for x in (0, 1)])
@@ -408,26 +418,21 @@ def rank_program(g, core, T, topo):
         op(V, "nm", PG + [cl], [nm], cp(T[nm][:], T.pg[:, 0:W].indirect(T[cl][:, 0:8])))
         if n == 0:
             first_constants()
-        if h == 0 and t > 0:
-            spread_w(n - 1, True)
-        if h == 2 and t > 0:
-            report(t - 1)
-        if h == 2:
+        if n in (3, 4, 6, 7):
             acc_add(n - 2, 0)
-        elif t > 0:
-            acc_add(n - 2, 1)
         qscale = -1.0 / 1024
         if h > 0:
-            op(S, "qs", ["kx", "kxx", cl], ["qs"],
-               act(T.qs[:], T.kx[:, 0:W + 128].indirect(T[cl][:, 8:16]), ACT.Identity, scale=qscale))
+            op(V, "qsv", ["kx", "kxx", cl], ["qs"],
+               ts(T.qs[:], T.kx[:, 0:W + 128].indirect(T[cl][:, 8:16]), qscale, None, A.mult))
             turn_v()
         elif t == 0:
             op(S, "qs", ["kx", cl], ["qs"], act(T.qs[:], T.kx[:, 0:W].indirect(T[cl][:, 0:8]), ACT.Identity, scale=qscale))
         else:
             op(S, "qs", ["px"], ["qs"], act(T.qs[:], RX, ACT.Identity, scale=qscale))
         if end:
-            acc_add(n - 2, 1)
+            acc_add(n - 2, 0)
             weights(n - 1, 3)
+            acc_out(S, 1)
             weights(n - 1, 1)
         op(V, "nd", [nm, "lists"], ["nd"], cp(T.nd[:, 0:1024].indirect(T.ln[:]), T[nm][:]))
         if end:
@@ -437,59 +442,78 @@ def rank_program(g, core, T, topo):
             op(P, "dn", ["nd", "em"], ["px"], lambda e, s: [
                 e.matmul(T.px[:, 0:2, 17 * x:17 * x + 17], T.nd[:, 128 * x:128 * x + 128], T.em[:], True, True)
                 for x in range(8)])
-        kchunk(V, nm, 0, 2, "k0")
+        kchunk(V, nm, 0, 4, "k0")
         if not end:
-            kchunk(S, nm, split, 8, "k3")
+            kchunk(S, nm, split, 16, "k3")
         if h == 0:
             op(S, "kxx", ["qs"], ["kxx"], act(T.kx[:, W:W + 128], T.qs[:], ACT.Identity, scale=-1024.0))
+            if n == 0:
+                late_constants()
         else:
             if not end:
                 weights(n - 1, 3)
-            if h == 1 and t > 0:
+            if n in (4, 7):
+                acc_out(S, 0)
+            if n == 5:
                 acc_out(S, 1)
             sigmoid(n - 1)
         op(V, "qd", ["qs", "lists"], ["qd"], cp(T.qd[:, 0:4096].indirect(T.lq[:]), T.qs[:]))
-        scores(0, 2, "sco0", stops)
+        scores(0, 4, "sco0", stops)
         if h > 0 and not end:
-            scores(split, 8, "sco3", stops)
+            scores(split, 16, "sco3", stops)
         op(V, "nv", ["nd", "lists"], ["nv"], cp(T.nv[:], T.nd[:, 0:1024].indirect(T.lv[:])))
         for x, b in enumerate(("pva", "pvb")):
             op(S, "vg" + b, ["vv", "nv"], ["vg" + b], act(
                 T.vg[:, 1024 * x:1024 * x + 1024], T.vv[:, 0:W].indirect(T.nv[:, 64 * x:64 * x + 64]), ACT.Identity))
         if h == 0:
-            scores(split, 8, "sco3", stops)
+            scores(split, 16, "sco3", stops)
         if end:
+            report(t - 1)
+            acc_open(1)
+            acc_add(n - 2, 1)
             spread_w(n - 1)
             acc_add(n - 1, 0)
-        kchunk(V, nm, 2, mid, "k1")
-        scores(2, mid, "sco1", stops)
+        kchunk(V, nm, 4, mid, "k1")
+        scores(4, mid, "sco1", stops)
         kchunk(V, nm, mid, split, "k2")
         scores(mid, split, "sco2", stops)
         if end:
-            kchunk(V, nm, 6, 8, "k3v")
-            scores(6, 8, "sco3", stops)
+            kchunk(V, nm, 12, 16, "k3v")
+            scores(12, 16, "sco3", stops)
             turn_v()
             acc_add(n - 1, 1)
         elif h > 0:
             weights(n - 1)
             turn_w()
-        elif t == 0:
-            late_constants_a()
-        else:
+            if n == 7:
+                acc_in(1)
+        elif t > 0:
             op(V, "d1", [msg], ["d1"], cp(T.d1[:, 0::17], T[msg][:, 8:16]))
             rest_row()
+            if n == 6:
+                report(0)
+                output(0)
+        if h == 0 and t < 2:
+            op(V, "xa", [camek, "ma", "lists"], ["xa"], tt(T.xa[:], came[:, 0:8].indirect(T.lj[:]), T.ma[:], A.mult))
+            op(V, "v0", [nm, "em"], ["v0"], ts(T.v0[:], T[nm][:], fc[10], None, A.mult))
+            op(P, "crp", ["xa", "bof"], ["pz"], mm(T.pz[:, 0:128], T.bof[:], T.xa[:]))
         if h == 2 and not end:
+            acc_open(1)
+        if n in (2, 3, 4, 5, 6, 7):
             acc_add(n - 2, 1)
-        if h == 0 and t > 0:
-            acc_add(n - 1, 0)
-            acc_out(S, 0)
         if h == 1:
-            acc_open()
+            acc_open(0)
         op(V, "clamp", ["ps"], [ff], lambda e, s: [
             e.tensor_scalar(T[ff][32 * b:32 * b + 32, 0:136], T.ps[32 * b:32 * b + 32, :, b, 0:17], 0.0625, 1.0, A.max, A.min)
             for b in range(4)])
         if not end:
             op(V, "g2", [qkk, "px"], ["px", "g2"], tt(T.px[:, 1, 16:136:17], qk, T.px[:, 1, 16:136:17], A.add))
+        if h > 0 and not end:
+            spread_w(n - 1)
+        if n == 7:
+            acc_take()
+        if h == 0 and t < 2:
+            op(V, "crow", ["pz"], ["crow"], cp(T.crow[:], T.pz[:, 0:128]))
         r0 = 128 + 136 * (n % 2)
         rall, r15 = T.pz[:, r0:r0 + 136], T.pz[:, r0 + 16:r0 + 136:17]
         op(V, "rs", [ff, "d1"], [rs, "pz"], lambda e, s: e.tensor_tensor_scan(
@@ -510,6 +534,8 @@ def rank_program(g, core, T, topo):
             spread_w(n)
             sigmoid(n)
             acc_in(t)
+            acc_take()
+            output(t - 1)
             acc_add(n, 0)
             acc_add(n, 1)
             acc_out(V, 0)
@@ -519,55 +545,39 @@ def rank_program(g, core, T, topo):
             break
         op(V, "ax", [rs, "pz", "tha"], [ax], tt(T[ax][:, 0:136], rall, T.tha[:], A.is_ge))
         op(V, "dead", [rs, "pz"], ["dead"], ts(T.dead[:], r15, 0.0625, None, A.is_lt))
-
-        def first_on():
-            op(V, "on", [], [ax], lambda e, s: e.memset(T[ax][:, 0:136:17], 1.0))
         op(V, "sc", [ax, "px"], ["sc"], lambda e, s: e.tensor_tensor_scan(
             T.sc[:, 135::-1], T[ax][:, 136:0:-1], T.px[:, 0, 135::-1], 0.0, A.mult, A.add))
-        if not end:
-            op(V, "scq", [ax, "px", "g2"], ["scq"], lambda e, s: e.tensor_tensor_scan(
-                T.sc[:, 271:135:-1], T[ax][:, 136:0:-1], T.px[:, 1, 135::-1], 0.0, A.mult, A.add))
-            op(P, "pc", ["sc", "scq", "pm"], ["px"], mm(T.px[:, 0, 136:152], T.pm[:, 0:128], T.sc[:, 0::17]))
-            first_on()
+        op(V, "scq", [ax, "px", "g2"], ["scq"], lambda e, s: e.tensor_tensor_scan(
+            T.sc[:, 271:135:-1], T[ax][:, 136:0:-1], T.px[:, 1, 135::-1], 0.0, A.mult, A.add))
+        op(P, "pc", ["sc", "scq", "pm"], ["px"], mm(T.px[:, 0, 136:152], T.pm[:, 0:128], T.sc[:, 0::17]))
         cs = T.sc[:, 0:136:17]
 
         def lists():
             op(V, "cvc", ["px"], [cn], cp(T[cn][:], T.px[:, 0, 136:152]))
         if h < 2:
+            op(G, "on", [], [ax], iota(T[ax][:, 0:136:17], [[0, 8]], 1, 0, True))
             op(V, "d1", ["dead", rs, "pz"], ["d1"], tt(T.d1[:, 0::17], T.dead[:], r15, A.max))
-            if h > 0:
-                spread_w(n - 1)
-                lists()
-            elif t < 2:
-                if t == 0:
-                    late_constants_b()
-                op(V, "xa", [camek, "ma", "lists"], ["xa"], tt(T.xa[:], came[:, 0:8].indirect(T.lj[:]), T.ma[:], A.mult))
+            if h == 0 and t < 2:
                 op(V, "cd", [camek, "lists"], ["cd"], tt(T.cd[:], came[:, 0:8], T.dum[:], A.subtract))
-                op(P, "crp", ["xa", "bof"], ["pz"], mm(T.pz[:, 0:128], T.bof[:], T.xa[:]))
-                lists()
-                op(V, "v0", [nm, "em"], ["v0"], ts(T.v0[:], T[nm][:], fc[10], None, A.mult))
-                op(V, "crow", ["pz"], ["crow"], cp(T.crow[:], T.pz[:, 0:128]))
-            else:
-                lists()
-                acc_in(t - 1)
-        elif t < 2:
+            lists()
+        else:
             u, snd = t + 1, "snd%d" % t
             op(V, "rn", ["dead", rs, "pz"], ["rn"], tt(T.rn[:], T.dead[:], r15, A.max))
             op(V, "cut", ["whole", "dead"], ["cut"], tt(T.cut[:], T.whole[:], T.dead[:], A.mult))
-            take_w()
+            op(P, "pq", ["sc", "rn", "pm", "jr"], ["pz"], lambda e, s: [
+                e.matmul(T.pz[:, 400:408], T.pm[:, 128 - 16 * u:256 - 16 * u], cs, True, True),
+                e.matmul(T.pz[:, 408:416], T["jr%d" % u][:], T.rn[:], True, True)])
             lists()
-            op(P, "pq", ["sc", "rn", "cut", "pm", "jr"], ["px"], lambda e, s: [
-                e.matmul(T.px[:, 1, 136:144], T.pm[:, 128 - 16 * u:256 - 16 * u], cs, True, True),
-                e.matmul(T.px[:, 1, 144:152], T["jr%d" % u][:], T.rn[:], True, True),
-                e.matmul(T.px[:, 1, 152:160], T.pm[:, 0:128], T.cut[:], True, True)])
+            op(P, "pcut", ["cut", "pm"], ["px"], mm(T.px[:, 1, 152:160], T.pm[:, 0:128], T.cut[:]))
             op(V, "snb", ["kx", "kxx", cn], [snd + "b"], cp(T[snd][:, 16:144], T.kx[:, 0:W + 128].indirect(T[cn][:, 8:16])))
-            op(V, "xa", ["sc", "ms", "lists"], ["xa"], tt(T.xa[:], T.sc[:, 0:136].indirect(T.lc[:]), T.ms[:], A.mult))
-            op(V, "sna", ["px"], [snd + "a"], cp(T[snd][:, 0:16], T.px[:, 1, 136:152]))
+            op(V, "sna", ["pz"], [snd + "a"], cp(T[snd][:, 0:16], T.pz[:, 400:416]))
             send("sm%d" % t, T["msg%d" % u][:], T[snd][:], "am%d" % u, [snd + "a", snd + "b"])
             op(V, "cutw", ["px", "colw", "cd"], ["cutw", "delta"], lambda e, s: [
                 e.tensor_tensor(T.cutw[:], T.px[:, 1, 152:160], T.colw[:], A.mult),
                 e.tensor_tensor(T.delta[:], T.px[:, 1, 152:160], T.cd[:], A.mult)])
+            op(V, "xa", ["sc", "ms", "lists"], ["xa"], tt(T.xa[:], T.sc[:, 0:136].indirect(T.lc[:]), T.ms[:], A.mult))
             op(P, "c15", ["xa", "sel15"], ["px"], mm(RX, T.sel15[:], T.xa[:]))
+            op(V, "onv", [], [ax], lambda e, s: e.memset(T[ax][:, 0:136:17], 1.0))
             op(V, "tt", ["crow", camek, "cutw"], ["tt"], lambda e, s: [
                 e.tensor_scalar(T.tt[:, 144 * x:128 * x + 128], T.crow[:, 16 * x:128], came[:, x:x + 1], T.cutw[:, x:x + 1],
                                 A.is_equal, A.mult) for x in range(8)])
@@ -575,21 +585,20 @@ def rank_program(g, core, T, topo):
                 e.matmul(T.pz[:, 16 * x:128], T.bob[:], T.tt[:, 144 * x:128 * x + 128], x == 0, x == 7)
                 for x in range(8)])
             turn_v()
-            spread_w(n - 1, True)
-            op(V, "win", ["pz", "thr"], ["win"], tt(T.win[:], T.pz[:, 0:128], T.thr[:], A.is_lt))
             weights(n, 0)
+            op(V, "vals", ["v0", "px"], ["vals"], tt(T.vals[:], T.v0[:], RX, A.add))
+            op(V, "win", ["pz", "thr"], ["win"], tt(T.win[:], T.pz[:, 0:128], T.thr[:], A.is_lt))
+            weights(n, 1)
             op(V, "wsum", ["win", "segm"], ["wsum"], lambda e, s: e.tensor_tensor_scan(
                 T.wsum[:], T.segm[:], T.win[:], 0.0, A.mult, A.add))
-            weights(n, 1)
-            op(V, "t1", ["wsum", "delta"], ["t1"], tt(T.t1[:], T.wsum[:, 15::16], T.delta[:], A.mult))
             weights(n, 2)
             turn_w()
-            acc_add(n - 1, 0)
+            acc_add(n - 2, 0)
+            op(V, "t1", ["wsum", "delta"], ["t1"], tt(T.t1[:], T.wsum[:, 15::16], T.delta[:], A.mult))
             op(V, "t2", ["t1", "lists"], ["t2"], tt(T.t2[:], T.t1[:], T.dum[:], A.add))
-            op(V, "vals", ["v0", "px"], ["vals"], tt(T.vals[:], T.v0[:], RX, A.add))
             op(V, "offs", ["t2"], ["offs"], cp(T.offs[:], T.t2[:]))
-            take_w()
             op(V, "cutp", ["vals", "offs"], PG, cp(T.pg[:, 0:W + 128].indirect(T.offs[:]), T.vals[:]))
+            spread_w(n)
             rest_value(cn)
             sigmoid(n)
 

@@ -1,8 +1,20 @@
 from concourse.mybir import AluOpType, AxisListType, ActivationFunctionType
 
 W = 4096
-SPLIT, MID = 10, 8
 F32, BF, I32, U16 = "float32", "bfloat16", "int32", "uint16"
+SHARE = (4, 4, 4, 6, 4, 4, 6, 5, 4)
+FILL = ((0, 0, 0, 0, 0), (0, 0, 0, 0, 0), (1, 0, 0, 0, 3), (2, 0, 0, 2, 3), (5, 1, 0, 0, 0), (2, 1, 0, 0, 3),
+        (3, 0, 0, 0, 8), (0, 0, 1, 1, 3), (2, 2, 0, 1, 6), (1,))
+WIN = (1, 5)
+NEAR = 6
+PARTS = 2
+GAPS = ((0, 0, 0, 0, 0), (1, 1, 0, 1, 1), (1, 1, 1, 0, 1), (0, 0, 0, 1, 0), (1, 1, 1, 2, 1), (2, 1, 1, 0, 0), (0, 1, 1, 1, 0), (1, 1, 0, 0, 1), (0, 1, 0, 1, 1))
+STEPS = (4, 4, 4, 4, 4, 4, 4, 4, 4)
+OUT = (4, 6)
+KEYS = (2,)
+QAT = (1, 1)
+WAT = (2, 2)
+LATE = (1, 1, 1, 1, 1, 1, 1, 1, 0)
 
 
 def _sb(shape, dtype):
@@ -10,49 +22,47 @@ def _sb(shape, dtype):
 
 
 SCRATCH = {
-    "kx": _sb([128, W + 128], BF), "vv": _sb([128, W], BF), "bpi": _sb([128, W // 2], I32),
-    "pg": _sb([128, W + 128], I32), "sti": _sb([128, 8], I32),
+    "kx": _sb([128, W + 256], BF), "vv": _sb([128, W], BF), "bpi": _sb([128, W // 2], I32),
+    "pg": _sb([128, W + 128], I32), "sti": _sb([128, 8], I32), "idm": _sb([128, W], F32),
     "cl0": _sb([128, 16], U16), "cl1": _sb([128, 16], U16),
-    "nm0": _sb([128, 128], U16), "nm1": _sb([128, 128], U16),
-    "qs": _sb([128, 128], BF), "qd": _sb([128, 4096], BF), "nd": _sb([128, 1024], F32),
-    "kg": _sb([128, 2048], BF), "vg": _sb([128, 2048], BF), "nv": _sb([128, 128], U16),
-    "lv": _sb([128, 8], U16), "i3": _sb([128, 8], F32), "fd": _sb([128, 2], F32),
-    "vs0": _sb([128, 2048], F32), "vs1": _sb([128, 2048], F32), "vs2": _sb([128, 2048], F32),
-    "ff0": _sb([128, 137], F32), "ff1": _sb([128, 137], F32),
-    "ax0": _sb([128, 137], F32), "ax1": _sb([128, 137], F32), "tha": _sb([128, 136], F32),
-    "d1": _sb([128, 136], F32), "sc": _sb([128, 272], F32),
-    "dead": _sb([128, 8], F32), "rn": _sb([128, 8], F32),
-    "dd": _sb([128, 8, 17], F32), "be": _sb([128, 8, 17], F32), "rm": _sb([128, 8, 17], F32),
-    "ww": _sb([128, 128], F32), "wt": _sb([128, 128], F32),
-    "wd0": _sb([128, 8, 128], F32), "wd1": _sb([128, 8, 128], F32), "wd2": _sb([128, 1024], F32),
-    "came": _sb([128, 8], F32), "xa": _sb([128, 128], F32), "xb": _sb([128, 128], F32), "crow": _sb([128, 128], F32),
-    "v0": _sb([128, 128], F32), "cd": _sb([128, 8], F32), "whole": _sb([128, 8], F32), "cut": _sb([128, 8], F32),
-    "cutw": _sb([128, 8], F32), "delta": _sb([128, 8], F32), "tt": _sb([128, 1024], BF),
-    "win": _sb([128, 128], F32), "wsum": _sb([128, 128], F32), "t1": _sb([128, 8], F32), "t2": _sb([128, 8], F32),
-    "offs": _sb([128, 8], U16), "vals": _sb([128, 128], F32),
+    "nm0": _sb([128, 128], U16), "nm1": _sb([128, 128], U16), "nv0": _sb([128, 128], U16), "nv1": _sb([128, 128], U16),
+    "qd": _sb([128, W + 64], BF), "nd": _sb([128, 1024], F32),
+    "kg": _sb([128, 2048], BF), "vg0": _sb([128, 2048], BF), "vg1": _sb([128, 2048], BF),
+    "vs0": _sb([128, 16, 128], F32), "vs1": _sb([128, 16, 128], F32), "vs2": _sb([128, 16, 128], F32),
+    "ff": _sb([128, 136], F32), "be": _sb([128, 8, 17], F32), "ww": _sb([128, 128], F32),
+    "dx0": _sb([128, 136], BF), "dx1": _sb([128, 136], BF), "dx2": _sb([128, 136], BF),
+    "e3": _sb([128, 8, 17], F32), "ee": _sb([128, 128], F32),
+    "d1": _sb([128, 136], F32), "sc": _sb([128, 136], F32), "rn": _sb([128, 8], F32),
+    "wt0": _sb([128, 128], F32), "wt1": _sb([128, 128], F32),
+    "wd0": _sb([128, 8, 128], F32), "wd1": _sb([128, 8, 128], F32), "wd2": _sb([128, 8, 128], F32),
+    "we0": _sb([128, 1024], F32), "we1": _sb([128, 1024], F32),
+    "xb": _sb([128, 128], F32), "crow": _sb([128, 128], F32), "v0": _sb([128, 128], F32), "cd": _sb([128, 8], F32),
+    "cut": _sb([128, 8], F32), "to": _sb([128, 8], F32), "tt": _sb([128, 8, 8, 17], BF),
+    "t2": _sb([128, 8], F32), "win": _sb([128, 136], F32), "so": _sb([128, 136], F32), "offs": _sb([128, 8], U16), "vals": _sb([128, 128], F32),
     "sg": _sb([128, 128], F32), "rep": _sb([128, 128], F32), "accs": _sb([128, 1024], F32),
     "accr": _sb([128, 128], F32), "yo0": _sb([128, 128], F32), "yo1": _sb([128, 128], F32), "yo2": _sb([128, 128], F32),
+    "snc0": _sb([128, 8], U16), "snc1": _sb([128, 8], U16),
+    "cin0": _sb([128, 8], U16), "cin1": _sb([128, 8], U16), "cin2": _sb([128, 8], U16),
     "snd0": _sb([128, 144], F32), "snd1": _sb([128, 144], F32), "msg1": _sb([128, 144], F32), "msg2": _sb([128, 144], F32),
     "acn0": _sb([128, 128], F32), "acn1": _sb([128, 128], F32), "ain1": _sb([128, 128], F32), "ain2": _sb([128, 128], F32),
     "ip": _sb([128, 1], I32), "ib": _sb([128, 8], I32), "fb": _sb([128, 8], F32), "fc": _sb([128, 12], F32),
-    "ij": _sb([128, 8], F32), "i2": _sb([128, 8], F32), "ia": _sb([128, 128], I32), "ia2": _sb([128, 128], I32),
-    "ma": _sb([128, 128], F32), "em": _sb([128, 34], F32), "ig": _sb([128, 128], I32), "ig2": _sb([128, 128], I32),
-    "ones": _sb([128, 256], F32), "pm": _sb([128, 256], F32), "id2": _sb([128, 256], F32), "idb": _sb([128, 128], BF),
+    "ij": _sb([128, 8], F32), "i2": _sb([128, 8], F32), "i5": _sb([128, 1024], F32), "ibias": _sb([128, 8], F32),
+    "il": _sb([128, 128], F32), "ig": _sb([128, 128], F32), "ik": _sb([128, 160], F32),
+    "ones": _sb([128, 256], F32), "nq": _sb([128, 128], BF), "pm": _sb([128, 256], F32), "id2": _sb([128, 256], F32),
+    "idb": _sb([128, 128], BF), "pmb": _sb([128, 128], BF), "npb": _sb([128, 128], BF),
     "jr": _sb([128, 16, 16], F32), "jr1": _sb([128, 128], F32), "jr2": _sb([128, 128], F32),
-    "bo0": _sb([128, 128], F32), "bof": _sb([128, 128], F32), "bob": _sb([128, 128], BF),
-    "ms0": _sb([128, 128], F32), "ms": _sb([128, 128], F32), "selg": _sb([128, 128], F32), "sel15": _sb([128, 128], F32),
-    "cb": _sb([128, 256], BF), "cc": _sb([128, 512], BF), "cs": _sb([128, 16, 17], BF),
+    "cs": _sb([128, 16, 17], BF), "kb": _sb([128, 128], BF), "kl": _sb([128, 256], BF), "kr": _sb([128, 3, 8, 17], BF),
+    "ea": _sb([128, 18], F32), "em": _sb([128, 17], F32), "segm": _sb([128, 136], F32),
+    "ma": _sb([128, 128], F32), "ms": _sb([128, 128], F32), "selg": _sb([128, 128], F32), "bob": _sb([128, 128], BF),
     "half": _sb([128, 128], F32), "pw": _sb([128, 128], F32), "pw2": _sb([128, 128], F32),
-    "thr": _sb([128, 128], F32), "segm": _sb([128, 128], F32), "pa": _sb([128, 16], F32), "colw": _sb([128, 8], F32),
-    "dum": _sb([128, 8], F32), "ds4": _sb([128, 8], F32),
-    "lq": _sb([128, 8], U16), "ln": _sb([128, 8], U16), "lx": _sb([128, 8], U16), "lw": _sb([128, 8], U16),
-    "lj": _sb([128, 8], U16), "lc": _sb([128, 8], U16),
-    "ps": ("psum", [128, 8, 4, 32], F32), "pz": ("psum", [128, 512], F32),
+    "thr": _sb([128, 8, 17], F32), "colw": _sb([128, 8], F32), "dum": _sb([128, 8], F32),
+    "lf": _sb([128, 48], F32), "la": _sb([128, 48], U16),
+    "ps": ("psum", [128, 8, 4, 32], F32), "px": ("psum", [128, 512], F32), "pz": ("psum", [128, 512], F32),
     "pva": ("psum", [128, 1024], BF), "pvb": ("psum", [128, 1024], BF),
-    "paa": ("psum", [128, 512], F32), "pab": ("psum", [128, 512], F32), "px": ("psum", [128, 3, 170], F32),
+    "paa": ("psum", [128, 512], F32), "pab": ("psum", [128, 512], F32),
 }
-BANKS = ("ps", "px", "pz", "pva", "pvb", "paa", "pab")
-SEMAPHORES = ["am1", "am2", "aa1", "aa2"] + ["sem%d" % k for k in range(140)]
+BANKS = ("ps0", "ps1", "px", "pz", "pva", "pvb", "paa", "pab")
+SEMAPHORES = ["ac1", "ac2", "am1", "am2", "aa1", "aa2"] + ["sem%d" % k for k in range(140)]
 
 
 def rank_program(g, core, T, topo):
@@ -165,12 +175,15 @@ def rank_program(g, core, T, topo):
     def mm(out, l, r):
         return lambda e, s: e.matmul(out, l, r, True, True)
 
-    def iota(out, pat, base, cm, flt=False):
-        if flt:
-            return lambda e, s: e.iota(out, pat, base, cm, allow_small_or_imprecise_dtypes=True)
-        return lambda e, s: e.iota(out, pat, base, cm)
+    def group(*terms):
+        return lambda e, s: [e.matmul(o, l, r, k == 0, k == len(terms) - 1) for k, (o, l, r) in enumerate(terms)]
 
-    def sel(out, a, pat, o, base, cm):
+    fl = dict(allow_small_or_imprecise_dtypes=True)
+
+    def iota(out, pat, base, cm):
+        return lambda e, s: e.iota(out, pat, base, cm, **fl)
+
+    def sel(out, a, pat, base, cm, o=A.is_equal):
         return lambda e, s: e.affine_select(out, a, pat, o, 0.0, base, cm)
 
     def dma(name, out, a, r, w, q=Y):
@@ -181,190 +194,207 @@ def rank_program(g, core, T, topo):
             e.remote_dma(dst, src, T.sem[rsem], s, pid, rid, out_mask)
         return op(G, name, key, [], fn, out_n)
 
+    codes = T.kx[:, 128:128 + W]
+
+    def qarea(n):
+        return T.kx[:, 0:128] if n % 2 == 0 else T.kx[:, 128 + W:256 + W]
+
+    def qwindow(n):
+        return T.kx[:, 0:128 + W] if n % 2 == 0 else T.kx[:, 128:256 + W]
+
     dma("ld_st", T.sti[:], T.st[:], [], ["sti"], S)
-    dma("ld_b0", T.bpi[:, 0:1024], T.bp[:, 0:1024], [], ["bpi0"])
-    dma("ld_b1", T.bpi[:, 1024:2048], T.bp[:, 1024:2048], [], ["bpi1"])
-    dma("ld_k", T.kx[:, 0:W], T.kt[:], [], ["kx"])
+    for k in range(PARTS):
+        a, b = 2048 * k // PARTS, 2048 * (k + 1) // PARTS
+        dma("ld_b%d" % k, T.bpi[:, a:b], T.bp[:, a:b], [], ["bpi%d" % k])
+    dma("ld_k", codes, T.kt[:], [], ["kx"])
     dma("ld_v", T.vv[:], T.vt[:], [], ["vv"])
     for t in (1, 2):
+        arrival("ac%d" % t, "cin%d" % t)
         arrival("am%d" % t, "msg%d" % t)
         arrival("aa%d" % t, "ain%d" % t)
 
-    const(G, [], ["ip"], iota(T.ip[:], [[0, 1]], 0, 1))
-    const(G, [], ["ia"], iota(T.ia[:], [[0, 8], [-1, 16]], 16, 1))
-    const(G, [], ["ij"], iota(T.ij[:], [[1, 8]], 0, 0, True))
-    const(G, [], ["i2"], iota(T.i2[:], [[64, 4], [512, 2]], 0, 0, True))
-    const(G, [], ["i3"], iota(T.i3[:], [[8, 4], [64, 2]], 0, 0, True))
-    const(V, [], ["nd"], lambda e, s: e.memset(T.nd[:], 0.0))
-    const(V, [], ["ones", "cc", "half"], lambda e, s: [
-        e.memset(T.ones[:], 1.0), e.memset(T.cc[0:1, :], 0.0), e.memset(T.half[:], 0.5),
-        e.memset(T.cs[0:1, :, 1:17], 1.75), e.memset(T.cs[0:1, :, 0], 0.0)])
-    const(S, ["nd"], ["qd"], lambda e, s: [
-        e.activation(T.qd[:, 1024 * x:1024 * x + 1024], T.nd[:], ACT.Identity) for x in range(4)])
-    const(S, ["nd"], ["wd0"], act(T.wd0[:], T.nd[:], ACT.Sigmoid, bias=-200.0))
-    fl = dict(allow_small_or_imprecise_dtypes=True)
-    const(G, [], ["cb", "ff0", "ff1", "ax0", "ax1", "d1", "pgx", "em0"], lambda e, s: [
-        e.iota(T.cb[0:1, :], [[-1, 2], [0, 128]], 1, 0, **fl),
-        e.iota(T.ff0[:, 136:137], [[0, 1]], 0, 0, **fl), e.iota(T.ff1[:, 136:137], [[0, 1]], 0, 0, **fl),
-        e.iota(T.ax0[:, 136:137], [[0, 1]], 0, 0, **fl), e.iota(T.ax1[:, 136:137], [[0, 1]], 0, 0, **fl),
-        e.iota(T.d1[:], [[0, 136]], 0, 0, **fl),
-        e.iota(T.em[:, 16:17], [[0, 1]], 0, 0, **fl), e.iota(T.pg[:, W:W + 128], [[0, 128]], 0, 0)])
-    const(G, [], ["d1"], iota(T.d1[:, 0::17], [[0, 8]], 1, 0, True))
-    const(G, [], ["ig"], iota(T.ig[:], [[-1, 8], [0, 16]], 8, 1))
-    pp = [[-1, 8], [-8, 4], [-32, 4]]
-    const(G, ["ones"], ["pm"], lambda e, s: [
-        e.affine_select(T.pm[:, 0:128], T.ones[:, 0:128], pp, A.is_equal, 0.0, 0, 1),
-        e.affine_select(T.pm[:, 128:256], T.ones[:, 0:128], pp, A.is_equal, 0.0, 0, 1)])
-    const(G, ["ones"], ["bo0"], sel(T.bo0[:], T.ones[:, 0:128], [[-16, 8], [0, 16]], A.is_ge, 0, 1))
-    const(G, ["ones"], ["id2"], sel(T.id2[:], T.ones[:], [[0, 2], [-1, 128]], A.is_equal, 0, 1))
-    const(G, ["bo0"], ["bof"], sel(T.bof[:], T.bo0[:], [[16, 8], [0, 16]], A.is_ge, 15, -1))
-    const(G, ["ones"], ["idb"], sel(T.idb[:], T.ones[:, 0:128], [[-1, 128]], A.is_equal, 0, 1))
-    const(G, ["ones"], ["ms0"], sel(T.ms0[:], T.ones[:, 0:128], [[0, 8], [-8, 4], [-32, 4]], A.is_ge, 0, 1))
-    const(G, ["bo0"], ["bob"], sel(T.bob[:], T.bo0[:], [[16, 8], [0, 16]], A.is_ge, 15, -1))
-    const(G, ["ms0"], ["ms"], sel(T.ms[:], T.ms0[:], [[0, 8], [8, 4], [32, 4]], A.is_ge, 7, -1))
-    const(G, ["ones"], ["jr0"], sel(T.jr[:], T.ones[:], [[-8, 16], [0, 2], [-1, 8]], A.is_equal, 0, 1))
-    const(G, ["jr0"], ["jr"], lambda e, s: [
-        e.affine_select(T["jr%d" % u][:], T.jr[:, :, 8 - u:16 - u], [[0, 128]], A.is_ge, 0.0, 0, 0) for u in (1, 2)])
-    const(G, ["ones"], ["segm"], sel(T.segm[:], T.ones[:, 0:128], [[0, 8], [1, 16]], A.is_gt, 0, 0))
-    const(G, [], ["wd1"], iota(T.wd1[:], [[0, 1024]], 0, 0, True))
-    const(G, [], ["wd2"], iota(T.wd2[:], [[0, 1024]], 0, 0, True))
-
-    sh, an = A.logical_shift_right, A.bitwise_and
-    const(V, ["ip"], ["ib"], lambda e, s: [
-        e.tensor_scalar(T.ib[:, 0:1], T.ip[:], 3, None, an),
-        e.tensor_scalar(T.ib[:, 1:2], T.ip[:], 12, None, an),
-        e.tensor_scalar(T.ib[:, 2:3], T.ip[:], 4, None, sh),
-        e.tensor_scalar(T.ib[:, 3:4], T.ip[:], 8, None, an),
-        e.tensor_scalar(T.ib[:, 4:5], T.ip[:], 7, None, an),
-        e.tensor_scalar(T.ib[:, 5:6], T.ip[:], 15, None, an),
-        e.tensor_scalar(T.ib[:, 6:7], T.ip[:], 3, 3, sh, an),
-        e.tensor_scalar(T.ib[:, 7:8], T.ip[:], 5, None, sh)])
-    const(V, ["ia"], ["ia2"], ts(T.ia2[:], T.ia[:], 15, None, an))
-    const(V, ["ib"], ["fb"], cp(T.fb[:], T.ib[:]))
-    const(V, ["ia2"], ["ma"], ts(T.ma[:], T.ia2[:], 0.0, None, A.is_equal))
+    one = T.ones[:, 0:128]
     fb = [T.fb[:, k:k + 1] for k in range(8)]
     fc = [T.fc[:, k:k + 1] for k in range(12)]
-    const(V, ["fb"], ["fca"], lambda e, s: [
-        e.tensor_scalar(fc[0], fb[0], 32.0, fb[2], A.mult, A.add),
-        e.tensor_scalar(fc[1], fb[0], 64.0, fb[2], A.mult, A.add),
-        e.tensor_scalar(fc[2], fb[3], 32.0, fb[4], A.mult, A.add),
-        e.tensor_scalar(fc[3], fb[6], 4.0, fb[7], A.mult, A.add),
-        e.tensor_scalar(T.fd[:, 0:1], fb[3], 4.0, fb[2], A.mult, A.add)])
-    op(V, "cvc", ["sti"], ["cl0"], cp(T.cl0[:, 0:8], T.sti[:]))
-    const(V, ["fb", "fca"], ["fcb"], lambda e, s: [
-        e.tensor_scalar(fc[4], fb[1], 2.0, fc[0], A.mult, A.add),
-        e.tensor_scalar(fc[5], fb[1], 34.0, fc[0], A.mult, A.add),
-        e.tensor_scalar(fc[6], fb[1], 64.0, fc[1], A.mult, A.add),
-        e.tensor_scalar(fc[7], fb[2], 8.0, fc[2], A.mult, A.add),
-        e.tensor_scalar(fc[8], fb[5], float(W), None, A.add),
-        e.tensor_scalar(fc[9], fc[3], float(W), None, A.add),
-        e.tensor_scalar(T.fd[:, 1:2], fb[4], 128.0, T.fd[:, 0:1], A.mult, A.add)])
-    for k in (0, 1):
-        a, b = 1024 * k, 1024 * k + 1024
+    ln, lq, lx, lw, lv, lj = [T.la[:, 8 * k:8 * k + 8] for k in range(6)]
+    sh, an = A.logical_shift_right, A.bitwise_and
+    const(V, [], ["qd"], lambda e, s: e.memset(T.qd[:, 0:1024], 0.0))
+    const(V, [], ["ones", "qd2"], lambda e, s: [e.memset(T.ones[:], 1.0), e.memset(T.qd[:, 1024:W + 64], 0.0)])
+    const(G, [], ["ip", "ij"], lambda e, s: [e.iota(T.ip[:], [[0, 1]], 0, 1), e.iota(T.ij[:], [[1, 8]], 0, 0, **fl),
+                                             e.iota(T.i2[:], [[64, 2], [8, 4]][::-1], 0, 0, **fl)])
+    const(G, [], ["i5"], iota(T.i5[:], [[1, 1024]], 0, 0))
+    const(S, ["qd"], ["nd"], act(T.nd[:], T.qd[:, 0:1024], ACT.Sigmoid, bias=-200.0))
+    const(V, ["ip"], ["ib"], lambda e, s: [e.tensor_scalar(T.ib[:, k:k + 1], T.ip[:], a, b, sh, an) for k, (a, b) in enumerate((
+        (0, 15), (4, 7), (0, 3), (0, 12), (0, 7), (3, 1), (1, 12), (5, 3)))])
+    const(V, ["ib"], ["fb"], cp(T.fb[:], T.ib[:]))
+    jl, gr, jb, u4, e7, e8, su4, sjb = fb
+    op(V, "cvc", ["sti"], ["cin0"], cp(T.cin0[:], T.sti[:]))
+
+    def mads(r, w, *calls):
+        const(S, r, w, lambda e, s: [e.activation(o, a, ACT.Identity, scale=x, bias=y) for o, a, x, y in calls])
+    mads(["fb", "ones"], ["fca", "cs", "nq"],
+         (fc[0], jl, -float(W), 15.0 * W),
+         (fc[7], jl, float(W), -15.0 * W), (fc[1], jb, 32.0, gr), (fc[3], jl, 32.0, gr), (fc[4], jl, 64.0, gr),
+         (fc[5], e8, 32.0, gr), (fc[6], su4, 1.0, sjb), (fc[8], jl, 1.0, float(W)), (T.nq[:], one, -1.0 / 1024, 0.0),
+         (T.cs[0:1, :, 1:17], T.ones[0:1, :], 1.75, 0.0), (T.cs[0:1, :, 0], T.ones[0:1, 0:16], 0.0, 0.0))
+    mads(["fca", "ij"], ["fc", "ibias", "dum", "lfa"],
+         (fc[9], u4, 2.0, fc[1]), (fc[10], e7, 128.0, fc[5]), (fc[11], gr, 7.0, fc[4]),
+         (T.ibias[:], T.ij[:], 1024.0, fc[7]), (T.dum[:], T.ij[:], 16.0, fc[8]),
+         (T.lf[:, 8:16], T.ij[:], 512.0, fc[3]), (T.lf[:, 16:24], T.ij[:], 8.0, fc[4]), (T.lf[:, 40:48], T.ij[:], 1.0, 0.0))
+    mads(["fc", "ij"], ["lfb", "half"], (T.lf[:, 0:8], T.ij[:], 128.0, fc[9]), (T.lf[:, 24:32], T.ij[:], 1.0, fc[11]),
+         (T.lf[:, 32:40], T.i2[:], 1.0, fc[10]), (T.half[:], one, 0.5, 0.0))
+    const(G, ["ones"], ["il", "ig", "ik", "npb", "kb", "kr", "pgx", "d1"], lambda e, s: [
+        e.iota(T.pg[:, W:W + 128], [[0, 128]], 0, 0), e.iota(T.kb[0:1, :], [[0, 128]], 1, 0, **fl),
+        e.iota(T.il[:], [[0, 8], [1, 16]], 0, 0, **fl), e.iota(T.kr[0:3], [[0, 408]], 0, 0, **fl),
+        e.iota(T.ik[0:3, 0:128], [[1, 4], [4, 4], [0, 8]], 0, 0, **fl),
+        e.iota(T.ik[0:3, 128:144], [[0, 2], [-16, 8]], 0, 0, **fl), e.iota(T.ik[0:3, 144:160], [[0, 2], [16, 8]], 0, 0, **fl),
+        e.iota(T.ig[:], [[1, 8], [0, 16]], 0, 0, **fl), e.iota(T.npb[:], [[0, 128]], -1, 0, **fl),
+        e.affine_select(T.d1[:], T.ones[:, 0:136], [[0, 8], [1, 17]], A.is_equal, 0.0, 0, 0)])
+    pp = [[-1, 8], [-8, 4], [-32, 4]]
+    const(G, ["il", "ik", "kr"], ["kr", "kl"], lambda e, s: [
+        e.affine_select(T.kr[0:3, 0:2, :, 15], T.ik[0:3, 128:144], [[0, 16]], A.is_equal, -1.0, -1, 1),
+        e.affine_select(T.kr[0:3, 0:2, :, 16], T.ik[0:3, 144:160], [[0, 16]], A.is_equal, 1.0, -1, 1),
+        e.affine_select(T.kr[0:3, 2, 0:2, 0:8], T.ik[0:3, 144:160], [[0, 16]], A.is_equal, 1.0, -1, 1),
+        e.affine_select(T.kl[0:3, 0:128], T.ik[0:3, 0:128], [[0, 128]], A.is_equal, 1.0, -2, 1),
+        e.affine_select(T.kl[0:3, 128:256], T.il[0:3, :], [[0, 128]], A.is_equal, 1.0, -2, 1)])
+    const(G, ["ones"], ["pm"], lambda e, s: [
+        e.affine_select(T.pm[:, 128 * x:128 * x + 128], one, pp, A.is_equal, 0.0, 0, 1) for x in (0, 1)])
+    const(G, [], ["kr"], lambda e, s: [
+        e.iota(T.kr[0:1, 0:2, :, 15], [[-128 - W, 2], [0, 8]], 128, 0, **fl), e.iota(T.kr[0:1, 0:2, :, 16], [[W, 2], [0, 8]], 0, 0, **fl),
+        e.iota(T.kr[0:1, 2, 0:2, 0:8], [[128 + W, 2], [0, 8]], -128, 0, **fl)])
+    const(G, ["ones"], ["id2"], sel(T.id2[:], T.ones[:], [[0, 2], [-1, 128]], 0, 1))
+    const(G, ["ones"], ["idb"], sel(T.idb[:], one, [[-1, 128]], 0, 1))
+    const(G, [], ["wd0"], iota(T.wd0[:], [[0, 1024]], 0, 0))
+    const(G, ["ones"], ["jr0"], sel(T.jr[:], T.ones[:], [[-8, 16], [0, 2], [-1, 8]], 0, 1))
+    const(G, ["npb"], ["npb"], sel(T.npb[:], T.npb[:], pp, 0, 1))
+    const(G, ["ones"], ["pmb"], sel(T.pmb[:], one, pp, 0, 1))
+    const(G, ["ones"], ["segm", "tt", "thr0"], lambda e, s: [
+        e.affine_select(T.segm[:], T.ones[:, 0:136], [[0, 8], [1, 17]], A.is_gt, 0.0, 0, 0),
+        e.iota(T.tt[:, :, :, 16], [[0, 64]], 0, 0, **fl), e.iota(T.thr[:, :, 16], [[0, 8]], 0, 0, **fl)])
+    const(G, ["jr0"], ["jr"], lambda e, s: [
+        e.affine_select(T["jr%d" % u][:], T.jr[:, :, 8 - u:16 - u], [[0, 128]], A.is_ge, 0.0, 0, 0) for u in (1, 2)])
+    for wd in ("wd1", "wd2", "we0", "we1"):
+        const(G, [], [wd], iota(T[wd][:], [[0, 1024]], 0, 0))
+
+    for k in range(PARTS):
+        a, b = 2048 * k // PARTS, 2048 * (k + 1) // PARTS
         op(V, "unp%d" % k, ["bpi%d" % k], ["pg%d" % k], lambda e, s: [
             e.tensor_scalar(T.pg[:, a:b], T.bpi[:, a:b], W - 1, None, an),
             e.tensor_scalar(T.pg[:, 2048 + a:2048 + b], T.bpi[:, a:b], 12, None, sh)])
-    PG = ["pg0", "pg1", "pgx"]
+    PG = ["pg%d" % k for k in range(PARTS)] + ["pgx"]
+    const(V, ["lfa", "lfb", "i5", "fb"], ["la", "ea"], lambda e, s: [
+        e.tensor_copy(T.la[:], T.lf[:]), e.tensor_scalar(T.ea[:], T.i5[:, 0:18], jl, None, A.is_equal)])
 
-    def first_constants():
-        const(V, ["fcb", "ij", "i2", "i3"], ["lists"], lambda e, s: [
-            e.tensor_scalar(T.lv[:], T.i3[:], T.fd[:, 1:2], None, A.add),
-            e.tensor_scalar(T.ln[:], T.ij[:], 128.0, fc[4], A.mult, A.add),
-            e.tensor_scalar(T.lq[:], T.ij[:], 512.0, fc[5], A.mult, A.add),
-            e.tensor_scalar(T.lx[:], T.ij[:], 8.0, fc[6], A.mult, A.add),
-            e.tensor_scalar(T.lw[:], T.i2[:], fc[7], None, A.add),
-            e.tensor_scalar(T.dum[:], T.ij[:], 16.0, fc[8], A.mult, A.add),
-            e.tensor_scalar(T.ds4[:], T.ij[:], 16.0, fc[9], A.mult, A.add),
-            e.tensor_scalar(T.lc[:], T.ij[:], 17.0, None, A.mult),
-            e.tensor_copy(T.lj[:], T.ij[:])])
-        const(V, ["ma", "em0", "sti"], ["em", "came", "tha"], lambda e, s: [
-            e.tensor_tensor(T.em[:, 1:16], T.ma[:, 1:16], T.ma[:, 0:15], A.subtract),
-            e.tensor_tensor(T.em[:, 18:33], T.ma[:, 1:16], T.ma[:, 0:15], A.subtract),
-            e.tensor_copy(T.em[:, 0:1], T.ma[:, 0:1]), e.tensor_copy(T.em[:, 17:18], T.ma[:, 0:1]),
-            e.tensor_scalar(T.em[:, 33:34], T.ma[:, 15:16], -1.0, None, A.mult),
-            e.memset(T.tha[:], 0.0625),
-            e.tensor_scalar(fc[10], T.ma[:, 15:16], -1.0, 1.0, A.mult, A.add),
-            e.tensor_copy(T.came[:], T.sti[:])])
-        const(V, ["ig"], ["ig2"], ts(T.ig2[:], T.ig[:], 7, None, an))
-        const(V, ["half", "ones"], ["pw"], lambda e, s: e.tensor_tensor_scan(
-            T.pw[:], T.half[:], T.ones[:, 0:128], 2.0 ** 64, A.mult, A.mult))
-        const(V, [], ["tha"], lambda e, s: e.memset(T.tha[:, 0::17], 2.0))
-        const(V, ["ig2"], ["selg"], ts(T.selg[:], T.ig2[:], 0.0, None, A.is_equal))
-        const(G, ["selg"], ["sel15"], sel(T.sel15[:], T.selg[:], [[0, 8], [1, 16]], A.is_equal, -15, 0))
-        const(V, ["pw", "ma"], ["pw2", "pa"], lambda e, s: [
-            e.tensor_tensor(T.pw2[:], T.pw[:], T.ma[:], A.mult),
-            e.tensor_tensor(T.pa[:], T.pw[:, 63:79], T.ma[:, 0:16], A.mult)])
-        const(V, ["pa"], ["fc11"], lambda e, s: e.tensor_reduce(fc[11], T.pa[:], AxisListType.X, A.add))
+    def mask(name, tile, col):
+        const(V, [tile, "fb", "fc"], [name], ts(T[name][:], T[tile][:], col, None, A.is_equal))
 
-    def late_constants():
-        const(S, ["pw2"], ["thr"], act(T.thr[:], T.pw2[:], ACT.Identity, scale=2.5))
-        const(S, ["fc11", "pw"], ["colw"], act(T.colw[:], T.pw[:, 0::16], ACT.Identity, scale=fc[11]))
+    def late_constants(k):
+        if k == 0:
+            mask("ma", "il", jl)
+            const(V, ["half", "ones"], ["pw"], lambda e, s: e.tensor_tensor_scan(
+                T.pw[:], T.half[:], one, 2.0 ** 64, A.mult, A.mult))
+            mask("bob", "ig", gr)
+        if k == 1:
+            const(V, ["pw", "ma"], ["pw2"], tt(T.pw2[:], T.pw[:], T.ma[:], A.mult))
+        if k == 2:
+            mask("ms", "il", fc[6])
+        if k == 3:
+            const(V, ["pw2"], ["fc2"], lambda e, s: e.tensor_reduce(fc[2], T.pw2[:, 48:64], AxisListType.X, A.add))
+            mask("selg", "ig", e7)
+        if k == 4:
+            const(V, ["pw2"], ["thr"], ts(T.thr[:, :, 0:16], T.pw2[:], 2.5, None, A.mult))
+            const(V, ["fc2", "pw"], ["colw"], ts(T.colw[:], T.pw[:, 15::16], fc[2], None, A.mult))
 
-    RX = T.px[:, 2, 0:128]
+    def key_numbers(x):
+        const(S, ["i5", "ibias"], ["idm%d" % x], act(T.idm[:, 1024 * x:1024 * x + 1024], T.i5[:], ACT.Identity, bias=T.ibias[:, x:x + 1]))
+    IDM = ["idm%d" % x for x in range(4)]
+    for x in range(KEYS[0]):
+        key_numbers(x)
 
-    def weights(n, part=None):
-        f, r, a, r0 = "ff%d" % (n % 2), "rs%d" % (n % 2), "ax%d" % (n % 2), 128 + 136 * (n % 2)
-        if part == 0:
-            op(V, "be", [f], ["be"], ts(T.be[:], T[f][:, 1:137], -1.0, 1.0, A.mult, A.add))
-        if part == 3:
-            op(S, "bes", [f], ["be"], act(T.be[:], T[f][:, 1:137], ACT.Identity, bias=1.0, scale=-1.0))
-        if part in (None, 1):
-            op(V, "rm", [r, a, "pz"], ["rm"], tt(T.rm[:], T.pz[:, r0:r0 + 136], T[a][:, 0:136], A.mult))
-        if part in (None, 2):
-            op(V, "ww", ["be", "rm"], ["ww"], tt(T.ww[:], T.rm[:, :, 0:16], T.be[:, :, 0:16], A.mult))
+    rall, r16 = T.pz[:, 0:136], T.pz[:, 16:136:17]
+    PR, PN, PX, PS, RM = T.px[:, 160:288], T.pz[:, 264:392], T.px[:, 288:416], ["ps0", "ps1"], T.ps
 
-    def turn_w():
-        op(P, "wtp", ["ww", "id2"], ["pz"], mm(T.pz[:, 0:128], T.ww[:], T.id2[:, 0:128]))
+    def kchunk(q, n, a, b):
+        nm = "nm%d" % (n % 2)
+        o, i = T.kg[:, 256 * a:256 * b], codes.indirect(T[nm][:, 16 * a:16 * b])
+        op(q, "k%d" % a, ["kx", nm], ["kg%d" % x for x in range(a, b)], cp(o, i) if q == V else act(o, i, ACT.Identity))
+
+    def scores(a, b, stops):
+        op(P, "sco%d" % a, ["qd"] + ["kg%d" % x for x in range(a, b)], sorted({"ps%d" % (x // 4) for x in range(a, b)}),
+           lambda e, s: [e.matmul(T.ps[:, m // 4, :, 1:17], T.qd[:, 128 * m + 32 - 8 * (m % 4):128 * m + 160 - 8 * (m % 4)],
+                                  T.kg[:, 64 * m:64 * m + 64], False, m % 4 == 3 and m // 4 in stops)
+                         for m in range(4 * a, 4 * b)])
+
+    def names(n):
+        nm = "nm%d" % (n % 2)
+        op(V, "nd", [nm, "la"], ["nd"], cp(T.nd[:, 0:1024].indirect(ln), T[nm][:]))
+
+    def steps(n):
+        op(P, "dn", ["nd", "kl", "kr", "em"], ["px"], group(
+            (T.px[:, 0:136], T.kl[0:3, 0:128], T.kr[0:3, n % 2, :, :]),
+            *[(T.px[:, 17 * x:17 * x + 17], T.nd[:, 128 * x:128 * x + 128], T.em[:]) for x in range(8)]))
+
+    def beta():
+        op(V, "be", ["ff"], ["be"], ts(T.be[:], T.ff[:], -1.0, 1.0, A.mult, A.add))
+
+    def rest(dx):
+        op(V, "rm", [dx, "rs", "pz"], ["ps0", "rm"], tt(RM[:, 0:4, 0:2, 0:17], rall, T[dx][:], A.subtract))
+
+    def weights():
+        op(V, "ww", ["be", "rm", "ps0"], ["ww"], tt(T.ww[:], RM[:, 0:4, 0:2, 0:16], T.be[:, :, 1:17], A.mult))
+
+    def turn_w(n):
+        op(P, "wtp", ["ww", "id2", "pm"], ["px"], mm(PR, T.ww[:], (T.pm if n >= NEAR else T.id2)[:, 0:128]))
 
     def spread_w(n):
-        wd = "wd%d" % (n % 2)
-        op(V, "wtc", ["pz"], ["wt"], cp(T.wt[:], T.pz[:, 0:128]))
-        if n >= 7:
-            op(V, "wds", ["wt", "lists"], ["wd2"], cp(T.wd2[:, 0:1024].indirect(T.lw[:]), T.wt[:]))
-        else:
-            op(Y, "wdd", ["wt"], [wd], lambda e, s: [
-                e.dma_start(T[wd][16 * x:16 * x + 16, x, :], T.wt[16 * x:16 * x + 16, :]) for x in range(8)], 16)
+        wd, wt = "wd%d" % (n % 3), "wt%d" % (n % 2)
+        if n >= NEAR:
+            we = "we%d" % (n % 2)
+            op(V, "wtv", ["px"], [wt], ts(T[wt][:], PR, 0.0, None, A.max))
+            return op(V, "wds", [wt, "la"], [we], cp(T[we][:, 0:1024].indirect(lw), T[wt][:]))
+        op(S, "wtc", ["px"], [wt], act(T[wt][:], PR, ACT.Relu))
+        op(Y, "wdd%d" % (n % 2), [wt], [wd], lambda e, s: [
+            e.dma_start(T[wd][16 * x:16 * x + 16, x, :], T[wt][16 * x:16 * x + 16, :]) for x in range(8)], 16)
 
-    def acc_in(t):
-        op(P, "arot", ["ain%d" % t, "id2"], ["px"], mm(RX, T.id2[:, 128 - 16 * t:256 - 16 * t], T["ain%d" % t][:]))
+    def vgather(q, n, a, b):
+        nv, vg = "nv%d" % (n % 2), "vg%d" % (n % 2)
+        o, i = T[vg][:, 128 * a:128 * b], T.vv[:, 0:W].indirect(T[nv][:, 8 * a:8 * b])
+        op(q, "vg%s%d" % (q, a), ["vv", nv], ["%s_%d" % (vg, x) for x in range(a, b)], cp(o, i) if q == V else act(o, i, ACT.Identity))
 
-    def acc_take():
-        op(V, "accr", ["px"], ["accr"], cp(T.accr[:], RX))
+    def list_v(n):
+        nv = "nv%d" % (n % 2)
+        op(V, "nv", ["nd", "la"], [nv], cp(T[nv][:], T.nd[:, 0:1024].indirect(lv)))
 
-    def turn_v():
-        for half, b in enumerate(("pva", "pvb")):
-            op(P, "vt" + b, ["vg" + b, "idb"], [b], lambda e, s: [
-                e.transpose(T[b][:, 128 * x:128 * x + 128], T.vg[:, 1024 * half + 128 * x:1024 * half + 128 * x + 128], T.idb[:])
-                for x in range(8)])
-
-    def sigmoid(n):
+    def turn_v(n, half):
+        vg, b = "vg%d" % (n % 2), ("pva", "pvb")[half]
+        op(P, "vt" + b, ["%s_%d" % (vg, 8 * half + x) for x in range(8)] + ["idb"], [b], lambda e, s: [
+            e.transpose(T[b][:, 128 * x:128 * x + 128], T[vg][:, 1024 * half + 128 * x:1024 * half + 128 * x + 128], T.idb[:])
+            for x in range(8)])
         vs = "vs%d" % (n % 3)
-        for half, b in enumerate(("pva", "pvb")):
-            op(S, "sg" + b, [b], [vs + b], act(T[vs][:, 1024 * half:1024 * half + 1024], T[b][:], ACT.Sigmoid))
+        op(S, "sg" + b, [b], [vs + b], act(T[vs][:, 8 * half:8 * half + 8, :], T[b][:], ACT.Sigmoid))
 
-    def acc_open(half):
-        b = ("paa", "pab")[half]
-        op(P, "ai" + b, ["cb", "cc"], [b], lambda e, s: e.matmul(T[b][:], T.cb[0:1, 128:256], T.cc[0:1, :], True, False))
+    def acc_add(n, half, x0=0, x1=8):
+        b, vs, wd = ("paa", "pab")[half], "vs%d" % (n % 3), "we%d" % (n % 2) if n >= NEAR else "wd%d" % (n % 3)
 
-    def acc_add(n, half):
-        b, vs, wd = ("paa", "pab")[half], "vs%d" % (n % 3), "wd%d" % (2 if n >= 7 else n % 2)
-
-        def spread(jl):
-            if n >= 7:
-                return T.wd2[:, 64 * jl:64 * jl + 64]
-            p = 32 * (jl % 4) + 8 * (jl // 4)
-            return T[wd][:, :, p:p + 8]
-        op(P, "am" + b, [vs + ("pva", "pvb")[half], wd], [b], lambda e, s: [
-            e.matmul(T[b][:, 64 * x:64 * x + 64], T[vs][:, 1024 * half + 128 * x:1024 * half + 128 * x + 128],
-                     spread(8 * half + x), False, n % 3 == 2 and x == 7) for x in range(8)])
+        def spread(j):
+            p = 32 * (j % 4) + 8 * (j // 4)
+            return T[wd][:, 64 * j:64 * j + 64] if n >= NEAR else T[wd][:, :, p:p + 8]
+        op(P, "am%s%d" % (b, x0), [vs + ("pva", "pvb")[half], wd], [b], lambda e, s: [
+            e.matmul(T[b][:, 64 * x:64 * x + 64], T[vs][:, 8 * half + x, :],
+                     spread(8 * half + x), n % 3 == 0 and x == 0, n % 3 == 2 and x == 7) for x in range(x0, x1)])
 
     def acc_out(q, half):
         b, o = ("paa", "pab")[half], T.accs[:, 512 * half:512 * half + 512]
         op(q, "ao" + q + b, [b], ["accs%d" % half], act(o, T[b][:], ACT.Identity) if q == S else cp(o, T[b][:]))
-    ACCS = ["accs0", "accs1", "lists"]
+    ACCS = ["accs0", "accs1", "la"]
 
     def picked():
-        return T.accs[:, 0:1024].indirect(T.lx[:])
+        return T.accs[:, 0:1024].indirect(lx)
+
+    def acc_in(t):
+        ain = T["ain%d" % t]
+        op(Y, "arot", ["ain%d" % t], ["accr"], lambda e, s: [
+            e.dma_start(T.accr[16 * t:128, :], ain[0:128 - 16 * t, :]), e.dma_start(T.accr[0:16 * t, :], ain[128 - 16 * t:128, :])], 16)
 
     def report(t):
         acn = "acn%d" % t
@@ -383,224 +413,232 @@ def rank_program(g, core, T, topo):
         op(S, "sgc", ["vv", cl], ["sg"], act(T.sg[:], T.vv[:, 0:W].indirect(T[cl][:, 0:8]), ACT.Sigmoid))
 
     def rest_row():
-        op(V, "xb", ["rn", "ms", "lists"], ["xb"], tt(T.xb[:], T.rn[:, 0:8].indirect(T.lj[:]), T.ms[:], A.mult))
-        op(P, "rrow", ["xb", "selg"], ["px"], mm(RX, T.selg[:], T.xb[:]))
+        op(V, "xb", ["rn", "ms", "la"], ["xb"], tt(T.xb[:], T.rn[:, 0:8].indirect(lj), T.ms[:], A.mult))
+        op(P, "rrow", ["xb", "selg"], ["px"], mm(PX, T.selg[:], T.xb[:]))
 
     def rest_term():
-        op(V, "rep", ["sg", "px"], ["rep"], tt(T.rep[:], T.sg[:], RX, A.mult))
+        op(V, "rep", ["sg", "px"], ["rep"], tt(T.rep[:], T.sg[:], PX, A.mult))
 
-    def kchunk(q, nm, a, b, name):
-        o, i = T.kg[:, 128 * a:128 * b], T.kx[:, 0:W].indirect(T[nm][:, 8 * a:8 * b])
-        op(q, name, ["kx", nm], ["kg%d" % x for x in range(a, b)], cp(o, i) if q == V else act(o, i, ACT.Identity))
+    taken = []
+    behind = []
 
-    def scores(a, b, name, stops):
-        op(P, name, ["qd"] + ["kg%d" % x for x in range(a, b)], ["ps"], lambda e, s: [
-            e.matmul(T.ps[:, m // 4, :, 1:17], T.qd[:, 128 * m:128 * m + 128], T.kg[:, 64 * m:64 * m + 64],
-                     False, m in stops) for m in range(2 * a, 2 * b)])
+    def fill(k):
+        for _ in range(k):
+            if behind and behind[0][0] // 3 == len(taken):
+                n, half, x = behind.pop(0)
+                acc_add(n, half, x, x + 2)
 
     for n in range(9):
         t, h = divmod(n, 3)
-        cl, cn, nm = "cl%d" % (n % 2), "cl%d" % ((n + 1) % 2), "nm%d" % (n % 2)
-        ff, rs, ax = "ff%d" % (n % 2), "rs%d" % (n % 2), "ax%d" % (n % 2)
-        msg = "msg%d" % t
-        came, camek = (T.came, "came") if t == 0 else (T[msg], msg)
-        qk, qkk = (T.ds4[:], "lists") if h == 0 else (T.sc[:, 136::17], "scq")
+        cl, cn, nm, dx = "cl%d" % (n % 2), "cl%d" % ((n + 1) % 2), "nm%d" % (n % 2), "dx%d" % h
+        msg, qn, came = "msg%d" % t, "q%d" % (n % 2), "cin%d" % t
+        clist = came if h == 0 else cl
         end = n == 8
-        split = 12 if end else (SPLIT if h > 0 else 8)
-        mid = 8 if end else (MID if h > 0 else 6)
-        stops = (15, 31 if (end or split == 8) else 2 * split - 1)
+        ns = SHARE[n]
+        landed = h == 0 and t > 0
 
-        op(P, "si", ["cb", "cc"], ["ps"], lambda e, s: [
-            e.matmul(T.ps[:, 4 * x:4 * x + 4, :, 0:17], T.cb[0:1, 0:128], T.cs[0:1], True, False) for x in (0, 1)])
-        if h == 0 and t > 0:
-            op(V, "cvc", [msg], [cl], cp(T[cl][:, 0:8], T[msg][:, 0:8]))
-            op(P, "qrot", [msg, "id2"], ["px"], mm(RX, T.id2[:, 128 - 16 * t:256 - 16 * t], T[msg][:, 16:144]))
-        op(V, "nm", PG + [cl], [nm], cp(T[nm][:], T.pg[:, 0:W].indirect(T[cl][:, 0:8])))
-        if n == 0:
-            first_constants()
-        if n in (3, 4, 6, 7):
-            acc_add(n - 2, 0)
-        qscale = -1.0 / 1024
-        if h > 0:
-            op(V, "qsv", ["kx", "kxx", cl], ["qs"],
-               ts(T.qs[:], T.kx[:, 0:W + 128].indirect(T[cl][:, 8:16]), qscale, None, A.mult))
-            turn_v()
-        elif t == 0:
-            op(S, "qs", ["kx", cl], ["qs"], act(T.qs[:], T.kx[:, 0:W].indirect(T[cl][:, 0:8]), ACT.Identity, scale=qscale))
-        else:
-            op(S, "qs", ["px"], ["qs"], act(T.qs[:], RX, ACT.Identity, scale=qscale))
-        if end:
-            acc_add(n - 2, 0)
-            weights(n - 1, 3)
-            acc_out(S, 1)
-            weights(n - 1, 1)
-        op(V, "nd", [nm, "lists"], ["nd"], cp(T.nd[:, 0:1024].indirect(T.ln[:]), T[nm][:]))
-        if end:
-            weights(n - 1, 2)
-            turn_w()
-        else:
-            op(P, "dn", ["nd", "em"], ["px"], lambda e, s: [
-                e.matmul(T.px[:, 0:2, 17 * x:17 * x + 17], T.nd[:, 128 * x:128 * x + 128], T.em[:], True, True)
-                for x in range(8)])
-        kchunk(V, nm, 0, 4, "k0")
-        if not end:
-            kchunk(S, nm, split, 16, "k3")
-        if h == 0:
-            op(S, "kxx", ["qs"], ["kxx"], act(T.kx[:, W:W + 128], T.qs[:], ACT.Identity, scale=-1024.0))
-            if n == 0:
-                late_constants()
-        else:
-            if not end:
-                weights(n - 1, 3)
-            if n in (4, 7):
-                acc_out(S, 0)
-            if n == 5:
-                acc_out(S, 1)
-            sigmoid(n - 1)
-        op(V, "qd", ["qs", "lists"], ["qd"], cp(T.qd[:, 0:4096].indirect(T.lq[:]), T.qs[:]))
-        scores(0, 4, "sco0", stops)
-        if h > 0 and not end:
-            scores(split, 16, "sco3", stops)
-        op(V, "nv", ["nd", "lists"], ["nv"], cp(T.nv[:], T.nd[:, 0:1024].indirect(T.lv[:])))
-        for x, b in enumerate(("pva", "pvb")):
-            op(S, "vg" + b, ["vv", "nv"], ["vg" + b], act(
-                T.vg[:, 1024 * x:1024 * x + 1024], T.vv[:, 0:W].indirect(T.nv[:, 64 * x:64 * x + 64]), ACT.Identity))
-        if h == 0:
-            scores(split, 16, "sco3", stops)
-        if end:
-            report(t - 1)
-            acc_open(1)
-            acc_add(n - 2, 1)
-            spread_w(n - 1)
-            acc_add(n - 1, 0)
-        kchunk(V, nm, 4, mid, "k1")
-        scores(4, mid, "sco1", stops)
-        kchunk(V, nm, mid, split, "k2")
-        scores(mid, split, "sco2", stops)
-        if end:
-            kchunk(V, nm, 12, 16, "k3v")
-            scores(12, 16, "sco3", stops)
-            turn_v()
-            acc_add(n - 1, 1)
-        elif h > 0:
-            weights(n - 1)
-            turn_w()
-            if n == 7:
-                acc_in(1)
-        elif t > 0:
-            op(V, "d1", [msg], ["d1"], cp(T.d1[:, 0::17], T[msg][:, 8:16]))
-            rest_row()
-            if n == 6:
-                report(0)
-                output(0)
-        if h == 0 and t < 2:
-            op(V, "xa", [camek, "ma", "lists"], ["xa"], tt(T.xa[:], came[:, 0:8].indirect(T.lj[:]), T.ma[:], A.mult))
-            op(V, "v0", [nm, "em"], ["v0"], ts(T.v0[:], T[nm][:], fc[10], None, A.mult))
-            op(P, "crp", ["xa", "bof"], ["pz"], mm(T.pz[:, 0:128], T.bof[:], T.xa[:]))
-        if h == 2 and not end:
-            acc_open(1)
-        if n in (2, 3, 4, 5, 6, 7):
-            acc_add(n - 2, 1)
-        if h == 1:
-            acc_open(0)
-        op(V, "clamp", ["ps"], [ff], lambda e, s: [
-            e.tensor_scalar(T[ff][32 * b:32 * b + 32, 0:136], T.ps[32 * b:32 * b + 32, :, b, 0:17], 0.0625, 1.0, A.max, A.min)
-            for b in range(4)])
-        if not end:
-            op(V, "g2", [qkk, "px"], ["px", "g2"], tt(T.px[:, 1, 16:136:17], qk, T.px[:, 1, 16:136:17], A.add))
-        if h > 0 and not end:
-            spread_w(n - 1)
-        if n == 7:
-            acc_take()
-        if h == 0 and t < 2:
-            op(V, "crow", ["pz"], ["crow"], cp(T.crow[:], T.pz[:, 0:128]))
-        r0 = 128 + 136 * (n % 2)
-        rall, r15 = T.pz[:, r0:r0 + 136], T.pz[:, r0 + 16:r0 + 136:17]
-        op(V, "rs", [ff, "d1"], [rs, "pz"], lambda e, s: e.tensor_tensor_scan(
-            rall, T[ff][:, 0:136], T.d1[:], 0.0, A.mult, A.max))
-        if h == 2 and t < 2:
-            op(V, "whole", ["ax0", "ax1"], ["whole"], tt(T.whole[:], T.ax0[:, 16:136:17], T.ax1[:, 16:136:17], A.mult))
-        if h == 0 and t > 0:
+        def turn_q():
+            op(P, "qrot", [msg, "id2"], ["px"], mm(PX, T.id2[:, 128 - 16 * t:256 - 16 * t], T[msg][:, 16:144]))
+
+        op(P, "si", ["kb", "cs"], PS, lambda e, s: [
+            e.matmul(T.ps[:, 4 * x:4 * x + 4, :, 0:17], T.kb[0:1, :], T.cs[0:1], True, False) for x in (0, 1)])
+        op(V, "nm", PG + [clist], [nm], cp(T[nm][:], T.pg[:, 0:W].indirect(T[clist][:, 0:8])))
+        if landed:
             rest_term()
+        if n == 0:
+            const(V, ["ea"], ["em"], tt(T.em[:], T.ea[:, 0:17], T.ea[:, 1:18], A.subtract))
+            names(n)
+        if h > 0:
+            op(V, "qs", ["kx", "q%d" % ((n - 1) % 2), cl], [qn], cp(qarea(n), qwindow(n - 1).indirect(T[cl][:, 8:16])))
+        elif t == 0:
+            op(V, "qs", ["kx", came], [qn], cp(qarea(n), codes.indirect(T[came][:])))
+        cuts = [ns] + [c for c in (3, 5, 7, 8) if c > ns]
+        bits = list(zip(cuts[:-1], cuts[1:]))
+        if ns:
+            kchunk(S, n, 0, ns)
+        if n == 0:
+            for x in range(KEYS[0], 4):
+                key_numbers(x)
+            list_v(n)
+        if landed:
+            names(n)
+            kchunk(V, n, *bits[0])
+            list_v(n)
+            turn_q()
+            op(V, "qs", ["px"], [qn], cp(qarea(n), PX))
+            op(V, "d1", [msg], ["d1"], cp(T.d1[:, 0::17], T[msg][:, 8:16]))
+            if t < 2:
+                op(V, "cd", [msg, "dum"], ["cd"], tt(T.cd[:], T[msg][:, 0:8], T.dum[:], A.subtract))
+        if h > 0:
+            turn_w(n - 1)
+            if n - 1 < NEAR:
+                spread_w(n - 1)
+            turn_v(n - 1, 0)
+            turn_v(n - 1, 1)
+        if h > 0:
+            names(n)
+        op(V, "qd", [qn, "la", "nq", "qd2"], ["qd"], tt(T.qd[:, 32:W + 64].indirect(lq), qarea(n), T.nq[:], A.mult))
+        if h > 0:
+            list_v(n)
+        sv = 16 - sum(GAPS[n])
+
+        def gap(k):
+            if n == 0:
+                late_constants(k)
+            if GAPS[n][k]:
+                vgather(V, n, sv + sum(GAPS[n][:k]), sv + sum(GAPS[n][:k + 1]))
+        vgather(S, n, 0, 8)
+        if STEPS[n] == 0 and not end:
+            steps(n)
+        fill(FILL[n][0])
+        if h > 0 and n - 1 < NEAR:
+            behind.extend((n - 1, half, x) for half in (0, 1) for x in (0, 2, 4, 6))
+        late = min(LATE[n], len(bits) - 1)
+        done = [x for k, (a, b) in enumerate(bits) for x in (list(range(ns)) if k == late else []) + list(range(a, b))]
+        stops = ([x for x in done if x < 4][-1], 7)
+        for k, (a, b) in enumerate(bits):
+            if not (landed and k == 0):
+                kchunk(V, n, a, b)
+            if k == late and ns:
+                scores(0, ns, stops)
+            scores(a, b, stops)
+            if h > 0 and n - 1 >= NEAR and k == min(WAT[n - 7], len(bits) - 1):
+                spread_w(n - 1)
+                behind.extend((n - 1, half, x) for half in (0, 1) for x in (0, 2, 4, 6))
+            if min(STEPS[n], len(bits)) == k + 1 and not end:
+                steps(n)
+            if k < len(bits) - 1:
+                fill(FILL[n][1 + k])
+        fill(FILL[n][-1])
+        assert sv >= 8
+        if sv > 8:
+            vgather(S, n, 8, sv)
+        if n in OUT:
+            fill(16)
+            acc_out(S, 0)
+            acc_out(S, 1)
+            taken.append(t)
+        if h == 1 and t < 2:
+            op(V, "crow", IDM + ["fc", came], ["crow"], ts(T.crow[:], T.idm[:, 0:W].indirect(T[came][:]), fc[0], None, A.add))
+        if h == 0 and t < 2:
+            op(V, "v0", [nm, "fc"], ["v0"], ts(T.v0[:], T[nm][:], fc[0], None, A.min))
+        if n == 0:
+            op(V, "cd", ["sti", "dum"], ["cd"], tt(T.cd[:], T.sti[:], T.dum[:], A.subtract))
+        if n == 6:
+            acc_in(1)
+        if n - 1 in OUT:
+            report(t - 1)
+        gap(0)
+        op(V, "clamp", PS, ["ff"], lambda e, s: [
+            e.tensor_scalar(T.ff[32 * b:32 * b + 32, :], T.ps[32 * b:32 * b + 32, :, b, 0:17], 0.0625, 1.0, A.max, A.min)
+            for b in range(4)])
+        gap(1)
+        op(V, "rs", ["ff", "d1"], ["rs", "pz"], lambda e, s: e.tensor_tensor_scan(rall, T.ff[:], T.d1[:], 0.0, A.mult, A.max))
+        beta()
         if end:
-            weights(n, 0)
-            op(V, "ax", [rs, "pz"], [ax], ts(T[ax][:, 0:136], rall, 0.0625, None, A.is_ge))
-            weights(n, 1)
-            op(V, "dd", [ax], ["dd"], tt(T.dd[:], T[ax][:, 0:136], T[ax][:, 1:137], A.subtract))
-            weights(n, 2)
-            op(V, "dd", ["dd", "rm"], ["dd"], tt(T.dd[:, :, 15], T.dd[:, :, 15], T.rm[:, :, 16], A.add))
-            op(V, "wwe", ["dd", "ww"], ["ww"], tt(T.ww[:], T.ww[:], T.dd[:, :, 0:16], A.add))
-            turn_w()
+            op(V, "e3", ["rs", "pz"], ["e3"], ts(T.e3[:], rall, 0.0625, None, A.is_lt))
+            gap(2)
+            op(V, "e16", ["e3", "rs", "pz"], ["rn"], tt(T.rn[:], T.e3[:, :, 16], r16, A.max))
+            rest("e3")
+            op(V, "ee", ["e3"], ["ee"], tt(T.ee[:], T.e3[:, :, 1:17], T.e3[:, :, 0:16], A.subtract))
+            weights()
+            op(V, "e15", ["e3", "rn", "ee"], ["ee"], tt(T.ee[:, 15::16], T.rn[:], T.e3[:, :, 15], A.subtract))
+            turn_v(n, 0)
+            fill(FILL[n + 1][0])
+            op(P, "wtp", ["ww", "ee", "pm"], ["px"], group((PR, T.ww[:], T.pm[:, 0:128]), (PR, T.ee[:], T.pm[:, 0:128])))
+            gap(3)
+            gap(4)
+            turn_v(n, 1)
             spread_w(n)
-            sigmoid(n)
+            fill(16)
             acc_in(t)
-            acc_take()
-            output(t - 1)
             acc_add(n, 0)
             acc_add(n, 1)
             acc_out(V, 0)
-            acc_out(V, 1)
+            acc_out(S, 1)
             op(V, "yo", ACCS + ["accr"], ["yo2"], tt(T.yo2[:], picked(), T.accr[:], A.add))
             dma("st2", T.ya[:, 256:384], T.yo2[:], ["yo2"], [])
             break
-        op(V, "ax", [rs, "pz", "tha"], [ax], tt(T[ax][:, 0:136], rall, T.tha[:], A.is_ge))
-        op(V, "dead", [rs, "pz"], ["dead"], ts(T.dead[:], r15, 0.0625, None, A.is_lt))
-        op(V, "sc", [ax, "px"], ["sc"], lambda e, s: e.tensor_tensor_scan(
-            T.sc[:, 135::-1], T[ax][:, 136:0:-1], T.px[:, 0, 135::-1], 0.0, A.mult, A.add))
-        op(V, "scq", [ax, "px", "g2"], ["scq"], lambda e, s: e.tensor_tensor_scan(
-            T.sc[:, 271:135:-1], T[ax][:, 136:0:-1], T.px[:, 1, 135::-1], 0.0, A.mult, A.add))
-        op(P, "pc", ["sc", "scq", "pm"], ["px"], mm(T.px[:, 0, 136:152], T.pm[:, 0:128], T.sc[:, 0::17]))
-        cs = T.sc[:, 0:136:17]
+        op(V, "dx", ["rs", "pz"], [dx], ts(T[dx][:], rall, 0.0625, None, A.is_lt))
+        gap(2)
+        if h == 2:
+            u, snc, snd = t + 1, "snc%d" % t, "snd%d" % t
+            op(P, "pcut", ["dx0", "dx1", "dx2", "pmb", "npb"], ["ps0"], group(
+                (T.ps[:, 0, 2, 0:8], T.pmb[:], T.dx2[:, 16::17]), (T.ps[:, 0, 2, 0:8], T.npb[:], T.dx1[:, 16::17]),
+                (T.ps[:, 0, 2, 0:8], T.npb[:], T.dx0[:, 16::17])))
+            op(V, "rn", [dx, "rs", "pz"], ["rn"], tt(T.rn[:], T[dx][:, 16::17], r16, A.max))
+            op(P, "pq2", ["rn", "jr"], ["ps1"], mm(T.ps[:, 4, 1, 8:16], T["jr%d" % u][:], T.rn[:]))
+        op(V, "sc", [dx, "px"], ["sc"], lambda e, s: e.tensor_tensor_scan(T.sc[:], T[dx][:], T.px[:, 0:136], 0.0, A.mult, A.add))
 
         def lists():
-            op(V, "cvc", ["px"], [cn], cp(T[cn][:], T.px[:, 0, 136:152]))
+            op(P, "pc", ["sc", "pm", "kl", "kr"], ["px"], group(
+                (T.px[:, 136:152], T.kl[0:3, 128:256], T.kr[0:3, 2, n % 2, 0:16]), (T.px[:, 136:144], T.pm[:, 0:128], T.sc[:, 15::17]),
+                (T.px[:, 144:152], T.pm[:, 0:128], T.sc[:, 16::17])))
+
+        def take_lists():
+            op(V, "cvc", ["px"], [cn], cp(T[cn][:], T.px[:, 136:152]))
         if h < 2:
-            op(G, "on", [], [ax], iota(T[ax][:, 0:136:17], [[0, 8]], 1, 0, True))
-            op(V, "d1", ["dead", rs, "pz"], ["d1"], tt(T.d1[:, 0::17], T.dead[:], r15, A.max))
-            if h == 0 and t < 2:
-                op(V, "cd", [camek, "lists"], ["cd"], tt(T.cd[:], came[:, 0:8], T.dum[:], A.subtract))
             lists()
+            rest(dx)
+            op(V, "d1", [dx, "rs", "pz"], ["d1"], tt(T.d1[:, 0::17], T[dx][:, 16::17], r16, A.max))
+            if n - 1 in OUT:
+                output(t - 1)
+            gap(3)
+            weights()
+            take_lists()
+            gap(4)
         else:
-            u, snd = t + 1, "snd%d" % t
-            op(V, "rn", ["dead", rs, "pz"], ["rn"], tt(T.rn[:], T.dead[:], r15, A.max))
-            op(V, "cut", ["whole", "dead"], ["cut"], tt(T.cut[:], T.whole[:], T.dead[:], A.mult))
-            op(P, "pq", ["sc", "rn", "pm", "jr"], ["pz"], lambda e, s: [
-                e.matmul(T.pz[:, 400:408], T.pm[:, 128 - 16 * u:256 - 16 * u], cs, True, True),
-                e.matmul(T.pz[:, 408:416], T["jr%d" % u][:], T.rn[:], True, True)])
+            op(P, "pq", ["sc", "pm", "kl", "kr"], ["ps1"], group(
+                (T.ps[:, 4, 1, 0:8], T.kl[0:3, 128:256], T.kr[0:3, 2, n % 2, 0:8]),
+                (T.ps[:, 4, 1, 0:8], T.pm[:, 128 - 16 * u:256 - 16 * u], T.sc[:, 15::17])))
             lists()
-            op(P, "pcut", ["cut", "pm"], ["px"], mm(T.px[:, 1, 152:160], T.pm[:, 0:128], T.cut[:]))
-            op(V, "snb", ["kx", "kxx", cn], [snd + "b"], cp(T[snd][:, 16:144], T.kx[:, 0:W + 128].indirect(T[cn][:, 8:16])))
-            op(V, "sna", ["pz"], [snd + "a"], cp(T[snd][:, 0:16], T.pz[:, 400:416]))
-            send("sm%d" % t, T["msg%d" % u][:], T[snd][:], "am%d" % u, [snd + "a", snd + "b"])
-            op(V, "cutw", ["px", "colw", "cd"], ["cutw", "delta"], lambda e, s: [
-                e.tensor_tensor(T.cutw[:], T.px[:, 1, 152:160], T.colw[:], A.mult),
-                e.tensor_tensor(T.delta[:], T.px[:, 1, 152:160], T.cd[:], A.mult)])
-            op(V, "xa", ["sc", "ms", "lists"], ["xa"], tt(T.xa[:], T.sc[:, 0:136].indirect(T.lc[:]), T.ms[:], A.mult))
-            op(P, "c15", ["xa", "sel15"], ["px"], mm(RX, T.sel15[:], T.xa[:]))
-            op(V, "onv", [], [ax], lambda e, s: e.memset(T[ax][:, 0:136:17], 1.0))
-            op(V, "tt", ["crow", camek, "cutw"], ["tt"], lambda e, s: [
-                e.tensor_scalar(T.tt[:, 144 * x:128 * x + 128], T.crow[:, 16 * x:128], came[:, x:x + 1], T.cutw[:, x:x + 1],
-                                A.is_equal, A.mult) for x in range(8)])
-            op(P, "ssum", ["tt", "bob"], ["pz"], lambda e, s: [
-                e.matmul(T.pz[:, 16 * x:128], T.bob[:], T.tt[:, 144 * x:128 * x + 128], x == 0, x == 7)
-                for x in range(8)])
-            turn_v()
-            weights(n, 0)
-            op(V, "vals", ["v0", "px"], ["vals"], tt(T.vals[:], T.v0[:], RX, A.add))
-            op(V, "win", ["pz", "thr"], ["win"], tt(T.win[:], T.pz[:, 0:128], T.thr[:], A.is_lt))
-            weights(n, 1)
-            op(V, "wsum", ["win", "segm"], ["wsum"], lambda e, s: e.tensor_tensor_scan(
-                T.wsum[:], T.segm[:], T.win[:], 0.0, A.mult, A.add))
-            weights(n, 2)
-            turn_w()
-            acc_add(n - 2, 0)
-            op(V, "t1", ["wsum", "delta"], ["t1"], tt(T.t1[:], T.wsum[:, 15::16], T.delta[:], A.mult))
-            op(V, "t2", ["t1", "lists"], ["t2"], tt(T.t2[:], T.t1[:], T.dum[:], A.add))
-            op(V, "offs", ["t2"], ["offs"], cp(T.offs[:], T.t2[:]))
-            op(V, "cutp", ["vals", "offs"], PG, cp(T.pg[:, 0:W + 128].indirect(T.offs[:]), T.vals[:]))
+            turn_v(n, 0)
+            op(V, "cut", ["ps0"], ["cut"], ts(T.cut[:], T.ps[:, 0, 2, 0:8], 0.0, None, A.max))
+            rest(dx)
+            op(V, "delta", ["cut", "cd"], ["segm"], tt(T.segm[:, 16::17], T.cut[:], T.cd[:], A.mult))
+            weights()
+            gap(3)
+            op(V, "to", ["segm", "dum"], ["to"], tt(T.to[:], T.segm[:, 16::17], T.dum[:], A.add))
+            op(V, "snc", ["ps1"], [snc], cp(T[snc][:], T.ps[:, 4, 1, 0:8]))
+            send("sc%d" % t, T["cin%d" % u][:], T[snc][:], "ac%d" % u, [snc])
+            take_lists()
+            turn_w(n)
             spread_w(n)
+            op(V, "sna", ["ps1"], [snd + "a"], cp(T[snd][:, 0:16], T.ps[:, 4, 1, 0:16]))
+
+            def send_q():
+                op(V, "snb", ["kx", qn, cn], [snd + "b"], cp(T[snd][:, 16:144], qwindow(n).indirect(T[cn][:, 8:16])))
+                send("sm%d" % t, T["msg%d" % u][:], T[snd][:], "am%d" % u, [snd + "a", snd + "b"])
+            if GAPS[n][4] == 0:
+                turn_v(n, 1)
+            fill(WIN[0])
+            for k, (a, b) in enumerate(((0, 3), (3, 8))):
+                if QAT[t] == k:
+                    send_q()
+                op(V, "tt%d" % a, ["crow", "to", "colw"], ["tt%d" % a], lambda e, s: [
+                    e.tensor_scalar(T.tt[:, x, x:8, 0:16], T.crow[:, 16 * x:128], T.to[:, x:x + 1], T.colw[:, x:x + 1],
+                                    A.is_equal, A.mult) for x in range(a, b)])
+                op(P, "ssum%d" % a, ["tt%d" % a, "tt", "bob"], ["pz"], lambda e, s: [
+                    e.matmul(T.pz[:, 264 + 17 * x:400], T.bob[:], T.tt[:, x, x:8, :], x == 0, x == 7) for x in range(a, b)])
+            if QAT[t] == 2:
+                send_q()
+            op(V, "win", ["pz", "thr", "thr0"], ["win"], tt(T.win[:], T.pz[:, 264:400], T.thr[:], A.is_lt))
+            op(V, "vals", IDM + ["v0", cn], ["vals"], tt(T.vals[:], T.idm[:, 0:W].indirect(T[cn][:, 0:8]), T.v0[:], A.max))
+            op(V, "so", ["segm", "win"], ["so"], lambda e, s: e.tensor_tensor_scan(
+                T.so[:], T.segm[:], T.win[:], 0.0, A.mult, A.add))
+            if GAPS[n][4]:
+                gap(4)
+                turn_v(n, 1)
+            fill(WIN[1])
             rest_value(cn)
-            sigmoid(n)
+            op(V, "t2", ["so", "dum"], ["t2"], tt(T.t2[:], T.so[:, 16::17], T.dum[:], A.add))
+            rest_row()
+            fill(16)
+            behind.extend((n, half, x) for half in (0, 1) for x in (0, 2, 4, 6))
+            op(V, "offs", ["t2"], ["offs"], cp(T.offs[:], T.t2[:]))
+            if n - 1 in OUT:
+                output(t - 1)
+            op(V, "cutp", ["vals", "offs"], PG, cp(T.pg[:, 0:W + 128].indirect(T.offs[:]), T.vals[:]))
 
     for name in list(lastop):
         if lastop[name] not in waited:

from concourse.mybir import AluOpType, AxisListType, ActivationFunctionType

W = 4096
F32, BF, I32, U16 = "float32", "bfloat16", "int32", "uint16"
SHARE = (4, 4, 4, 6, 4, 4, 6, 5, 4)
FILL = ((0, 0, 0, 0, 0), (0, 0, 0, 0, 0), (1, 0, 0, 0, 3), (2, 0, 0, 2, 3), (5, 1, 0, 0, 0), (2, 1, 0, 0, 3),
        (3, 0, 0, 0, 8), (0, 0, 1, 1, 3), (2, 2, 0, 1, 6), (1,))
WIN = (1, 5)
NEAR = 6
PARTS = 2
GAPS = ((0, 0, 0, 0, 0), (1, 1, 0, 1, 1), (1, 1, 1, 0, 1), (0, 0, 0, 1, 0), (1, 1, 1, 2, 1), (2, 1, 1, 0, 0), (0, 1, 1, 1, 0), (1, 1, 0, 0, 1), (0, 1, 0, 1, 1))
STEPS = (4, 4, 4, 4, 4, 4, 4, 4, 4)
OUT = (4, 6)
KEYS = (2,)
QAT = (1, 1)
WAT = (2, 2)
LATE = (1, 1, 1, 1, 1, 1, 1, 1, 0)


def _sb(shape, dtype):
    return ("sbuf", shape, dtype)


SCRATCH = {
    "kx": _sb([128, W + 256], BF), "vv": _sb([128, W], BF), "bpi": _sb([128, W // 2], I32),
    "pg": _sb([128, W + 128], I32), "sti": _sb([128, 8], I32), "idm": _sb([128, W], F32),
    "cl0": _sb([128, 16], U16), "cl1": _sb([128, 16], U16),
    "nm0": _sb([128, 128], U16), "nm1": _sb([128, 128], U16), "nv0": _sb([128, 128], U16), "nv1": _sb([128, 128], U16),
    "qd": _sb([128, W + 64], BF), "nd": _sb([128, 1024], F32),
    "kg": _sb([128, 2048], BF), "vg0": _sb([128, 2048], BF), "vg1": _sb([128, 2048], BF),
    "vs0": _sb([128, 16, 128], F32), "vs1": _sb([128, 16, 128], F32), "vs2": _sb([128, 16, 128], F32),
    "ff": _sb([128, 136], F32), "be": _sb([128, 8, 17], F32), "ww": _sb([128, 128], F32),
    "dx0": _sb([128, 136], BF), "dx1": _sb([128, 136], BF), "dx2": _sb([128, 136], BF),
    "e3": _sb([128, 8, 17], F32), "ee": _sb([128, 128], F32),
    "d1": _sb([128, 136], F32), "sc": _sb([128, 136], F32), "rn": _sb([128, 8], F32),
    "wt0": _sb([128, 128], F32), "wt1": _sb([128, 128], F32),
    "wd0": _sb([128, 8, 128], F32), "wd1": _sb([128, 8, 128], F32), "wd2": _sb([128, 8, 128], F32),
    "we0": _sb([128, 1024], F32), "we1": _sb([128, 1024], F32),
    "xb": _sb([128, 128], F32), "crow": _sb([128, 128], F32), "v0": _sb([128, 128], F32), "cd": _sb([128, 8], F32),
    "cut": _sb([128, 8], F32), "to": _sb([128, 8], F32), "tt": _sb([128, 8, 8, 17], BF),
    "t2": _sb([128, 8], F32), "win": _sb([128, 136], F32), "so": _sb([128, 136], F32), "offs": _sb([128, 8], U16), "vals": _sb([128, 128], F32),
    "sg": _sb([128, 128], F32), "rep": _sb([128, 128], F32), "accs": _sb([128, 1024], F32),
    "accr": _sb([128, 128], F32), "yo0": _sb([128, 128], F32), "yo1": _sb([128, 128], F32), "yo2": _sb([128, 128], F32),
    "snc0": _sb([128, 8], U16), "snc1": _sb([128, 8], U16),
    "cin0": _sb([128, 8], U16), "cin1": _sb([128, 8], U16), "cin2": _sb([128, 8], U16),
    "snd0": _sb([128, 144], F32), "snd1": _sb([128, 144], F32), "msg1": _sb([128, 144], F32), "msg2": _sb([128, 144], F32),
    "acn0": _sb([128, 128], F32), "acn1": _sb([128, 128], F32), "ain1": _sb([128, 128], F32), "ain2": _sb([128, 128], F32),
    "ip": _sb([128, 1], I32), "ib": _sb([128, 8], I32), "fb": _sb([128, 8], F32), "fc": _sb([128, 12], F32),
    "ij": _sb([128, 8], F32), "i2": _sb([128, 8], F32), "i5": _sb([128, 1024], F32), "ibias": _sb([128, 8], F32),
    "il": _sb([128, 128], F32), "ig": _sb([128, 128], F32), "ik": _sb([128, 160], F32),
    "ones": _sb([128, 256], F32), "nq": _sb([128, 128], BF), "pm": _sb([128, 256], F32), "id2": _sb([128, 256], F32),
    "idb": _sb([128, 128], BF), "pmb": _sb([128, 128], BF), "npb": _sb([128, 128], BF),
    "jr": _sb([128, 16, 16], F32), "jr1": _sb([128, 128], F32), "jr2": _sb([128, 128], F32),
    "cs": _sb([128, 16, 17], BF), "kb": _sb([128, 128], BF), "kl": _sb([128, 256], BF), "kr": _sb([128, 3, 8, 17], BF),
    "ea": _sb([128, 18], F32), "em": _sb([128, 17], F32), "segm": _sb([128, 136], F32),
    "ma": _sb([128, 128], F32), "ms": _sb([128, 128], F32), "selg": _sb([128, 128], F32), "bob": _sb([128, 128], BF),
    "half": _sb([128, 128], F32), "pw": _sb([128, 128], F32), "pw2": _sb([128, 128], F32),
    "thr": _sb([128, 8, 17], F32), "colw": _sb([128, 8], F32), "dum": _sb([128, 8], F32),
    "lf": _sb([128, 48], F32), "la": _sb([128, 48], U16),
    "ps": ("psum", [128, 8, 4, 32], F32), "px": ("psum", [128, 512], F32), "pz": ("psum", [128, 512], F32),
    "pva": ("psum", [128, 1024], BF), "pvb": ("psum", [128, 1024], BF),
    "paa": ("psum", [128, 512], F32), "pab": ("psum", [128, 512], F32),
}
BANKS = ("ps0", "ps1", "px", "pz", "pva", "pvb", "paa", "pab")
SEMAPHORES = ["ac1", "ac2", "am1", "am2", "aa1", "aa2"] + ["sem%d" % k for k in range(140)]


def rank_program(g, core, T, topo):
    rank = T.rank_of(core)
    if rank is None:
        return
    A = AluOpType
    ACT = ActivationFunctionType
    nxt = T.cores[(rank + 1) % len(T.cores)]
    prv = T.cores[(rank - 1) % len(T.cores)]
    rid, pid, _se = topo.addr(nxt)

    def eight(src, dst):
        eng = topo.engines(src, dst)[:8]
        return sum(1 << e for e in eng), len(eng)
    out_mask, out_n = eight(core, nxt)
    in_n = eight(prv, core)[1]

    V, S, P, Y, G = "v", "s", "p", "y", "g"
    queue = {V: g.vector, S: g.scalar, P: g.tensor, Y: g.sync, G: g}
    known = {q: set() for q in queue}
    ops = []
    lastw, readers, bank = {}, {}, {b: [] for b in BANKS}
    semof, count, lastop, waited = {}, {}, {}, set()

    def sem_of(name):
        if name not in semof:
            semof[name] = name if name in SEMAPHORES else "sem%d" % len([k for k in semof if k not in SEMAPHORES])
            count[name] = 0
        return T.sem[semof[name]]

    def wait(q, d):
        if d in known[q]:
            return
        name, n, before = ops[d]
        queue[q].wait_ge(sem_of(name), n)
        waited.add(d)
        known[q] |= before
        known[q].add(d)

    def note(me, q, r, w):
        for k in r:
            if k in bank:
                bank[k].append((q, me))
            else:
                readers.setdefault(k, []).append(me)
        for k in w:
            if k in bank:
                bank[k].append((q, me))
            else:
                lastw[k] = me
                readers[k] = []

    def op(q, name, r, w, fn, step=1):
        deps = set()
        for k in list(r) + list(w):
            if k in bank:
                deps |= {d for (e, d) in bank[k] if e != q}
                bank[k] = [(e, d) for (e, d) in bank[k] if e == q]
            elif k in lastw:
                deps.add(lastw[k])
        for k in w:
            deps |= set(readers.get(k, []))
        if name in lastop:
            deps.add(lastop[name])
        for d in sorted(deps, reverse=True):
            wait(q, d)
        sem = sem_of(name)
        ins = fn(queue[q], sem)
        if ins is None:
            count[name] += step
        else:
            for i in (ins if isinstance(ins, list) else [ins]):
                i.then_inc(sem, step)
                count[name] += step
        me = len(ops)
        ops.append((name, count[name], set(known[q])))
        lastop[name] = me
        note(me, q, r, w)
        return me

    def arrival(name, key):
        sem_of(name)
        count[name] += in_n
        me = len(ops)
        ops.append((name, count[name], set()))
        lastop[name] = me
        lastw[key] = me

    nc = [0]

    def const(q, r, w, fn):
        nc[0] += 1
        return op(q, "c%s%d" % (q, nc[0] % 8), r, w, fn)

    def ts(out, in0, s1, s2, o0, o1=None):
        if o1 is None:
            return lambda e, s: e.tensor_scalar(out, in0, s1, None, o0)
        return lambda e, s: e.tensor_scalar(out, in0, s1, s2, o0, o1)

    def tt(out, a, b, o):
        return lambda e, s: e.tensor_tensor(out, a, b, o)

    def cp(out, a):
        return lambda e, s: e.tensor_copy(out, a)

    def act(out, a, f, **kw):
        return lambda e, s: e.activation(out, a, f, **kw)

    def mm(out, l, r):
        return lambda e, s: e.matmul(out, l, r, True, True)

    def group(*terms):
        return lambda e, s: [e.matmul(o, l, r, k == 0, k == len(terms) - 1) for k, (o, l, r) in enumerate(terms)]

    fl = dict(allow_small_or_imprecise_dtypes=True)

    def iota(out, pat, base, cm):
        return lambda e, s: e.iota(out, pat, base, cm, **fl)

    def sel(out, a, pat, base, cm, o=A.is_equal):
        return lambda e, s: e.affine_select(out, a, pat, o, 0.0, base, cm)

    def dma(name, out, a, r, w, q=Y):
        return op(q, name, r, w, lambda e, s: e.dma_start(out, a), 16)

    def send(name, dst, src, rsem, key):
        def fn(e, s):
            e.remote_dma(dst, src, T.sem[rsem], s, pid, rid, out_mask)
        return op(G, name, key, [], fn, out_n)

    codes = T.kx[:, 128:128 + W]

    def qarea(n):
        return T.kx[:, 0:128] if n % 2 == 0 else T.kx[:, 128 + W:256 + W]

    def qwindow(n):
        return T.kx[:, 0:128 + W] if n % 2 == 0 else T.kx[:, 128:256 + W]

    dma("ld_st", T.sti[:], T.st[:], [], ["sti"], S)
    for k in range(PARTS):
        a, b = 2048 * k // PARTS, 2048 * (k + 1) // PARTS
        dma("ld_b%d" % k, T.bpi[:, a:b], T.bp[:, a:b], [], ["bpi%d" % k])
    dma("ld_k", codes, T.kt[:], [], ["kx"])
    dma("ld_v", T.vv[:], T.vt[:], [], ["vv"])
    for t in (1, 2):
        arrival("ac%d" % t, "cin%d" % t)
        arrival("am%d" % t, "msg%d" % t)
        arrival("aa%d" % t, "ain%d" % t)

    one = T.ones[:, 0:128]
    fb = [T.fb[:, k:k + 1] for k in range(8)]
    fc = [T.fc[:, k:k + 1] for k in range(12)]
    ln, lq, lx, lw, lv, lj = [T.la[:, 8 * k:8 * k + 8] for k in range(6)]
    sh, an = A.logical_shift_right, A.bitwise_and
    const(V, [], ["qd"], lambda e, s: e.memset(T.qd[:, 0:1024], 0.0))
    const(V, [], ["ones", "qd2"], lambda e, s: [e.memset(T.ones[:], 1.0), e.memset(T.qd[:, 1024:W + 64], 0.0)])
    const(G, [], ["ip", "ij"], lambda e, s: [e.iota(T.ip[:], [[0, 1]], 0, 1), e.iota(T.ij[:], [[1, 8]], 0, 0, **fl),
                                             e.iota(T.i2[:], [[64, 2], [8, 4]][::-1], 0, 0, **fl)])
    const(G, [], ["i5"], iota(T.i5[:], [[1, 1024]], 0, 0))
    const(S, ["qd"], ["nd"], act(T.nd[:], T.qd[:, 0:1024], ACT.Sigmoid, bias=-200.0))
    const(V, ["ip"], ["ib"], lambda e, s: [e.tensor_scalar(T.ib[:, k:k + 1], T.ip[:], a, b, sh, an) for k, (a, b) in enumerate((
        (0, 15), (4, 7), (0, 3), (0, 12), (0, 7), (3, 1), (1, 12), (5, 3)))])
    const(V, ["ib"], ["fb"], cp(T.fb[:], T.ib[:]))
    jl, gr, jb, u4, e7, e8, su4, sjb = fb
    op(V, "cvc", ["sti"], ["cin0"], cp(T.cin0[:], T.sti[:]))

    def mads(r, w, *calls):
        const(S, r, w, lambda e, s: [e.activation(o, a, ACT.Identity, scale=x, bias=y) for o, a, x, y in calls])
    mads(["fb", "ones"], ["fca", "cs", "nq"],
         (fc[0], jl, -float(W), 15.0 * W),
         (fc[7], jl, float(W), -15.0 * W), (fc[1], jb, 32.0, gr), (fc[3], jl, 32.0, gr), (fc[4], jl, 64.0, gr),
         (fc[5], e8, 32.0, gr), (fc[6], su4, 1.0, sjb), (fc[8], jl, 1.0, float(W)), (T.nq[:], one, -1.0 / 1024, 0.0),
         (T.cs[0:1, :, 1:17], T.ones[0:1, :], 1.75, 0.0), (T.cs[0:1, :, 0], T.ones[0:1, 0:16], 0.0, 0.0))
    mads(["fca", "ij"], ["fc", "ibias", "dum", "lfa"],
         (fc[9], u4, 2.0, fc[1]), (fc[10], e7, 128.0, fc[5]), (fc[11], gr, 7.0, fc[4]),
         (T.ibias[:], T.ij[:], 1024.0, fc[7]), (T.dum[:], T.ij[:], 16.0, fc[8]),
         (T.lf[:, 8:16], T.ij[:], 512.0, fc[3]), (T.lf[:, 16:24], T.ij[:], 8.0, fc[4]), (T.lf[:, 40:48], T.ij[:], 1.0, 0.0))
    mads(["fc", "ij"], ["lfb", "half"], (T.lf[:, 0:8], T.ij[:], 128.0, fc[9]), (T.lf[:, 24:32], T.ij[:], 1.0, fc[11]),
         (T.lf[:, 32:40], T.i2[:], 1.0, fc[10]), (T.half[:], one, 0.5, 0.0))
    const(G, ["ones"], ["il", "ig", "ik", "npb", "kb", "kr", "pgx", "d1"], lambda e, s: [
        e.iota(T.pg[:, W:W + 128], [[0, 128]], 0, 0), e.iota(T.kb[0:1, :], [[0, 128]], 1, 0, **fl),
        e.iota(T.il[:], [[0, 8], [1, 16]], 0, 0, **fl), e.iota(T.kr[0:3], [[0, 408]], 0, 0, **fl),
        e.iota(T.ik[0:3, 0:128], [[1, 4], [4, 4], [0, 8]], 0, 0, **fl),
        e.iota(T.ik[0:3, 128:144], [[0, 2], [-16, 8]], 0, 0, **fl), e.iota(T.ik[0:3, 144:160], [[0, 2], [16, 8]], 0, 0, **fl),
        e.iota(T.ig[:], [[1, 8], [0, 16]], 0, 0, **fl), e.iota(T.npb[:], [[0, 128]], -1, 0, **fl),
        e.affine_select(T.d1[:], T.ones[:, 0:136], [[0, 8], [1, 17]], A.is_equal, 0.0, 0, 0)])
    pp = [[-1, 8], [-8, 4], [-32, 4]]
    const(G, ["il", "ik", "kr"], ["kr", "kl"], lambda e, s: [
        e.affine_select(T.kr[0:3, 0:2, :, 15], T.ik[0:3, 128:144], [[0, 16]], A.is_equal, -1.0, -1, 1),
        e.affine_select(T.kr[0:3, 0:2, :, 16], T.ik[0:3, 144:160], [[0, 16]], A.is_equal, 1.0, -1, 1),
        e.affine_select(T.kr[0:3, 2, 0:2, 0:8], T.ik[0:3, 144:160], [[0, 16]], A.is_equal, 1.0, -1, 1),
        e.affine_select(T.kl[0:3, 0:128], T.ik[0:3, 0:128], [[0, 128]], A.is_equal, 1.0, -2, 1),
        e.affine_select(T.kl[0:3, 128:256], T.il[0:3, :], [[0, 128]], A.is_equal, 1.0, -2, 1)])
    const(G, ["ones"], ["pm"], lambda e, s: [
        e.affine_select(T.pm[:, 128 * x:128 * x + 128], one, pp, A.is_equal, 0.0, 0, 1) for x in (0, 1)])
    const(G, [], ["kr"], lambda e, s: [
        e.iota(T.kr[0:1, 0:2, :, 15], [[-128 - W, 2], [0, 8]], 128, 0, **fl), e.iota(T.kr[0:1, 0:2, :, 16], [[W, 2], [0, 8]], 0, 0, **fl),
        e.iota(T.kr[0:1, 2, 0:2, 0:8], [[128 + W, 2], [0, 8]], -128, 0, **fl)])
    const(G, ["ones"], ["id2"], sel(T.id2[:], T.ones[:], [[0, 2], [-1, 128]], 0, 1))
    const(G, ["ones"], ["idb"], sel(T.idb[:], one, [[-1, 128]], 0, 1))
    const(G, [], ["wd0"], iota(T.wd0[:], [[0, 1024]], 0, 0))
    const(G, ["ones"], ["jr0"], sel(T.jr[:], T.ones[:], [[-8, 16], [0, 2], [-1, 8]], 0, 1))
    const(G, ["npb"], ["npb"], sel(T.npb[:], T.npb[:], pp, 0, 1))
    const(G, ["ones"], ["pmb"], sel(T.pmb[:], one, pp, 0, 1))
    const(G, ["ones"], ["segm", "tt", "thr0"], lambda e, s: [
        e.affine_select(T.segm[:], T.ones[:, 0:136], [[0, 8], [1, 17]], A.is_gt, 0.0, 0, 0),
        e.iota(T.tt[:, :, :, 16], [[0, 64]], 0, 0, **fl), e.iota(T.thr[:, :, 16], [[0, 8]], 0, 0, **fl)])
    const(G, ["jr0"], ["jr"], lambda e, s: [
        e.affine_select(T["jr%d" % u][:], T.jr[:, :, 8 - u:16 - u], [[0, 128]], A.is_ge, 0.0, 0, 0) for u in (1, 2)])
    for wd in ("wd1", "wd2", "we0", "we1"):
        const(G, [], [wd], iota(T[wd][:], [[0, 1024]], 0, 0))

    for k in range(PARTS):
        a, b = 2048 * k // PARTS, 2048 * (k + 1) // PARTS
        op(V, "unp%d" % k, ["bpi%d" % k], ["pg%d" % k], lambda e, s: [
            e.tensor_scalar(T.pg[:, a:b], T.bpi[:, a:b], W - 1, None, an),
            e.tensor_scalar(T.pg[:, 2048 + a:2048 + b], T.bpi[:, a:b], 12, None, sh)])
    PG = ["pg%d" % k for k in range(PARTS)] + ["pgx"]
    const(V, ["lfa", "lfb", "i5", "fb"], ["la", "ea"], lambda e, s: [
        e.tensor_copy(T.la[:], T.lf[:]), e.tensor_scalar(T.ea[:], T.i5[:, 0:18], jl, None, A.is_equal)])

    def mask(name, tile, col):
        const(V, [tile, "fb", "fc"], [name], ts(T[name][:], T[tile][:], col, None, A.is_equal))

    def late_constants(k):
        if k == 0:
            mask("ma", "il", jl)
            const(V, ["half", "ones"], ["pw"], lambda e, s: e.tensor_tensor_scan(
                T.pw[:], T.half[:], one, 2.0 ** 64, A.mult, A.mult))
            mask("bob", "ig", gr)
        if k == 1:
            const(V, ["pw", "ma"], ["pw2"], tt(T.pw2[:], T.pw[:], T.ma[:], A.mult))
        if k == 2:
            mask("ms", "il", fc[6])
        if k == 3:
            const(V, ["pw2"], ["fc2"], lambda e, s: e.tensor_reduce(fc[2], T.pw2[:, 48:64], AxisListType.X, A.add))
            mask("selg", "ig", e7)
        if k == 4:
            const(V, ["pw2"], ["thr"], ts(T.thr[:, :, 0:16], T.pw2[:], 2.5, None, A.mult))
            const(V, ["fc2", "pw"], ["colw"], ts(T.colw[:], T.pw[:, 15::16], fc[2], None, A.mult))

    def key_numbers(x):
        const(S, ["i5", "ibias"], ["idm%d" % x], act(T.idm[:, 1024 * x:1024 * x + 1024], T.i5[:], ACT.Identity, bias=T.ibias[:, x:x + 1]))
    IDM = ["idm%d" % x for x in range(4)]
    for x in range(KEYS[0]):
        key_numbers(x)

    rall, r16 = T.pz[:, 0:136], T.pz[:, 16:136:17]
    PR, PN, PX, PS, RM = T.px[:, 160:288], T.pz[:, 264:392], T.px[:, 288:416], ["ps0", "ps1"], T.ps

    def kchunk(q, n, a, b):
        nm = "nm%d" % (n % 2)
        o, i = T.kg[:, 256 * a:256 * b], codes.indirect(T[nm][:, 16 * a:16 * b])
        op(q, "k%d" % a, ["kx", nm], ["kg%d" % x for x in range(a, b)], cp(o, i) if q == V else act(o, i, ACT.Identity))

    def scores(a, b, stops):
        op(P, "sco%d" % a, ["qd"] + ["kg%d" % x for x in range(a, b)], sorted({"ps%d" % (x // 4) for x in range(a, b)}),
           lambda e, s: [e.matmul(T.ps[:, m // 4, :, 1:17], T.qd[:, 128 * m + 32 - 8 * (m % 4):128 * m + 160 - 8 * (m % 4)],
                                  T.kg[:, 64 * m:64 * m + 64], False, m % 4 == 3 and m // 4 in stops)
                         for m in range(4 * a, 4 * b)])

    def names(n):
        nm = "nm%d" % (n % 2)
        op(V, "nd", [nm, "la"], ["nd"], cp(T.nd[:, 0:1024].indirect(ln), T[nm][:]))

    def steps(n):
        op(P, "dn", ["nd", "kl", "kr", "em"], ["px"], group(
            (T.px[:, 0:136], T.kl[0:3, 0:128], T.kr[0:3, n % 2, :, :]),
            *[(T.px[:, 17 * x:17 * x + 17], T.nd[:, 128 * x:128 * x + 128], T.em[:]) for x in range(8)]))

    def beta():
        op(V, "be", ["ff"], ["be"], ts(T.be[:], T.ff[:], -1.0, 1.0, A.mult, A.add))

    def rest(dx):
        op(V, "rm", [dx, "rs", "pz"], ["ps0", "rm"], tt(RM[:, 0:4, 0:2, 0:17], rall, T[dx][:], A.subtract))

    def weights():
        op(V, "ww", ["be", "rm", "ps0"], ["ww"], tt(T.ww[:], RM[:, 0:4, 0:2, 0:16], T.be[:, :, 1:17], A.mult))

    def turn_w(n):
        op(P, "wtp", ["ww", "id2", "pm"], ["px"], mm(PR, T.ww[:], (T.pm if n >= NEAR else T.id2)[:, 0:128]))

    def spread_w(n):
        wd, wt = "wd%d" % (n % 3), "wt%d" % (n % 2)
        if n >= NEAR:
            we = "we%d" % (n % 2)
            op(V, "wtv", ["px"], [wt], ts(T[wt][:], PR, 0.0, None, A.max))
            return op(V, "wds", [wt, "la"], [we], cp(T[we][:, 0:1024].indirect(lw), T[wt][:]))
        op(S, "wtc", ["px"], [wt], act(T[wt][:], PR, ACT.Relu))
        op(Y, "wdd%d" % (n % 2), [wt], [wd], lambda e, s: [
            e.dma_start(T[wd][16 * x:16 * x + 16, x, :], T[wt][16 * x:16 * x + 16, :]) for x in range(8)], 16)

    def vgather(q, n, a, b):
        nv, vg = "nv%d" % (n % 2), "vg%d" % (n % 2)
        o, i = T[vg][:, 128 * a:128 * b], T.vv[:, 0:W].indirect(T[nv][:, 8 * a:8 * b])
        op(q, "vg%s%d" % (q, a), ["vv", nv], ["%s_%d" % (vg, x) for x in range(a, b)], cp(o, i) if q == V else act(o, i, ACT.Identity))

    def list_v(n):
        nv = "nv%d" % (n % 2)
        op(V, "nv", ["nd", "la"], [nv], cp(T[nv][:], T.nd[:, 0:1024].indirect(lv)))

    def turn_v(n, half):
        vg, b = "vg%d" % (n % 2), ("pva", "pvb")[half]
        op(P, "vt" + b, ["%s_%d" % (vg, 8 * half + x) for x in range(8)] + ["idb"], [b], lambda e, s: [
            e.transpose(T[b][:, 128 * x:128 * x + 128], T[vg][:, 1024 * half + 128 * x:1024 * half + 128 * x + 128], T.idb[:])
            for x in range(8)])
        vs = "vs%d" % (n % 3)
        op(S, "sg" + b, [b], [vs + b], act(T[vs][:, 8 * half:8 * half + 8, :], T[b][:], ACT.Sigmoid))

    def acc_add(n, half, x0=0, x1=8):
        b, vs, wd = ("paa", "pab")[half], "vs%d" % (n % 3), "we%d" % (n % 2) if n >= NEAR else "wd%d" % (n % 3)

        def spread(j):
            p = 32 * (j % 4) + 8 * (j // 4)
            return T[wd][:, 64 * j:64 * j + 64] if n >= NEAR else T[wd][:, :, p:p + 8]
        op(P, "am%s%d" % (b, x0), [vs + ("pva", "pvb")[half], wd], [b], lambda e, s: [
            e.matmul(T[b][:, 64 * x:64 * x + 64], T[vs][:, 8 * half + x, :],
                     spread(8 * half + x), n % 3 == 0 and x == 0, n % 3 == 2 and x == 7) for x in range(x0, x1)])

    def acc_out(q, half):
        b, o = ("paa", "pab")[half], T.accs[:, 512 * half:512 * half + 512]
        op(q, "ao" + q + b, [b], ["accs%d" % half], act(o, T[b][:], ACT.Identity) if q == S else cp(o, T[b][:]))
    ACCS = ["accs0", "accs1", "la"]

    def picked():
        return T.accs[:, 0:1024].indirect(lx)

    def acc_in(t):
        ain = T["ain%d" % t]
        op(Y, "arot", ["ain%d" % t], ["accr"], lambda e, s: [
            e.dma_start(T.accr[16 * t:128, :], ain[0:128 - 16 * t, :]), e.dma_start(T.accr[0:16 * t, :], ain[128 - 16 * t:128, :])], 16)

    def report(t):
        acn = "acn%d" % t
        if t == 0:
            op(V, "acn", ACCS, [acn], cp(T[acn][:], picked()))
        else:
            op(V, "acn", ACCS + ["accr"], [acn], tt(T[acn][:], picked(), T.accr[:], A.add))
        send("sa%d" % t, T["ain%d" % (t + 1)][:], T[acn][:], "aa%d" % (t + 1), [acn])

    def output(t):
        acn, yo = "acn%d" % t, "yo%d" % t
        op(V, "yo", [acn, "rep"], [yo], tt(T[yo][:], T[acn][:], T.rep[:], A.add))
        dma("st%d" % t, T.ya[:, 128 * t:128 * t + 128], T[yo][:], [yo], [])

    def rest_value(cl):
        op(S, "sgc", ["vv", cl], ["sg"], act(T.sg[:], T.vv[:, 0:W].indirect(T[cl][:, 0:8]), ACT.Sigmoid))

    def rest_row():
        op(V, "xb", ["rn", "ms", "la"], ["xb"], tt(T.xb[:], T.rn[:, 0:8].indirect(lj), T.ms[:], A.mult))
        op(P, "rrow", ["xb", "selg"], ["px"], mm(PX, T.selg[:], T.xb[:]))

    def rest_term():
        op(V, "rep", ["sg", "px"], ["rep"], tt(T.rep[:], T.sg[:], PX, A.mult))

    taken = []
    behind = []

    def fill(k):
        for _ in range(k):
            if behind and behind[0][0] // 3 == len(taken):
                n, half, x = behind.pop(0)
                acc_add(n, half, x, x + 2)

    for n in range(9):
        t, h = divmod(n, 3)
        cl, cn, nm, dx = "cl%d" % (n % 2), "cl%d" % ((n + 1) % 2), "nm%d" % (n % 2), "dx%d" % h
        msg, qn, came = "msg%d" % t, "q%d" % (n % 2), "cin%d" % t
        clist = came if h == 0 else cl
        end = n == 8
        ns = SHARE[n]
        landed = h == 0 and t > 0

        def turn_q():
            op(P, "qrot", [msg, "id2"], ["px"], mm(PX, T.id2[:, 128 - 16 * t:256 - 16 * t], T[msg][:, 16:144]))

        op(P, "si", ["kb", "cs"], PS, lambda e, s: [
            e.matmul(T.ps[:, 4 * x:4 * x + 4, :, 0:17], T.kb[0:1, :], T.cs[0:1], True, False) for x in (0, 1)])
        op(V, "nm", PG + [clist], [nm], cp(T[nm][:], T.pg[:, 0:W].indirect(T[clist][:, 0:8])))
        if landed:
            rest_term()
        if n == 0:
            const(V, ["ea"], ["em"], tt(T.em[:], T.ea[:, 0:17], T.ea[:, 1:18], A.subtract))
            names(n)
        if h > 0:
            op(V, "qs", ["kx", "q%d" % ((n - 1) % 2), cl], [qn], cp(qarea(n), qwindow(n - 1).indirect(T[cl][:, 8:16])))
        elif t == 0:
            op(V, "qs", ["kx", came], [qn], cp(qarea(n), codes.indirect(T[came][:])))
        cuts = [ns] + [c for c in (3, 5, 7, 8) if c > ns]
        bits = list(zip(cuts[:-1], cuts[1:]))
        if ns:
            kchunk(S, n, 0, ns)
        if n == 0:
            for x in range(KEYS[0], 4):
                key_numbers(x)
            list_v(n)
        if landed:
            names(n)
            kchunk(V, n, *bits[0])
            list_v(n)
            turn_q()
            op(V, "qs", ["px"], [qn], cp(qarea(n), PX))
            op(V, "d1", [msg], ["d1"], cp(T.d1[:, 0::17], T[msg][:, 8:16]))
            if t < 2:
                op(V, "cd", [msg, "dum"], ["cd"], tt(T.cd[:], T[msg][:, 0:8], T.dum[:], A.subtract))
        if h > 0:
            turn_w(n - 1)
            if n - 1 < NEAR:
                spread_w(n - 1)
            turn_v(n - 1, 0)
            turn_v(n - 1, 1)
        if h > 0:
            names(n)
        op(V, "qd", [qn, "la", "nq", "qd2"], ["qd"], tt(T.qd[:, 32:W + 64].indirect(lq), qarea(n), T.nq[:], A.mult))
        if h > 0:
            list_v(n)
        sv = 16 - sum(GAPS[n])

        def gap(k):
            if n == 0:
                late_constants(k)
            if GAPS[n][k]:
                vgather(V, n, sv + sum(GAPS[n][:k]), sv + sum(GAPS[n][:k + 1]))
        vgather(S, n, 0, 8)
        if STEPS[n] == 0 and not end:
            steps(n)
        fill(FILL[n][0])
        if h > 0 and n - 1 < NEAR:
            behind.extend((n - 1, half, x) for half in (0, 1) for x in (0, 2, 4, 6))
        late = min(LATE[n], len(bits) - 1)
        done = [x for k, (a, b) in enumerate(bits) for x in (list(range(ns)) if k == late else []) + list(range(a, b))]
        stops = ([x for x in done if x < 4][-1], 7)
        for k, (a, b) in enumerate(bits):
            if not (landed and k == 0):
                kchunk(V, n, a, b)
            if k == late and ns:
                scores(0, ns, stops)
            scores(a, b, stops)
            if h > 0 and n - 1 >= NEAR and k == min(WAT[n - 7], len(bits) - 1):
                spread_w(n - 1)
                behind.extend((n - 1, half, x) for half in (0, 1) for x in (0, 2, 4, 6))
            if min(STEPS[n], len(bits)) == k + 1 and not end:
                steps(n)
            if k < len(bits) - 1:
                fill(FILL[n][1 + k])
        fill(FILL[n][-1])
        assert sv >= 8
        if sv > 8:
            vgather(S, n, 8, sv)
        if n in OUT:
            fill(16)
            acc_out(S, 0)
            acc_out(S, 1)
            taken.append(t)
        if h == 1 and t < 2:
            op(V, "crow", IDM + ["fc", came], ["crow"], ts(T.crow[:], T.idm[:, 0:W].indirect(T[came][:]), fc[0], None, A.add))
        if h == 0 and t < 2:
            op(V, "v0", [nm, "fc"], ["v0"], ts(T.v0[:], T[nm][:], fc[0], None, A.min))
        if n == 0:
            op(V, "cd", ["sti", "dum"], ["cd"], tt(T.cd[:], T.sti[:], T.dum[:], A.subtract))
        if n == 6:
            acc_in(1)
        if n - 1 in OUT:
            report(t - 1)
        gap(0)
        op(V, "clamp", PS, ["ff"], lambda e, s: [
            e.tensor_scalar(T.ff[32 * b:32 * b + 32, :], T.ps[32 * b:32 * b + 32, :, b, 0:17], 0.0625, 1.0, A.max, A.min)
            for b in range(4)])
        gap(1)
        op(V, "rs", ["ff", "d1"], ["rs", "pz"], lambda e, s: e.tensor_tensor_scan(rall, T.ff[:], T.d1[:], 0.0, A.mult, A.max))
        beta()
        if end:
            op(V, "e3", ["rs", "pz"], ["e3"], ts(T.e3[:], rall, 0.0625, None, A.is_lt))
            gap(2)
            op(V, "e16", ["e3", "rs", "pz"], ["rn"], tt(T.rn[:], T.e3[:, :, 16], r16, A.max))
            rest("e3")
            op(V, "ee", ["e3"], ["ee"], tt(T.ee[:], T.e3[:, :, 1:17], T.e3[:, :, 0:16], A.subtract))
            weights()
            op(V, "e15", ["e3", "rn", "ee"], ["ee"], tt(T.ee[:, 15::16], T.rn[:], T.e3[:, :, 15], A.subtract))
            turn_v(n, 0)
            fill(FILL[n + 1][0])
            op(P, "wtp", ["ww", "ee", "pm"], ["px"], group((PR, T.ww[:], T.pm[:, 0:128]), (PR, T.ee[:], T.pm[:, 0:128])))
            gap(3)
            gap(4)
            turn_v(n, 1)
            spread_w(n)
            fill(16)
            acc_in(t)
            acc_add(n, 0)
            acc_add(n, 1)
            acc_out(V, 0)
            acc_out(S, 1)
            op(V, "yo", ACCS + ["accr"], ["yo2"], tt(T.yo2[:], picked(), T.accr[:], A.add))
            dma("st2", T.ya[:, 256:384], T.yo2[:], ["yo2"], [])
            break
        op(V, "dx", ["rs", "pz"], [dx], ts(T[dx][:], rall, 0.0625, None, A.is_lt))
        gap(2)
        if h == 2:
            u, snc, snd = t + 1, "snc%d" % t, "snd%d" % t
            op(P, "pcut", ["dx0", "dx1", "dx2", "pmb", "npb"], ["ps0"], group(
                (T.ps[:, 0, 2, 0:8], T.pmb[:], T.dx2[:, 16::17]), (T.ps[:, 0, 2, 0:8], T.npb[:], T.dx1[:, 16::17]),
                (T.ps[:, 0, 2, 0:8], T.npb[:], T.dx0[:, 16::17])))
            op(V, "rn", [dx, "rs", "pz"], ["rn"], tt(T.rn[:], T[dx][:, 16::17], r16, A.max))
            op(P, "pq2", ["rn", "jr"], ["ps1"], mm(T.ps[:, 4, 1, 8:16], T["jr%d" % u][:], T.rn[:]))
        op(V, "sc", [dx, "px"], ["sc"], lambda e, s: e.tensor_tensor_scan(T.sc[:], T[dx][:], T.px[:, 0:136], 0.0, A.mult, A.add))

        def lists():
            op(P, "pc", ["sc", "pm", "kl", "kr"], ["px"], group(
                (T.px[:, 136:152], T.kl[0:3, 128:256], T.kr[0:3, 2, n % 2, 0:16]), (T.px[:, 136:144], T.pm[:, 0:128], T.sc[:, 15::17]),
                (T.px[:, 144:152], T.pm[:, 0:128], T.sc[:, 16::17])))

        def take_lists():
            op(V, "cvc", ["px"], [cn], cp(T[cn][:], T.px[:, 136:152]))
        if h < 2:
            lists()
            rest(dx)
            op(V, "d1", [dx, "rs", "pz"], ["d1"], tt(T.d1[:, 0::17], T[dx][:, 16::17], r16, A.max))
            if n - 1 in OUT:
                output(t - 1)
            gap(3)
            weights()
            take_lists()
            gap(4)
        else:
            op(P, "pq", ["sc", "pm", "kl", "kr"], ["ps1"], group(
                (T.ps[:, 4, 1, 0:8], T.kl[0:3, 128:256], T.kr[0:3, 2, n % 2, 0:8]),
                (T.ps[:, 4, 1, 0:8], T.pm[:, 128 - 16 * u:256 - 16 * u], T.sc[:, 15::17])))
            lists()
            turn_v(n, 0)
            op(V, "cut", ["ps0"], ["cut"], ts(T.cut[:], T.ps[:, 0, 2, 0:8], 0.0, None, A.max))
            rest(dx)
            op(V, "delta", ["cut", "cd"], ["segm"], tt(T.segm[:, 16::17], T.cut[:], T.cd[:], A.mult))
            weights()
            gap(3)
            op(V, "to", ["segm", "dum"], ["to"], tt(T.to[:], T.segm[:, 16::17], T.dum[:], A.add))
            op(V, "snc", ["ps1"], [snc], cp(T[snc][:], T.ps[:, 4, 1, 0:8]))
            send("sc%d" % t, T["cin%d" % u][:], T[snc][:], "ac%d" % u, [snc])
            take_lists()
            turn_w(n)
            spread_w(n)
            op(V, "sna", ["ps1"], [snd + "a"], cp(T[snd][:, 0:16], T.ps[:, 4, 1, 0:16]))

            def send_q():
                op(V, "snb", ["kx", qn, cn], [snd + "b"], cp(T[snd][:, 16:144], qwindow(n).indirect(T[cn][:, 8:16])))
                send("sm%d" % t, T["msg%d" % u][:], T[snd][:], "am%d" % u, [snd + "a", snd + "b"])
            if GAPS[n][4] == 0:
                turn_v(n, 1)
            fill(WIN[0])
            for k, (a, b) in enumerate(((0, 3), (3, 8))):
                if QAT[t] == k:
                    send_q()
                op(V, "tt%d" % a, ["crow", "to", "colw"], ["tt%d" % a], lambda e, s: [
                    e.tensor_scalar(T.tt[:, x, x:8, 0:16], T.crow[:, 16 * x:128], T.to[:, x:x + 1], T.colw[:, x:x + 1],
                                    A.is_equal, A.mult) for x in range(a, b)])
                op(P, "ssum%d" % a, ["tt%d" % a, "tt", "bob"], ["pz"], lambda e, s: [
                    e.matmul(T.pz[:, 264 + 17 * x:400], T.bob[:], T.tt[:, x, x:8, :], x == 0, x == 7) for x in range(a, b)])
            if QAT[t] == 2:
                send_q()
            op(V, "win", ["pz", "thr", "thr0"], ["win"], tt(T.win[:], T.pz[:, 264:400], T.thr[:], A.is_lt))
            op(V, "vals", IDM + ["v0", cn], ["vals"], tt(T.vals[:], T.idm[:, 0:W].indirect(T[cn][:, 0:8]), T.v0[:], A.max))
            op(V, "so", ["segm", "win"], ["so"], lambda e, s: e.tensor_tensor_scan(
                T.so[:], T.segm[:], T.win[:], 0.0, A.mult, A.add))
            if GAPS[n][4]:
                gap(4)
                turn_v(n, 1)
            fill(WIN[1])
            rest_value(cn)
            op(V, "t2", ["so", "dum"], ["t2"], tt(T.t2[:], T.so[:, 16::17], T.dum[:], A.add))
            rest_row()
            fill(16)
            behind.extend((n, half, x) for half in (0, 1) for x in (0, 2, 4, 6))
            op(V, "offs", ["t2"], ["offs"], cp(T.offs[:], T.t2[:]))
            if n - 1 in OUT:
                output(t - 1)
            op(V, "cutp", ["vals", "offs"], PG, cp(T.pg[:, 0:W + 128].indirect(T.offs[:]), T.vals[:]))

    for name in list(lastop):
        if lastop[name] not in waited:
            wait(G, lastop[name])
